import numpy as np
import ml_dtypes


def mxq(x, axis, fmt="e4m3"):
    dtype, down = {"e4m3": (ml_dtypes.float8_e4m3fn, 7), "e5m2": (ml_dtypes.float8_e5m2, 14)}[fmt]
    v = np.moveaxis(np.asarray(x, np.float32).astype(ml_dtypes.bfloat16).astype(np.float64), axis, -1)
    blocks = v.reshape(v.shape[:-1] + (-1, 32))
    amax = np.abs(blocks).max(-1, keepdims=True)
    byte = np.maximum(np.where(amax > 0, np.frexp(amax)[1] - 1 + 127, 0) - down, 1)
    scale = np.exp2(byte - 127.0)
    codes = (blocks / scale).astype(np.float32).astype(dtype).astype(np.float64)
    return np.moveaxis((codes * scale).reshape(v.shape), -1, axis)


WIDE = False


def mx_kscale(k):
    if not WIDE:
        return np.ones(k)
    levels = np.array([10, -10, 5, -5, 0])
    if k % 512:
        return np.exp2(np.random.permutation(np.resize(levels, k // 32))).repeat(32)
    a = np.empty((k // 512, 16))
    for p in range(k // 512):
        a[p, :8] = np.random.permutation(np.resize(levels, 8))
        for g in range(8):
            far = levels[np.abs(levels - a[p, g]) >= 10]
            a[p, g + 8] = far[np.random.randint(len(far))]
    return np.exp2(a.ravel()).repeat(32)


def f64(x):
    return np.asarray(x).astype(np.float64)


def striped(idx):
    return np.tile(idx.reshape(-1, 16).T, (8, 1)).astype(np.uint16)


def unstriped(offs):
    return offs[:16].T.reshape(-1).astype(np.int64)


E2M1 = np.array([0.0, 0.5, 1.0, 1.5, 2.0, 3.0, 4.0, 6.0, -0.0, -0.5, -1.0, -1.5, -2.0, -3.0, -4.0, -6.0])


def pack_weight(w, fmt):
    k, n = w.shape
    w = f64(np.asarray(w, np.float32).astype(ml_dtypes.bfloat16)).reshape(k // 32, 32, n)
    amax = np.abs(w).max(1)
    if fmt == "e4m3":
        byte = np.frexp(amax)[1] - 1 + 127 - 7
    else:
        mant, ex = np.frexp(amax / 6.0)
        byte = np.where(mant > 0.5, ex, ex - 1) + 127
    byte = np.clip(np.where(amax > 0, byte, 1), 1, 254)
    scaled = (w * np.exp2(127.0 - byte)[:, None, :]).reshape(k, n).astype(np.float32)
    by_word = np.ascontiguousarray(scaled.reshape(k // 512, 128, 4, n).transpose(0, 1, 3, 2))
    if fmt == "e4m3":
        words = by_word.astype(ml_dtypes.float8_e4m3fn).view(np.uint8)
    else:
        c = by_word.astype(ml_dtypes.float4_e2m1fn).view(np.uint8) & 0xF
        words = (c[..., 0::2] | (c[..., 1::2] << 4)).reshape(k // 512, 128, 2 * n)
    return np.ascontiguousarray(words), np.ascontiguousarray(byte.astype(np.uint8).reshape(k // 512, 16, n))


def unpack_weight(words, scales, fmt):
    g, _, n = scales.shape
    words = np.ascontiguousarray(words).reshape(g, 128, n, -1)
    if fmt == "e4m3":
        vals = words.view(ml_dtypes.float8_e4m3fn).astype(np.float64)
    else:
        nib = np.empty((g, 128, n, 4), np.uint8)
        nib[..., 0::2] = words & 0xF
        nib[..., 1::2] = words >> 4
        vals = E2M1[nib]
    vals = vals * np.repeat(np.exp2(scales.astype(np.float64) - 127.0), 8, axis=1)[..., None]
    return vals.transpose(0, 1, 3, 2).reshape(g * 512, n)


K, T, S1, S2 = 512, 2048, 1024, 1024


def setup_inputs():
    n = np.random.standard_normal
    s = mx_kscale(K)
    u = mx_kscale(K)
    first, second = np.random.permutation(T)[:S1], np.random.permutation(T)[:S2]
    xf = n((K, T))
    x = pack_weight(xf * s[:, None], "e4m3")
    w1 = pack_weight(n((K, K)) / np.sqrt(K) / s[:, None] * u, "e4m3")
    return {
        "x_words": x[0],
        "x_scales": x[1],
        "xr": (xf * u[:, None]).astype(np.float32),
        "w1_words": w1[0],
        "w1_scales": w1[1],
        "w2": (n((K, K)) / np.sqrt(K) / u[:, None] * u).astype(np.float32),
        "gate1": (np.tile(np.random.uniform(0.2, 1.0, S1), (128, 1))).astype(np.float32),
        "gate2": (np.tile(np.random.uniform(0.2, 1.0, S2), (128, 1))).astype(np.float32),
        "offs": striped(first),
        "offs2": striped(second),
    }


def reference(x_words, x_scales, xr, w1_words, w1_scales, w2, gate1, gate2, offs, offs2):
    w1 = unpack_weight(w1_words, w1_scales, "e4m3")
    w2q = mxq(f64(w2), 0, "e4m3")
    idx, idx2 = unstriped(offs), unstriped(offs2)
    r = f64(xr)
    r[:, idx] += f64(gate1[:1]) * (w1.T @ unpack_weight(x_words, x_scales, "e4m3")[:, idx])
    r2 = r.copy()
    r2[:, idx2] += f64(gate2[:1]) * (w2q.T @ mxq(r[:, idx2], 0, "e4m3"))
    return r2

@@ -1,0 +1,207 @@
+from contextlib import ExitStack
+
+import concourse.mybir as mybir
+from concourse.masks import make_identity
+
+K, T, S = 512, 2048, 1024
+FLOPS = 2 * 2 * K * K * S
+
+F32 = mybir.dt.float32
+BF16 = mybir.dt.bfloat16
+I32 = mybir.dt.int32
+U32 = mybir.dt.uint32
+U16 = mybir.dt.uint16
+U8 = mybir.dt.uint8
+FP8X4 = mybir.dt.float8_e4m3fn_x4
+COPY = mybir.ActivationFunctionType.Copy
+ADD = mybir.AluOpType.add
+MULT = mybir.AluOpType.mult
+
+P = 128
+PACK = 4
+CHUNK = 256
+CHUNKS = S // CHUNK
+BLOCKS = S // P
+LAST = PACK - 1
+
+
+def tile_moe_mod_none_kernel(
+    tc, x_words, x_scales, xr, w1_words, w1_scales, w2, gate1, gate2, offs, offs2, out
+):
+    nc = tc.nc
+    with ExitStack() as ctx:
+        keep = ctx.enter_context(tc.tile_pool(name="keep", bufs=1))
+        psum = ctx.enter_context(tc.psum_pool(name="psum", bufs=1))
+
+        def sbuf(name, shape, dtype):
+            return keep.tile(shape, dtype, name=name, align_bytes=64)
+
+        list1 = sbuf("list1", [P, S // 16], U16)
+        list2 = sbuf("list2", [P, S // 16], U16)
+        tok_words = sbuf("tok_words", [P, T], I32)
+        tok_scales = sbuf("tok_scales", [P, T], U8)
+        w1_codes = sbuf("w1_codes", [P, K], I32)
+        w1_plane = sbuf("w1_plane", [P, K], U8)
+        gate_rows = sbuf("gate_rows", [P, P], F32)
+        gate_cols = sbuf("gate_cols", [P, P], F32)
+        ident = sbuf("ident", [P, P], F32)
+        w2_raw = sbuf("w2_raw", [P, PACK, K], F32)
+        w2_bf = sbuf("w2_bf", [P, K, PACK], BF16)
+        w2_codes = sbuf("w2_codes", [P, K], U32)
+        w2_plane = sbuf("w2_plane", [P, K], U8)
+        stream = [sbuf("stream%d" % t, [P, T], F32) for t in range(PACK)]
+        spread1 = [sbuf("spread1_%d" % i, [P, T], F32) for i in range(2)]
+        spread2 = [sbuf("spread2_%d" % i, [P, T], F32) for i in range(2)]
+        stream_bf = [sbuf("stream_bf%d" % t, [P, T], BF16) for t in range(LAST)]
+        x_codes = sbuf("x_codes", [P, S], U32)
+        x_plane = sbuf("x_plane", [P, S], U8)
+        r_last = sbuf("r_last", [P, S], F32)
+        r_bf = sbuf("r_bf", [P, S, PACK], BF16)
+        r_codes = sbuf("r_codes", [P, S], U32)
+        r_plane = sbuf("r_plane", [P, S], U8)
+        turned = [sbuf("turned%d" % l, [P, BLOCKS, PACK, P], F32) for l in range(2)]
+        gated = [sbuf("gated%d" % l, [P, PACK, S], F32) for l in range(2)]
+        last_sum = sbuf("last_sum", [P, S], F32)
+
+        product_banks = [psum.tile([P, K], F32, name="product%d" % i) for i in range(2)]
+        turn_banks = [psum.tile([P, K], F32, name="turn%d" % i) for i in range(4)]
+        turn_count = [0]
+
+        def chunk_cols(c):
+            return slice(c * CHUNK, (c + 1) * CHUNK)
+
+        def chunk_list(lst, c):
+            return lst[:, c * CHUNK // 16 : (c + 1) * CHUNK // 16]
+
+        nc.vector.memset(tok_scales[:].bitcast(I32), 0)
+        nc.vector.memset(w1_plane[:].bitcast(I32), 0)
+        make_identity(nc, ident[:])
+        for tile in spread1 + spread2:
+            nc.gpsimd.memset(tile[:], 0.0)
+
+        xr_rows = xr.rearrange("(p t) n -> p t n", t=PACK)
+        out_rows = out.rearrange("(p t) n -> p t n", t=PACK)
+
+        nc.sync.dma_start(list1[:], offs)
+        for q in range(4):
+            nc.sync.dma_start(
+                tok_scales[32 * q : 32 * q + 4, :].bitcast(I32), x_scales[0, 4 * q : 4 * q + 4, :].bitcast(I32)
+            )
+        nc.sync.dma_start(tok_words[:], x_words[0].rearrange("p t d -> p (t d)").bitcast(I32))
+        nc.sync.dma_start(w1_codes[:], w1_words[0].rearrange("p i d -> p (i d)").bitcast(I32))
+        for half, gate in enumerate((gate1, gate2)):
+            nc.sync.dma_start(
+                gate_rows[64 * half : 64 * half + 64, :], gate.rearrange("p (b s) -> (p b) s", s=P)[0:64, :]
+            )
+        for q in range(4):
+            nc.sync.dma_start(
+                w1_plane[32 * q : 32 * q + 4, :].bitcast(I32), w1_scales[0, 4 * q : 4 * q + 4, :].bitcast(I32)
+            )
+        nc.sync.dma_start(stream[0][:], xr_rows[:, 0, :])
+        nc.sync.dma_start(list2[:], offs2)
+        nc.sync.dma_start(w2_raw[:], w2.rearrange("(p j) n -> p j n", j=PACK))
+        for t in range(1, PACK):
+            nc.sync.dma_start(stream[t][:], xr_rows[:, t, :])
+
+        nc.tensor.transpose(turn_banks[3][:, 0:P], gate_rows[:], ident[:])
+        nc.scalar.activation(gate_cols[:], turn_banks[3][:, 0:P], COPY)
+
+        def product(layer, b, codes, plane, w_codes, w_plane):
+            cols = slice(b * P, (b + 1) * P)
+            bank = product_banks[b % 2]
+            nc.tensor.matmul_mx(
+                out=bank[:],
+                lhsT=codes[:, cols].bitcast(FP8X4),
+                lhsT_scale=plane[:, cols],
+                rhs=w_codes[:].bitcast(FP8X4),
+                rhs_scale=w_plane[:],
+                start=True,
+                stop=True,
+            )
+            g = 64 * layer + b
+            nc.scalar.activation(
+                turned[layer][:, b, :, :],
+                bank[:].rearrange("s (m t) -> s t m", t=PACK),
+                COPY,
+                scale=gate_cols[:, g : g + 1],
+            )
+
+        def turn_back(layer, t, b0, b1):
+            bank = turn_banks[turn_count[0] % 4]
+            turn_count[0] += 1
+            for b in range(b0, b1):
+                nc.tensor.transpose(bank[:, (b - b0) * P : (b - b0 + 1) * P], turned[layer][:, b, t, :], ident[:])
+            nc.scalar.copy(gated[layer][:, t, b0 * P : b1 * P], bank[:, 0 : (b1 - b0) * P])
+
+        for c in range(CHUNKS):
+            nc.vector.tensor_copy(x_plane[:, chunk_cols(c)], tok_scales[:].indirect(chunk_list(list1, c)))
+            nc.vector.tensor_copy(
+                x_codes[:, chunk_cols(c)], tok_words[:].bitcast(U32).indirect(chunk_list(list1, c))
+            )
+        for c in range(CHUNKS):
+            for b in (2 * c, 2 * c + 1):
+                product(0, b, x_codes, x_plane, w1_codes, w1_plane)
+            turn_back(0, 0, 2 * c, 2 * c + 2)
+            nc.vector.tensor_copy(spread1[0][:].indirect(chunk_list(list1, c)), gated[0][:, 0, chunk_cols(c)])
+            if c == 0:
+                turn_back(0, 1, 0, 2)
+                nc.vector.tensor_copy(spread1[1][:].indirect(chunk_list(list1, c)), gated[0][:, 1, chunk_cols(c)])
+        turn_back(0, 1, 2, 4)
+        turn_back(0, 1, 4, 8)
+        for t in range(2, PACK):
+            turn_back(0, t, 0, 4)
+            turn_back(0, t, 4, 8)
+        nc.gpsimd.tensor_scalar(w2_bf[:], w2_raw[:].rearrange("p j n -> p n j"), 1.0, 0.0, MULT, ADD)
+        for t in range(PACK):
+            if t == 1:
+                nc.vector.tensor_copy(spread1[1][:].indirect(list1[:, CHUNK // 16 :]), gated[0][:, t, CHUNK:])
+            if t > 1:
+                nc.vector.tensor_copy(spread1[t % 2][:].indirect(list1[:]), gated[0][:, t, :])
+            if t < LAST:
+                for h in range(2):
+                    cols = slice(h * T // 2, (h + 1) * T // 2)
+                    nc.gpsimd.tensor_tensor(stream[t][:, cols], stream[t][:, cols], spread1[t % 2][:, cols], ADD)
+                    nc.scalar.copy(stream_bf[t][:, cols], stream[t][:, cols])
+            if t < LAST - 1:
+                nc.scalar.activation(r_bf[:, :, t], stream_bf[t][:].indirect(list2[:]), COPY)
+        nc.vector.tensor_tensor(stream[LAST][:], stream[LAST][:], spread1[LAST % 2][:], ADD)
+
+        for c in range(CHUNKS):
+            nc.vector.tensor_copy(r_last[:, chunk_cols(c)], stream[LAST][:].indirect(chunk_list(list2, c)))
+            if c == 0:
+                nc.vector.quantize_mx(
+                    out=w2_codes[:].bitcast(FP8X4), scales=w2_plane[:], in_=w2_bf[:].rearrange("p n j -> p (n j)")
+                )
+            nc.scalar.activation(
+                r_bf[:, chunk_cols(c), LAST - 1], stream_bf[LAST - 1][:].indirect(chunk_list(list2, c)), COPY
+            )
+            nc.scalar.copy(r_bf[:, chunk_cols(c), LAST], r_last[:, chunk_cols(c)])
+            nc.vector.quantize_mx(
+                out=r_codes[:, chunk_cols(c)].bitcast(FP8X4),
+                scales=r_plane[:, chunk_cols(c)],
+                in_=r_bf[:, chunk_cols(c), :].rearrange("p s j -> p (s j)"),
+            )
+            for b in (2 * c, 2 * c + 1):
+                product(1, b, r_codes, r_plane, w2_codes, w2_plane)
+            turn_back(1, 0, 2 * c, 2 * c + 2)
+            nc.vector.tensor_copy(spread2[0][:].indirect(chunk_list(list2, c)), gated[1][:, 0, chunk_cols(c)])
+            if c == 0:
+                turn_back(1, 1, 0, 2)
+                nc.vector.tensor_copy(spread2[1][:].indirect(chunk_list(list2, c)), gated[1][:, 1, chunk_cols(c)])
+        turn_back(1, 1, 2, 4)
+        turn_back(1, 1, 4, 8)
+        for t in range(2, PACK):
+            turn_back(1, t, 0, 4)
+            turn_back(1, t, 4, 8)
+        nc.gpsimd.tensor_tensor(last_sum[:], gated[1][:, LAST, :], r_last[:], ADD)
+        for t in range(LAST):
+            if t == 1:
+                nc.vector.tensor_copy(spread2[1][:].indirect(list2[:, CHUNK // 16 :]), gated[1][:, t, CHUNK:])
+            if t > 1:
+                nc.vector.tensor_copy(spread2[t % 2][:].indirect(list2[:]), gated[1][:, t, :])
+            for h in range(2):
+                cols = slice(h * T // 2, (h + 1) * T // 2)
+                nc.gpsimd.tensor_tensor(stream[t][:, cols], stream[t][:, cols], spread2[t % 2][:, cols], ADD)
+                nc.sync.dma_start(out_rows[:, t, cols], stream[t][:, cols])
+        nc.vector.tensor_copy(stream[LAST][:].indirect(list2[:]), last_sum[:])
+        nc.sync.dma_start(out_rows[:, LAST, :], stream[LAST][:])

@@ -19,8 +19,9 @@ MULT = mybir.AluOpType.mult
 
 P = 128
 PACK = 4
-CHUNK = 256
-CHUNKS = S // CHUNK
+QUARTERS = [slice(c * S // 4, (c + 1) * S // 4) for c in range(4)]
+HALVES = [slice(0, S // 2), slice(S // 2, S)]
+PIECES = [QUARTERS[0], QUARTERS[1], HALVES[1]]
 BLOCKS = S // P
 LAST = PACK - 1
 
@@ -36,42 +37,43 @@ def tile_moe_mod_none_kernel(
         def sbuf(name, shape, dtype):
             return keep.tile(shape, dtype, name=name, align_bytes=64)
 
+        def staged_tile(name, shape, dtype):
+            return keep.tile(shape, dtype, name=name, tag="staged", align_bytes=64)
+
         list1 = sbuf("list1", [P, S // 16], U16)
         list2 = sbuf("list2", [P, S // 16], U16)
         tok_words = sbuf("tok_words", [P, T], I32)
         tok_scales = sbuf("tok_scales", [P, T], U8)
         w1_codes = sbuf("w1_codes", [P, K], I32)
         w1_plane = sbuf("w1_plane", [P, K], U8)
-        gate_rows = sbuf("gate_rows", [P, P], F32)
-        gate_cols = sbuf("gate_cols", [P, P], F32)
+        w1_codes0 = sbuf("w1_codes0", [P, P], I32)
+        w1_plane0 = sbuf("w1_plane0", [P, P], U8)
+        gates = [sbuf("gate%d" % l, [P, S], F32) for l in range(2)]
+        gate_rows = [sbuf("gate_rows%d" % l, [P, P], F32) for l in range(2)]
+        gate_cols = [sbuf("gate_cols%d" % l, [P, BLOCKS], F32) for l in range(2)]
         ident = sbuf("ident", [P, P], F32)
-        w2_raw = sbuf("w2_raw", [P, PACK, K], F32)
         w2_bf = sbuf("w2_bf", [P, K, PACK], BF16)
         w2_codes = sbuf("w2_codes", [P, K], U32)
         w2_plane = sbuf("w2_plane", [P, K], U8)
         stream = [sbuf("stream%d" % t, [P, T], F32) for t in range(PACK)]
         spread1 = [sbuf("spread1_%d" % i, [P, T], F32) for i in range(2)]
         spread2 = [sbuf("spread2_%d" % i, [P, T], F32) for i in range(2)]
-        stream_bf = [sbuf("stream_bf%d" % t, [P, T], BF16) for t in range(LAST)]
         x_codes = sbuf("x_codes", [P, S], U32)
         x_plane = sbuf("x_plane", [P, S], U8)
-        r_last = sbuf("r_last", [P, S], F32)
         r_bf = sbuf("r_bf", [P, S, PACK], BF16)
         r_codes = sbuf("r_codes", [P, S], U32)
         r_plane = sbuf("r_plane", [P, S], U8)
-        turned = [sbuf("turned%d" % l, [P, BLOCKS, PACK, P], F32) for l in range(2)]
-        gated = [sbuf("gated%d" % l, [P, PACK, S], F32) for l in range(2)]
+        turned = [staged_tile("turned0", [P, BLOCKS, LAST, P], F32), sbuf("turned1", [P, BLOCKS, LAST, P], F32)]
+        sums = [sbuf("sums%d" % l, [P, PACK, S], F32) for l in range(2)]
         last_sum = sbuf("last_sum", [P, S], F32)
 
-        product_banks = [psum.tile([P, K], F32, name="product%d" % i) for i in range(2)]
-        turn_banks = [psum.tile([P, K], F32, name="turn%d" % i) for i in range(4)]
+        direct_banks = [psum.tile([P, K], F32, name="direct%d" % i) for i in range(2)]
+        product_banks = [psum.tile([P, K], F32, name="product%d" % i) for i in range(3)]
+        turn_banks = [psum.tile([P, K], F32, name="turn%d" % i) for i in range(3)]
         turn_count = [0]
 
-        def chunk_cols(c):
-            return slice(c * CHUNK, (c + 1) * CHUNK)
-
-        def chunk_list(lst, c):
-            return lst[:, c * CHUNK // 16 : (c + 1) * CHUNK // 16]
+        def entries(lst, cols):
+            return lst[:, cols.start // 16 : cols.stop // 16]
 
         nc.vector.memset(tok_scales[:].bitcast(I32), 0)
         nc.vector.memset(w1_plane[:].bitcast(I32), 0)
@@ -89,119 +91,145 @@ def tile_moe_mod_none_kernel(
             )
         nc.sync.dma_start(tok_words[:], x_words[0].rearrange("p t d -> p (t d)").bitcast(I32))
         nc.sync.dma_start(w1_codes[:], w1_words[0].rearrange("p i d -> p (i d)").bitcast(I32))
-        for half, gate in enumerate((gate1, gate2)):
-            nc.sync.dma_start(
-                gate_rows[64 * half : 64 * half + 64, :], gate.rearrange("p (b s) -> (p b) s", s=P)[0:64, :]
-            )
+        nc.sync.dma_start(gate_rows[0][:], gate1.rearrange("p (b s) -> (p b) s", s=P)[0:P, :])
         for q in range(4):
             nc.sync.dma_start(
                 w1_plane[32 * q : 32 * q + 4, :].bitcast(I32), w1_scales[0, 4 * q : 4 * q + 4, :].bitcast(I32)
             )
-        nc.sync.dma_start(stream[0][:], xr_rows[:, 0, :])
+        nc.sync.dma_start(gates[0][:], gate1)
+        nc.sync.dma_start(gate_rows[1][:], gate2.rearrange("p (b s) -> (p b) s", s=P)[0:P, :])
         nc.sync.dma_start(list2[:], offs2)
-        nc.sync.dma_start(w2_raw[:], w2.rearrange("(p j) n -> p j n", j=PACK))
-        for t in range(1, PACK):
+        for t in range(PACK):
             nc.sync.dma_start(stream[t][:], xr_rows[:, t, :])
+        nc.sync.dma_start(gates[1][:], gate2)
 
-        nc.tensor.transpose(turn_banks[3][:, 0:P], gate_rows[:], ident[:])
-        nc.scalar.activation(gate_cols[:], turn_banks[3][:, 0:P], COPY)
+        def turn_gate(layer):
+            nc.tensor.transpose(turn_banks[2][:, 0:P], gate_rows[layer][:], ident[:])
+            nc.scalar.activation(gate_cols[layer][:], turn_banks[2][:, 0:BLOCKS], COPY)
 
-        def product(layer, b, codes, plane, w_codes, w_plane):
-            cols = slice(b * P, (b + 1) * P)
-            bank = product_banks[b % 2]
+        def mx(bank_ap, lhs_codes, lhs_plane, rhs_codes, rhs_plane):
             nc.tensor.matmul_mx(
-                out=bank[:],
-                lhsT=codes[:, cols].bitcast(FP8X4),
-                lhsT_scale=plane[:, cols],
-                rhs=w_codes[:].bitcast(FP8X4),
-                rhs_scale=w_plane[:],
+                out=bank_ap,
+                lhsT=lhs_codes.bitcast(FP8X4),
+                lhsT_scale=lhs_plane,
+                rhs=rhs_codes.bitcast(FP8X4),
+                rhs_scale=rhs_plane,
                 start=True,
                 stop=True,
             )
-            g = 64 * layer + b
+
+        def direct(layer, c, codes, plane, w_codes, w_plane):
+            cols = PIECES[c]
+            bank = direct_banks[c % 2][:, 0 : cols.stop - cols.start]
+            mx(bank, w_codes[:, 0:P], w_plane[:, 0:P], codes[:, cols], plane[:, cols])
+            nc.scalar.copy(sums[layer][:, 0, cols], bank)
+
+        def scatter_gated(layer, cols, lst, window):
+            nc.vector.tensor_tensor(
+                window[:].indirect(entries(lst, cols)), sums[layer][:, 0, cols], gates[layer][:, cols], MULT
+            )
+
+        def product(layer, b, codes, plane, w_codes, w_plane, by_plane):
+            cols = slice(b * P, (b + 1) * P)
+            bank = product_banks[b % 3]
+            mx(bank[:], codes[:, cols], plane[:, cols], w_codes[:], w_plane[:])
             nc.scalar.activation(
-                turned[layer][:, b, :, :],
-                bank[:].rearrange("s (m t) -> s t m", t=PACK),
-                COPY,
-                scale=gate_cols[:, g : g + 1],
+                turned[layer][:, b, :, :], by_plane(bank)[:, 1:PACK, :], COPY, scale=gate_cols[layer][:, b : b + 1]
             )
 
-        def turn_back(layer, t, b0, b1):
-            bank = turn_banks[turn_count[0] % 4]
+        def turn_back(layer, t, half):
+            bank = turn_banks[turn_count[0] % 3]
             turn_count[0] += 1
-            for b in range(b0, b1):
-                nc.tensor.transpose(bank[:, (b - b0) * P : (b - b0 + 1) * P], turned[layer][:, b, t, :], ident[:])
-            nc.scalar.copy(gated[layer][:, t, b0 * P : b1 * P], bank[:, 0 : (b1 - b0) * P])
+            b0 = 4 * half
+            for b in range(4):
+                nc.tensor.transpose(bank[:, b * P : (b + 1) * P], turned[layer][:, b0 + b, t - 1, :], ident[:])
+            nc.scalar.copy(sums[layer][:, t, b0 * P : (b0 + 4) * P], bank[:])
 
-        for c in range(CHUNKS):
-            nc.vector.tensor_copy(x_plane[:, chunk_cols(c)], tok_scales[:].indirect(chunk_list(list1, c)))
-            nc.vector.tensor_copy(
-                x_codes[:, chunk_cols(c)], tok_words[:].bitcast(U32).indirect(chunk_list(list1, c))
-            )
-        for c in range(CHUNKS):
-            for b in (2 * c, 2 * c + 1):
-                product(0, b, x_codes, x_plane, w1_codes, w1_plane)
-            turn_back(0, 0, 2 * c, 2 * c + 2)
-            nc.vector.tensor_copy(spread1[0][:].indirect(chunk_list(list1, c)), gated[0][:, 0, chunk_cols(c)])
+        def turned_planes(layer, codes, plane, w_codes, w_plane, by_plane):
+            for half in range(2):
+                for b in range(4 * half, 4 * half + 4):
+                    product(layer, b, codes, plane, w_codes, w_plane, by_plane)
+                turn_back(layer, 1, half)
+            for t in range(2, PACK):
+                for half in range(2):
+                    turn_back(layer, t, half)
+
+        turn_gate(0)
+        nc.vector.tensor_copy(x_plane[:], tok_scales[:].indirect(list1[:]))
+        for c, cols in enumerate(PIECES):
+            nc.vector.tensor_copy(x_codes[:, cols], tok_words[:].bitcast(U32).indirect(entries(list1, cols)))
             if c == 0:
-                turn_back(0, 1, 0, 2)
-                nc.vector.tensor_copy(spread1[1][:].indirect(chunk_list(list1, c)), gated[0][:, 1, chunk_cols(c)])
-        turn_back(0, 1, 2, 4)
-        turn_back(0, 1, 4, 8)
-        for t in range(2, PACK):
-            turn_back(0, t, 0, 4)
-            turn_back(0, t, 4, 8)
-        nc.gpsimd.tensor_scalar(w2_bf[:], w2_raw[:].rearrange("p j n -> p n j"), 1.0, 0.0, MULT, ADD)
+                nc.vector.tensor_copy(w1_codes0[:], w1_codes[:, 0:K:PACK])
+                nc.vector.tensor_copy(w1_plane0[:], w1_plane[:, 0:K:PACK])
+        for c in range(len(PIECES)):
+            direct(0, c, x_codes, x_plane, w1_codes0, w1_plane0)
+        for cols in HALVES:
+            scatter_gated(0, cols, list1, spread1[0])
+        turned_planes(
+            0, x_codes, x_plane, w1_codes, w1_plane, lambda bank: bank[:].rearrange("s (m t) -> s t m", t=PACK)
+        )
         for t in range(PACK):
-            if t == 1:
-                nc.vector.tensor_copy(spread1[1][:].indirect(list1[:, CHUNK // 16 :]), gated[0][:, t, CHUNK:])
-            if t > 1:
-                nc.vector.tensor_copy(spread1[t % 2][:].indirect(list1[:]), gated[0][:, t, :])
+            if t > 0:
+                nc.vector.tensor_copy(spread1[t % 2][:].indirect(list1[:]), sums[0][:, t, :])
             if t < LAST:
-                for h in range(2):
-                    cols = slice(h * T // 2, (h + 1) * T // 2)
+                stream_bf = staged_tile("stream_bf%d" % t, [P, T], BF16)
+                pieces = 4 if t == LAST - 1 else 2
+                for h in range(pieces):
+                    cols = slice(h * T // pieces, (h + 1) * T // pieces)
                     nc.gpsimd.tensor_tensor(stream[t][:, cols], stream[t][:, cols], spread1[t % 2][:, cols], ADD)
-                    nc.scalar.copy(stream_bf[t][:, cols], stream[t][:, cols])
-            if t < LAST - 1:
-                nc.scalar.activation(r_bf[:, :, t], stream_bf[t][:].indirect(list2[:]), COPY)
+                    nc.scalar.copy(stream_bf[:, cols], stream[t][:, cols])
+                nc.scalar.activation(r_bf[:, :, t], stream_bf[:].indirect(list2[:]), COPY)
+            if t == 0:
+                for h, stage in enumerate((gates[0][:], sums[0][:, 0, :])):
+                    staged = stage.rearrange("p (j n) -> p j n", j=PACK)
+                    nc.sync.dma_start(
+                        staged, w2.rearrange("(p j) n -> p j n", j=PACK)[:, :, h * K // 2 : (h + 1) * K // 2]
+                    )
+                    nc.gpsimd.tensor_scalar(
+                        w2_bf[:].rearrange("p (t m) j -> p t m j", t=PACK)[:, :, h * P // 2 : (h + 1) * P // 2, :],
+                        staged.rearrange("p j (m t) -> p t m j", t=PACK),
+                        1.0,
+                        0.0,
+                        MULT,
+                        ADD,
+                    )
+                turn_gate(1)
+        nc.vector.quantize_mx(
+            out=w2_codes[:].bitcast(FP8X4), scales=w2_plane[:], in_=w2_bf[:].rearrange("p n j -> p (n j)")
+        )
         nc.vector.tensor_tensor(stream[LAST][:], stream[LAST][:], spread1[LAST % 2][:], ADD)
 
-        for c in range(CHUNKS):
-            nc.vector.tensor_copy(r_last[:, chunk_cols(c)], stream[LAST][:].indirect(chunk_list(list2, c)))
-            if c == 0:
-                nc.vector.quantize_mx(
-                    out=w2_codes[:].bitcast(FP8X4), scales=w2_plane[:], in_=w2_bf[:].rearrange("p n j -> p (n j)")
-                )
-            nc.scalar.activation(
-                r_bf[:, chunk_cols(c), LAST - 1], stream_bf[LAST - 1][:].indirect(chunk_list(list2, c)), COPY
-            )
-            nc.scalar.copy(r_bf[:, chunk_cols(c), LAST], r_last[:, chunk_cols(c)])
+        r_last = staged_tile("r_last", [P, S], F32)
+        for c, cols in enumerate(QUARTERS):
+            nc.vector.tensor_copy(r_last[:, cols], stream[LAST][:].indirect(entries(list2, cols)))
+            nc.scalar.copy(r_bf[:, cols, LAST], r_last[:, cols])
             nc.vector.quantize_mx(
-                out=r_codes[:, chunk_cols(c)].bitcast(FP8X4),
-                scales=r_plane[:, chunk_cols(c)],
-                in_=r_bf[:, chunk_cols(c), :].rearrange("p s j -> p (s j)"),
+                out=r_codes[:, cols].bitcast(FP8X4),
+                scales=r_plane[:, cols],
+                in_=r_bf[:, cols, :].rearrange("p s j -> p (s j)"),
             )
-            for b in (2 * c, 2 * c + 1):
-                product(1, b, r_codes, r_plane, w2_codes, w2_plane)
-            turn_back(1, 0, 2 * c, 2 * c + 2)
-            nc.vector.tensor_copy(spread2[0][:].indirect(chunk_list(list2, c)), gated[1][:, 0, chunk_cols(c)])
-            if c == 0:
-                turn_back(1, 1, 0, 2)
-                nc.vector.tensor_copy(spread2[1][:].indirect(chunk_list(list2, c)), gated[1][:, 1, chunk_cols(c)])
-        turn_back(1, 1, 2, 4)
-        turn_back(1, 1, 4, 8)
-        for t in range(2, PACK):
-            turn_back(1, t, 0, 4)
-            turn_back(1, t, 4, 8)
-        nc.gpsimd.tensor_tensor(last_sum[:], gated[1][:, LAST, :], r_last[:], ADD)
+            if c != 2:
+                piece = min(c, 2)
+                direct(1, piece, r_codes, r_plane, w2_codes, w2_plane)
+                scatter_gated(1, PIECES[piece], list2, spread2[0])
+        turned_planes(
+            1, r_codes, r_plane, w2_codes, w2_plane, lambda bank: bank[:].rearrange("s (t m) -> s t m", t=PACK)
+        )
         for t in range(LAST):
             if t == 1:
-                nc.vector.tensor_copy(spread2[1][:].indirect(list2[:, CHUNK // 16 :]), gated[1][:, t, CHUNK:])
+                for cols in HALVES:
+                    nc.vector.tensor_copy(spread2[1][:].indirect(entries(list2, cols)), sums[1][:, t, cols])
             if t > 1:
-                nc.vector.tensor_copy(spread2[t % 2][:].indirect(list2[:]), gated[1][:, t, :])
-            for h in range(2):
-                cols = slice(h * T // 2, (h + 1) * T // 2)
-                nc.gpsimd.tensor_tensor(stream[t][:, cols], stream[t][:, cols], spread2[t % 2][:, cols], ADD)
-                nc.sync.dma_start(out_rows[:, t, cols], stream[t][:, cols])
+                nc.vector.tensor_copy(spread2[t % 2][:].indirect(list2[:]), sums[1][:, t, :])
+            pieces = 4 if t == LAST - 1 else 1
+            result = staged_tile("result1", [P, T], F32) if t == 1 else stream[max(t - 1, 0)]
+            for h in range(pieces):
+                cols = slice(h * T // pieces, (h + 1) * T // pieces)
+                nc.gpsimd.tensor_tensor(result[:, cols], stream[t][:, cols], spread2[t % 2][:, cols], ADD)
+                nc.sync.dma_start(out_rows[:, t, cols], result[:, cols])
+            if t == 0:
+                nc.gpsimd.tensor_tensor(last_sum[:], sums[1][:, LAST, :], r_last[:], ADD)
         nc.vector.tensor_copy(stream[LAST][:].indirect(list2[:]), last_sum[:])
-        nc.sync.dma_start(out_rows[:, LAST, :], stream[LAST][:])
+        for h in range(4):
+            cols = slice(h * T // 4, (h + 1) * T // 4)
+            nc.scalar.dma_start(out_rows[:, LAST, cols], stream[LAST][:, cols])

@@ -21,6 +21,7 @@ P = 128
 PACK = 4
 QUARTERS = [slice(c * S // 4, (c + 1) * S // 4) for c in range(4)]
 HALVES = [slice(0, S // 2), slice(S // 2, S)]
+WHOLE = [slice(0, S)]
 PIECES = [QUARTERS[0], QUARTERS[1], HALVES[1]]
 BLOCKS = S // P
 LAST = PACK - 1
@@ -32,13 +33,22 @@ def tile_moe_mod_none_kernel(
     nc = tc.nc
     with ExitStack() as ctx:
         keep = ctx.enter_context(tc.tile_pool(name="keep", bufs=1))
+        relay = ctx.enter_context(tc.tile_pool(name="relay", bufs=1))
         psum = ctx.enter_context(tc.psum_pool(name="psum", bufs=1))
 
         def sbuf(name, shape, dtype):
             return keep.tile(shape, dtype, name=name, align_bytes=64)
 
-        def staged_tile(name, shape, dtype):
-            return keep.tile(shape, dtype, name=name, tag="staged", align_bytes=64)
+        def staged_tile(name, shape, dtype, offset=0):
+            return relay.tile(shape, dtype, name=name, offset=offset, align_bytes=64)
+
+        def width(cols):
+            return cols.stop - cols.start
+
+        def within(pieces, tiles, cols):
+            for piece, tile in zip(pieces, tiles):
+                if piece.start <= cols.start and cols.stop <= piece.stop:
+                    return tile[:, cols.start - piece.start : cols.stop - piece.start]
 
         list1 = sbuf("list1", [P, S // 16], U16)
         list2 = sbuf("list2", [P, S // 16], U16)
@@ -53,18 +63,28 @@ def tile_moe_mod_none_kernel(
         gate_cols = [sbuf("gate_cols%d" % l, [P, BLOCKS], F32) for l in range(2)]
         ident = sbuf("ident", [P, P], F32)
         w2_bf = sbuf("w2_bf", [P, K, PACK], BF16)
-        w2_codes = sbuf("w2_codes", [P, K], U32)
         w2_plane = sbuf("w2_plane", [P, K], U8)
         stream = [sbuf("stream%d" % t, [P, T], F32) for t in range(PACK)]
         spread1 = [sbuf("spread1_%d" % i, [P, T], F32) for i in range(2)]
         spread2 = [sbuf("spread2_%d" % i, [P, T], F32) for i in range(2)]
-        x_codes = sbuf("x_codes", [P, S], U32)
+        x_codes = [sbuf("x_codes%d" % c, [P, width(cols)], U32) for c, cols in enumerate(PIECES)]
         x_plane = sbuf("x_plane", [P, S], U8)
         r_bf = sbuf("r_bf", [P, S, PACK], BF16)
         r_codes = sbuf("r_codes", [P, S], U32)
         r_plane = sbuf("r_plane", [P, S], U8)
         turned = [staged_tile("turned0", [P, BLOCKS, LAST, P], F32), sbuf("turned1", [P, BLOCKS, LAST, P], F32)]
-        sums = [sbuf("sums%d" % l, [P, PACK, S], F32) for l in range(2)]
+        cuts = [[HALVES, WHOLE, WHOLE, WHOLE], [PIECES, HALVES, WHOLE, WHOLE]]
+        sums = [
+            [
+                [sbuf("sums%d_%d_%d" % (l, t, c), [P, width(cols)], F32) for c, cols in enumerate(cuts[l][t])]
+                for t in range(PACK)
+            ]
+            for l in range(2)
+        ]
+
+        def sums_at(layer, t, cols):
+            return within(cuts[layer][t], sums[layer][t], cols)
+
         last_sum = sbuf("last_sum", [P, S], F32)
 
         direct_banks = [psum.tile([P, K], F32, name="direct%d" % i) for i in range(2)]
@@ -75,30 +95,32 @@ def tile_moe_mod_none_kernel(
         def entries(lst, cols):
             return lst[:, cols.start // 16 : cols.stop // 16]
 
-        nc.vector.memset(tok_scales[:].bitcast(I32), 0)
-        nc.vector.memset(w1_plane[:].bitcast(I32), 0)
+        nc.gpsimd.memset(tok_scales[:].bitcast(I32), 0)
+        nc.gpsimd.memset(w1_plane[:].bitcast(I32), 0)
         make_identity(nc, ident[:])
-        for tile in spread1 + spread2:
-            nc.gpsimd.memset(tile[:], 0.0)
+        nc.gpsimd.memset(spread1[0][:], 0.0)
+        nc.vector.memset(spread1[1][:], 0.0)
+        for tile in spread2:
+            nc.scalar.copy(tile[:], spread1[1][:])
 
         xr_rows = xr.rearrange("(p t) n -> p t n", t=PACK)
         out_rows = out.rearrange("(p t) n -> p t n", t=PACK)
 
         nc.sync.dma_start(list1[:], offs)
+        nc.sync.dma_start(list2[:], offs2)
+        nc.sync.dma_start(gate_rows[0][:], gate1.rearrange("p (b s) -> (p b) s", s=P)[0:P, :])
         for q in range(4):
             nc.sync.dma_start(
                 tok_scales[32 * q : 32 * q + 4, :].bitcast(I32), x_scales[0, 4 * q : 4 * q + 4, :].bitcast(I32)
             )
         nc.sync.dma_start(tok_words[:], x_words[0].rearrange("p t d -> p (t d)").bitcast(I32))
         nc.sync.dma_start(w1_codes[:], w1_words[0].rearrange("p i d -> p (i d)").bitcast(I32))
-        nc.sync.dma_start(gate_rows[0][:], gate1.rearrange("p (b s) -> (p b) s", s=P)[0:P, :])
         for q in range(4):
             nc.sync.dma_start(
                 w1_plane[32 * q : 32 * q + 4, :].bitcast(I32), w1_scales[0, 4 * q : 4 * q + 4, :].bitcast(I32)
             )
         nc.sync.dma_start(gates[0][:], gate1)
         nc.sync.dma_start(gate_rows[1][:], gate2.rearrange("p (b s) -> (p b) s", s=P)[0:P, :])
-        nc.sync.dma_start(list2[:], offs2)
         for t in range(PACK):
             nc.sync.dma_start(stream[t][:], xr_rows[:, t, :])
         nc.sync.dma_start(gates[1][:], gate2)
@@ -106,6 +128,12 @@ def tile_moe_mod_none_kernel(
         def turn_gate(layer):
             nc.tensor.transpose(turn_banks[2][:, 0:P], gate_rows[layer][:], ident[:])
             nc.scalar.activation(gate_cols[layer][:], turn_banks[2][:, 0:BLOCKS], COPY)
+
+        def x_codes_at(cols):
+            return within(PIECES, x_codes, cols)
+
+        def r_codes_at(cols):
+            return r_codes[:, cols]
 
         def mx(bank_ap, lhs_codes, lhs_plane, rhs_codes, rhs_plane):
             nc.tensor.matmul_mx(
@@ -121,18 +149,18 @@ def tile_moe_mod_none_kernel(
         def direct(layer, c, codes, plane, w_codes, w_plane):
             cols = PIECES[c]
             bank = direct_banks[c % 2][:, 0 : cols.stop - cols.start]
-            mx(bank, w_codes[:, 0:P], w_plane[:, 0:P], codes[:, cols], plane[:, cols])
-            nc.scalar.copy(sums[layer][:, 0, cols], bank)
+            mx(bank, w_codes[:, 0:P], w_plane[:, 0:P], codes(cols), plane[:, cols])
+            nc.scalar.copy(sums_at(layer, 0, cols), bank)
 
         def scatter_gated(layer, cols, lst, window):
             nc.vector.tensor_tensor(
-                window[:].indirect(entries(lst, cols)), sums[layer][:, 0, cols], gates[layer][:, cols], MULT
+                window[:].indirect(entries(lst, cols)), sums_at(layer, 0, cols), gates[layer][:, cols], MULT
             )
 
         def product(layer, b, codes, plane, w_codes, w_plane, by_plane):
             cols = slice(b * P, (b + 1) * P)
             bank = product_banks[b % 3]
-            mx(bank[:], codes[:, cols], plane[:, cols], w_codes[:], w_plane[:])
+            mx(bank[:], codes(cols), plane[:, cols], w_codes[:], w_plane[:])
             nc.scalar.activation(
                 turned[layer][:, b, :, :], by_plane(bank)[:, 1:PACK, :], COPY, scale=gate_cols[layer][:, b : b + 1]
             )
@@ -143,7 +171,7 @@ def tile_moe_mod_none_kernel(
             b0 = 4 * half
             for b in range(4):
                 nc.tensor.transpose(bank[:, b * P : (b + 1) * P], turned[layer][:, b0 + b, t - 1, :], ident[:])
-            nc.scalar.copy(sums[layer][:, t, b0 * P : (b0 + 4) * P], bank[:])
+            nc.scalar.copy(sums_at(layer, t, HALVES[half]), bank[:])
 
         def turned_planes(layer, codes, plane, w_codes, w_plane, by_plane):
             for half in range(2):
@@ -155,22 +183,22 @@ def tile_moe_mod_none_kernel(
                     turn_back(layer, t, half)
 
         turn_gate(0)
-        nc.vector.tensor_copy(x_plane[:], tok_scales[:].indirect(list1[:]))
         for c, cols in enumerate(PIECES):
-            nc.vector.tensor_copy(x_codes[:, cols], tok_words[:].bitcast(U32).indirect(entries(list1, cols)))
+            nc.vector.tensor_copy(x_plane[:, cols], tok_scales[:].indirect(entries(list1, cols)))
+            nc.vector.tensor_copy(x_codes[c][:], tok_words[:].bitcast(U32).indirect(entries(list1, cols)))
             if c == 0:
-                nc.vector.tensor_copy(w1_codes0[:], w1_codes[:, 0:K:PACK])
-                nc.vector.tensor_copy(w1_plane0[:], w1_plane[:, 0:K:PACK])
+                nc.gpsimd.tensor_copy(w1_codes0[:], w1_codes[:, 0:K:PACK])
+                nc.gpsimd.tensor_copy(w1_plane0[:], w1_plane[:, 0:K:PACK])
         for c in range(len(PIECES)):
-            direct(0, c, x_codes, x_plane, w1_codes0, w1_plane0)
+            direct(0, c, x_codes_at, x_plane, w1_codes0, w1_plane0)
         for cols in HALVES:
             scatter_gated(0, cols, list1, spread1[0])
         turned_planes(
-            0, x_codes, x_plane, w1_codes, w1_plane, lambda bank: bank[:].rearrange("s (m t) -> s t m", t=PACK)
+            0, x_codes_at, x_plane, w1_codes, w1_plane, lambda bank: bank[:].rearrange("s (m t) -> s t m", t=PACK)
         )
         for t in range(PACK):
             if t > 0:
-                nc.vector.tensor_copy(spread1[t % 2][:].indirect(list1[:]), sums[0][:, t, :])
+                nc.vector.tensor_copy(spread1[t % 2][:].indirect(list1[:]), sums[0][t][0][:])
             if t < LAST:
                 stream_bf = staged_tile("stream_bf%d" % t, [P, T], BF16)
                 pieces = 4 if t == LAST - 1 else 2
@@ -179,30 +207,34 @@ def tile_moe_mod_none_kernel(
                     nc.gpsimd.tensor_tensor(stream[t][:, cols], stream[t][:, cols], spread1[t % 2][:, cols], ADD)
                     nc.scalar.copy(stream_bf[:, cols], stream[t][:, cols])
                 nc.scalar.activation(r_bf[:, :, t], stream_bf[:].indirect(list2[:]), COPY)
+            if t < 2:
+                staged = (gates[0], sums[0][1][0])[t][:].rearrange("p (j n) -> p j n", j=PACK)
+                nc.sync.dma_start(
+                    staged, w2.rearrange("(p j) n -> p j n", j=PACK)[:, :, t * K // 2 : (t + 1) * K // 2]
+                )
+                nc.gpsimd.tensor_scalar(
+                    w2_bf[:].rearrange("p (u m) j -> p u m j", u=PACK)[:, :, t * P // 2 : (t + 1) * P // 2, :],
+                    staged.rearrange("p j (m u) -> p u m j", u=PACK),
+                    1.0,
+                    0.0,
+                    MULT,
+                    ADD,
+                )
             if t == 0:
-                for h, stage in enumerate((gates[0][:], sums[0][:, 0, :])):
-                    staged = stage.rearrange("p (j n) -> p j n", j=PACK)
-                    nc.sync.dma_start(
-                        staged, w2.rearrange("(p j) n -> p j n", j=PACK)[:, :, h * K // 2 : (h + 1) * K // 2]
-                    )
-                    nc.gpsimd.tensor_scalar(
-                        w2_bf[:].rearrange("p (t m) j -> p t m j", t=PACK)[:, :, h * P // 2 : (h + 1) * P // 2, :],
-                        staged.rearrange("p j (m t) -> p t m j", t=PACK),
-                        1.0,
-                        0.0,
-                        MULT,
-                        ADD,
-                    )
                 turn_gate(1)
+        nc.vector.tensor_tensor(stream[LAST][:], stream[LAST][:], spread1[LAST % 2][:], ADD)
+        w2_codes = keep.tile([P, K], U32, name="w2_codes", tag="sums0_3_0", align_bytes=64)
         nc.vector.quantize_mx(
             out=w2_codes[:].bitcast(FP8X4), scales=w2_plane[:], in_=w2_bf[:].rearrange("p n j -> p (n j)")
         )
-        nc.vector.tensor_tensor(stream[LAST][:], stream[LAST][:], spread1[LAST % 2][:], ADD)
 
-        r_last = staged_tile("r_last", [P, S], F32)
+        r_last = [
+            staged_tile("r_last%d" % c, [P, width(cols)], F32, 4 * cols.start) for c, cols in enumerate(PIECES)
+        ]
         for c, cols in enumerate(QUARTERS):
-            nc.vector.tensor_copy(r_last[:, cols], stream[LAST][:].indirect(entries(list2, cols)))
-            nc.scalar.copy(r_bf[:, cols, LAST], r_last[:, cols])
+            if c < len(PIECES):
+                nc.vector.tensor_copy(r_last[c][:], stream[LAST][:].indirect(entries(list2, PIECES[c])))
+            nc.scalar.copy(r_bf[:, cols, LAST], within(PIECES, r_last, cols))
             nc.vector.quantize_mx(
                 out=r_codes[:, cols].bitcast(FP8X4),
                 scales=r_plane[:, cols],
@@ -210,17 +242,17 @@ def tile_moe_mod_none_kernel(
             )
             if c != 2:
                 piece = min(c, 2)
-                direct(1, piece, r_codes, r_plane, w2_codes, w2_plane)
+                direct(1, piece, r_codes_at, r_plane, w2_codes, w2_plane)
                 scatter_gated(1, PIECES[piece], list2, spread2[0])
         turned_planes(
-            1, r_codes, r_plane, w2_codes, w2_plane, lambda bank: bank[:].rearrange("s (t m) -> s t m", t=PACK)
+            1, r_codes_at, r_plane, w2_codes, w2_plane, lambda bank: bank[:].rearrange("s (t m) -> s t m", t=PACK)
         )
         for t in range(LAST):
             if t == 1:
                 for cols in HALVES:
-                    nc.vector.tensor_copy(spread2[1][:].indirect(entries(list2, cols)), sums[1][:, t, cols])
+                    nc.vector.tensor_copy(spread2[1][:].indirect(entries(list2, cols)), sums_at(1, t, cols))
             if t > 1:
-                nc.vector.tensor_copy(spread2[t % 2][:].indirect(list2[:]), sums[1][:, t, :])
+                nc.vector.tensor_copy(spread2[t % 2][:].indirect(list2[:]), sums[1][t][0][:])
             pieces = 4 if t == LAST - 1 else 1
             result = staged_tile("result1", [P, T], F32) if t == 1 else stream[max(t - 1, 0)]
             for h in range(pieces):
@@ -228,7 +260,8 @@ def tile_moe_mod_none_kernel(
                 nc.gpsimd.tensor_tensor(result[:, cols], stream[t][:, cols], spread2[t % 2][:, cols], ADD)
                 nc.sync.dma_start(out_rows[:, t, cols], result[:, cols])
             if t == 0:
-                nc.gpsimd.tensor_tensor(last_sum[:], sums[1][:, LAST, :], r_last[:], ADD)
+                for c, cols in enumerate(PIECES):
+                    nc.gpsimd.tensor_tensor(last_sum[:, cols], sums_at(1, LAST, cols), r_last[c][:], ADD)
         nc.vector.tensor_copy(stream[LAST][:].indirect(list2[:]), last_sum[:])
         for h in range(4):
             cols = slice(h * T // 4, (h + 1) * T // 4)

@@ -213,8 +213,8 @@ def tile_moe_mod_none_kernel(
                     staged, w2.rearrange("(p j) n -> p j n", j=PACK)[:, :, t * K // 2 : (t + 1) * K // 2]
                 )
                 nc.gpsimd.tensor_scalar(
-                    w2_bf[:].rearrange("p (u m) j -> p u m j", u=PACK)[:, :, t * P // 2 : (t + 1) * P // 2, :],
-                    staged.rearrange("p j (m u) -> p u m j", u=PACK),
+                    w2_bf[:].rearrange("p (u m) j -> p m u j", u=PACK)[:, t * P // 2 : (t + 1) * P // 2, :, :],
+                    staged.rearrange("p j (m u) -> p m u j", u=PACK),
                     1.0,
                     0.0,
                     MULT,
@@ -253,7 +253,7 @@ def tile_moe_mod_none_kernel(
                     nc.vector.tensor_copy(spread2[1][:].indirect(entries(list2, cols)), sums_at(1, t, cols))
             if t > 1:
                 nc.vector.tensor_copy(spread2[t % 2][:].indirect(list2[:]), sums[1][t][0][:])
-            pieces = 4 if t == LAST - 1 else 1
+            pieces = 4 if t == LAST - 1 else 2
             result = staged_tile("result1", [P, T], F32) if t == 1 else stream[max(t - 1, 0)]
             for h in range(pieces):
                 cols = slice(h * T // pieces, (h + 1) * T // pieces)

@@ -19,12 +19,25 @@ MULT = mybir.AluOpType.mult
 
 P = 128
 PACK = 4
+LAST = PACK - 1
+GROUP = 16
+QUADRANTS = 4
+BLOCKS = S // P
+BANK_BLOCKS = 4
+
 QUARTERS = [slice(c * S // 4, (c + 1) * S // 4) for c in range(4)]
 HALVES = [slice(0, S // 2), slice(S // 2, S)]
 WHOLE = [slice(0, S)]
 PIECES = [QUARTERS[0], QUARTERS[1], HALVES[1]]
-BLOCKS = S // P
-LAST = PACK - 1
+
+
+def token_cuts(*bounds):
+    return [slice(a, b) for a, b in zip(bounds, bounds[1:])]
+
+
+TOKEN_HALVES = token_cuts(0, T // 2, T)
+PLANE2_CUTS_LAYER1 = token_cuts(0, 1024, 1792, T)
+PLANE2_CUTS_LAYER2 = token_cuts(0, 1024, 1536, T)
 
 
 def tile_moe_mod_none_kernel(
@@ -39,47 +52,49 @@ def tile_moe_mod_none_kernel(
         def sbuf(name, shape, dtype):
             return keep.tile(shape, dtype, name=name, align_bytes=64)
 
-        def staged_tile(name, shape, dtype, offset=0):
+        def relay_tile(name, shape, dtype, offset=0):
             return relay.tile(shape, dtype, name=name, offset=offset, align_bytes=64)
 
         def width(cols):
             return cols.stop - cols.start
 
         def within(pieces, tiles, cols):
-            for piece, tile in zip(pieces, tiles):
-                if piece.start <= cols.start and cols.stop <= piece.stop:
-                    return tile[:, cols.start - piece.start : cols.stop - piece.start]
+            c = max(i for i, piece in enumerate(pieces) if piece.start <= cols.start)
+            return tiles[c][:, cols.start - pieces[c].start : cols.stop - pieces[c].start]
 
-        list1 = sbuf("list1", [P, S // 16], U16)
-        list2 = sbuf("list2", [P, S // 16], U16)
+        def entries(lst, cols):
+            return lst[:, cols.start // GROUP : cols.stop // GROUP]
+
+        list1 = sbuf("list1", [P, S // GROUP], U16)
+        list2 = sbuf("list2", [P, S // GROUP], U16)
         tok_words = sbuf("tok_words", [P, T], I32)
         tok_scales = sbuf("tok_scales", [P, T], U8)
         w1_codes = sbuf("w1_codes", [P, K], I32)
-        w1_plane = sbuf("w1_plane", [P, K], U8)
+        w1_scale = sbuf("w1_scale", [P, K], U8)
         w1_codes0 = sbuf("w1_codes0", [P, P], I32)
-        w1_plane0 = sbuf("w1_plane0", [P, P], U8)
-        gates = [sbuf("gate%d" % l, [P, S], F32) for l in range(2)]
-        gate_rows = [sbuf("gate_rows%d" % l, [P, P], F32) for l in range(2)]
-        gate_cols = [sbuf("gate_cols%d" % l, [P, BLOCKS], F32) for l in range(2)]
+        w1_scale0 = sbuf("w1_scale0", [P, P], U8)
+        gates = [sbuf("gate%d" % layer, [P, S], F32) for layer in range(2)]
+        gate_rows = [sbuf("gate_rows%d" % layer, [P, P], F32) for layer in range(2)]
+        gate_cols = [sbuf("gate_cols%d" % layer, [P, BLOCKS], F32) for layer in range(2)]
         ident = sbuf("ident", [P, P], F32)
         w2_bf = sbuf("w2_bf", [P, K, PACK], BF16)
-        w2_plane = sbuf("w2_plane", [P, K], U8)
+        w2_scale = sbuf("w2_scale", [P, K], U8)
         stream = [sbuf("stream%d" % t, [P, T], F32) for t in range(PACK)]
         spread1 = [sbuf("spread1_%d" % i, [P, T], F32) for i in range(2)]
         spread2 = [sbuf("spread2_%d" % i, [P, T], F32) for i in range(2)]
         x_codes = [sbuf("x_codes%d" % c, [P, width(cols)], U32) for c, cols in enumerate(PIECES)]
-        x_plane = sbuf("x_plane", [P, S], U8)
+        x_scale = sbuf("x_scale", [P, S], U8)
         r_bf = sbuf("r_bf", [P, S, PACK], BF16)
         r_codes = sbuf("r_codes", [P, S], U32)
-        r_plane = sbuf("r_plane", [P, S], U8)
-        turned = [staged_tile("turned0", [P, BLOCKS, LAST, P], F32), sbuf("turned1", [P, BLOCKS, LAST, P], F32)]
-        cuts = [[HALVES, WHOLE, WHOLE, WHOLE], [PIECES, HALVES, WHOLE, WHOLE]]
+        r_scale = sbuf("r_scale", [P, S], U8)
+        turned = [relay_tile("turned0", [P, BLOCKS, LAST, P], F32), sbuf("turned1", [P, BLOCKS, LAST, P], F32)]
+        cuts = [[HALVES, WHOLE, WHOLE, WHOLE], [PIECES, WHOLE, WHOLE, WHOLE]]
         sums = [
             [
-                [sbuf("sums%d_%d_%d" % (l, t, c), [P, width(cols)], F32) for c, cols in enumerate(cuts[l][t])]
+                [sbuf("sums%d_%d_%d" % (layer, t, c), [P, width(cols)], F32) for c, cols in enumerate(cuts[layer][t])]
                 for t in range(PACK)
             ]
-            for l in range(2)
+            for layer in range(2)
         ]
 
         def sums_at(layer, t, cols):
@@ -90,13 +105,9 @@ def tile_moe_mod_none_kernel(
         direct_banks = [psum.tile([P, K], F32, name="direct%d" % i) for i in range(2)]
         product_banks = [psum.tile([P, K], F32, name="product%d" % i) for i in range(3)]
         turn_banks = [psum.tile([P, K], F32, name="turn%d" % i) for i in range(3)]
-        turn_count = [0]
-
-        def entries(lst, cols):
-            return lst[:, cols.start // 16 : cols.stop // 16]
 
         nc.gpsimd.memset(tok_scales[:].bitcast(I32), 0)
-        nc.gpsimd.memset(w1_plane[:].bitcast(I32), 0)
+        nc.gpsimd.memset(w1_scale[:].bitcast(I32), 0)
         make_identity(nc, ident[:])
         nc.gpsimd.memset(spread1[0][:], 0.0)
         nc.vector.memset(spread1[1][:], 0.0)
@@ -106,28 +117,31 @@ def tile_moe_mod_none_kernel(
         xr_rows = xr.rearrange("(p t) n -> p t n", t=PACK)
         out_rows = out.rearrange("(p t) n -> p t n", t=PACK)
 
+        def load_scales(tile, scales):
+            for q in range(QUADRANTS):
+                nc.sync.dma_start(
+                    tile[32 * q : 32 * q + 4, :].bitcast(I32), scales[0, 4 * q : 4 * q + 4, :].bitcast(I32)
+                )
+
+        def load_gate_rows(layer, gate):
+            nc.sync.dma_start(gate_rows[layer][:], gate.rearrange("p (b s) -> (p b) s", s=P)[0:P, :])
+
         nc.sync.dma_start(list1[:], offs)
         nc.sync.dma_start(list2[:], offs2)
-        nc.sync.dma_start(gate_rows[0][:], gate1.rearrange("p (b s) -> (p b) s", s=P)[0:P, :])
-        for q in range(4):
-            nc.sync.dma_start(
-                tok_scales[32 * q : 32 * q + 4, :].bitcast(I32), x_scales[0, 4 * q : 4 * q + 4, :].bitcast(I32)
-            )
+        load_gate_rows(0, gate1)
+        load_scales(tok_scales, x_scales)
         nc.sync.dma_start(tok_words[:], x_words[0].rearrange("p t d -> p (t d)").bitcast(I32))
         nc.sync.dma_start(w1_codes[:], w1_words[0].rearrange("p i d -> p (i d)").bitcast(I32))
-        for q in range(4):
-            nc.sync.dma_start(
-                w1_plane[32 * q : 32 * q + 4, :].bitcast(I32), w1_scales[0, 4 * q : 4 * q + 4, :].bitcast(I32)
-            )
+        load_scales(w1_scale, w1_scales)
         nc.sync.dma_start(gates[0][:], gate1)
-        nc.sync.dma_start(gate_rows[1][:], gate2.rearrange("p (b s) -> (p b) s", s=P)[0:P, :])
+        load_gate_rows(1, gate2)
         for t in range(PACK):
             nc.sync.dma_start(stream[t][:], xr_rows[:, t, :])
         nc.sync.dma_start(gates[1][:], gate2)
 
         def turn_gate(layer):
-            nc.tensor.transpose(turn_banks[2][:, 0:P], gate_rows[layer][:], ident[:])
-            nc.scalar.activation(gate_cols[layer][:], turn_banks[2][:, 0:BLOCKS], COPY)
+            nc.tensor.transpose(turn_banks[-1][:, 0:P], gate_rows[layer][:], ident[:])
+            nc.scalar.activation(gate_cols[layer][:], turn_banks[-1][:, 0:BLOCKS], COPY)
 
         def x_codes_at(cols):
             return within(PIECES, x_codes, cols)
@@ -135,21 +149,21 @@ def tile_moe_mod_none_kernel(
         def r_codes_at(cols):
             return r_codes[:, cols]
 
-        def mx(bank_ap, lhs_codes, lhs_plane, rhs_codes, rhs_plane):
+        def mx(bank, lhs_codes, lhs_scale, rhs_codes, rhs_scale):
             nc.tensor.matmul_mx(
-                out=bank_ap,
+                out=bank,
                 lhsT=lhs_codes.bitcast(FP8X4),
-                lhsT_scale=lhs_plane,
+                lhsT_scale=lhs_scale,
                 rhs=rhs_codes.bitcast(FP8X4),
-                rhs_scale=rhs_plane,
+                rhs_scale=rhs_scale,
                 start=True,
                 stop=True,
             )
 
-        def direct(layer, c, codes, plane, w_codes, w_plane):
+        def direct(layer, c, codes_at, scale, w_codes, w_scale):
             cols = PIECES[c]
-            bank = direct_banks[c % 2][:, 0 : cols.stop - cols.start]
-            mx(bank, w_codes[:, 0:P], w_plane[:, 0:P], codes(cols), plane[:, cols])
+            bank = direct_banks[c % len(direct_banks)][:, 0 : width(cols)]
+            mx(bank, w_codes[:, 0:P], w_scale[:, 0:P], codes_at(cols), scale[:, cols])
             nc.scalar.copy(sums_at(layer, 0, cols), bank)
 
         def scatter_gated(layer, cols, lst, window):
@@ -157,112 +171,105 @@ def tile_moe_mod_none_kernel(
                 window[:].indirect(entries(lst, cols)), sums_at(layer, 0, cols), gates[layer][:, cols], MULT
             )
 
-        def product(layer, b, codes, plane, w_codes, w_plane, by_plane):
+        def product(layer, b, codes_at, scale, w_codes, w_scale, by_plane):
             cols = slice(b * P, (b + 1) * P)
-            bank = product_banks[b % 3]
-            mx(bank[:], codes(cols), plane[:, cols], w_codes[:], w_plane[:])
+            bank = product_banks[b % len(product_banks)]
+            mx(bank[:], codes_at(cols), scale[:, cols], w_codes[:], w_scale[:])
             nc.scalar.activation(
-                turned[layer][:, b, :, :], by_plane(bank)[:, 1:PACK, :], COPY, scale=gate_cols[layer][:, b : b + 1]
+                turned[layer][:, b, :, :],
+                bank[:].rearrange(by_plane, t=PACK)[:, 1:PACK, :],
+                COPY,
+                scale=gate_cols[layer][:, b : b + 1],
             )
 
         def turn_back(layer, t, half):
-            bank = turn_banks[turn_count[0] % 3]
-            turn_count[0] += 1
-            b0 = 4 * half
-            for b in range(4):
-                nc.tensor.transpose(bank[:, b * P : (b + 1) * P], turned[layer][:, b0 + b, t - 1, :], ident[:])
+            bank = turn_banks[(len(HALVES) * (t - 1) + half) % len(turn_banks)]
+            for j in range(BANK_BLOCKS):
+                block = turned[layer][:, BANK_BLOCKS * half + j, t - 1, :]
+                nc.tensor.transpose(bank[:, j * P : (j + 1) * P], block, ident[:])
             nc.scalar.copy(sums_at(layer, t, HALVES[half]), bank[:])
 
-        def turned_planes(layer, codes, plane, w_codes, w_plane, by_plane):
-            for half in range(2):
-                for b in range(4 * half, 4 * half + 4):
-                    product(layer, b, codes, plane, w_codes, w_plane, by_plane)
+        def turned_planes(layer, codes_at, scale, w_codes, w_scale, by_plane):
+            for half in range(len(HALVES)):
+                for b in range(BANK_BLOCKS * half, BANK_BLOCKS * (half + 1)):
+                    product(layer, b, codes_at, scale, w_codes, w_scale, by_plane)
                 turn_back(layer, 1, half)
             for t in range(2, PACK):
-                for half in range(2):
+                for half in range(len(HALVES)):
                     turn_back(layer, t, half)
+
+        def round_w2(half, stage):
+            staged = stage[:].rearrange("p (j n) -> p j n", j=PACK)
+            nc.sync.dma_start(
+                staged, w2.rearrange("(p j) n -> p j n", j=PACK)[:, :, half * K // 2 : (half + 1) * K // 2]
+            )
+            nc.gpsimd.tensor_scalar(
+                w2_bf[:].rearrange("p (u m) j -> p m u j", u=PACK)[:, half * P // 2 : (half + 1) * P // 2, :, :],
+                staged.rearrange("p j (m u) -> p m u j", u=PACK),
+                1.0,
+                0.0,
+                MULT,
+                ADD,
+            )
 
         turn_gate(0)
         for c, cols in enumerate(PIECES):
-            nc.vector.tensor_copy(x_plane[:, cols], tok_scales[:].indirect(entries(list1, cols)))
+            nc.vector.tensor_copy(x_scale[:, cols], tok_scales[:].indirect(entries(list1, cols)))
             nc.vector.tensor_copy(x_codes[c][:], tok_words[:].bitcast(U32).indirect(entries(list1, cols)))
             if c == 0:
                 nc.gpsimd.tensor_copy(w1_codes0[:], w1_codes[:, 0:K:PACK])
-                nc.gpsimd.tensor_copy(w1_plane0[:], w1_plane[:, 0:K:PACK])
+                nc.gpsimd.tensor_copy(w1_scale0[:], w1_scale[:, 0:K:PACK])
         for c in range(len(PIECES)):
-            direct(0, c, x_codes_at, x_plane, w1_codes0, w1_plane0)
+            direct(0, c, x_codes_at, x_scale, w1_codes0, w1_scale0)
         for cols in HALVES:
             scatter_gated(0, cols, list1, spread1[0])
-        turned_planes(
-            0, x_codes_at, x_plane, w1_codes, w1_plane, lambda bank: bank[:].rearrange("s (m t) -> s t m", t=PACK)
-        )
+        turned_planes(0, x_codes_at, x_scale, w1_codes, w1_scale, "s (m t) -> s t m")
+        w2_stages = [gates[0], sums[0][1][0]]
         for t in range(PACK):
             if t > 0:
                 nc.vector.tensor_copy(spread1[t % 2][:].indirect(list1[:]), sums[0][t][0][:])
             if t < LAST:
-                stream_bf = staged_tile("stream_bf%d" % t, [P, T], BF16)
-                pieces = 4 if t == LAST - 1 else 2
-                for h in range(pieces):
-                    cols = slice(h * T // pieces, (h + 1) * T // pieces)
+                stream_bf = relay_tile("stream_bf%d" % t, [P, T], BF16)
+                for cols in PLANE2_CUTS_LAYER1 if t == LAST - 1 else TOKEN_HALVES:
                     nc.gpsimd.tensor_tensor(stream[t][:, cols], stream[t][:, cols], spread1[t % 2][:, cols], ADD)
                     nc.scalar.copy(stream_bf[:, cols], stream[t][:, cols])
                 nc.scalar.activation(r_bf[:, :, t], stream_bf[:].indirect(list2[:]), COPY)
-            if t < 2:
-                staged = (gates[0], sums[0][1][0])[t][:].rearrange("p (j n) -> p j n", j=PACK)
-                nc.sync.dma_start(
-                    staged, w2.rearrange("(p j) n -> p j n", j=PACK)[:, :, t * K // 2 : (t + 1) * K // 2]
-                )
-                nc.gpsimd.tensor_scalar(
-                    w2_bf[:].rearrange("p (u m) j -> p m u j", u=PACK)[:, t * P // 2 : (t + 1) * P // 2, :, :],
-                    staged.rearrange("p j (m u) -> p m u j", u=PACK),
-                    1.0,
-                    0.0,
-                    MULT,
-                    ADD,
-                )
+            if t < len(w2_stages):
+                round_w2(t, w2_stages[t])
             if t == 0:
                 turn_gate(1)
         nc.vector.tensor_tensor(stream[LAST][:], stream[LAST][:], spread1[LAST % 2][:], ADD)
-        w2_codes = keep.tile([P, K], U32, name="w2_codes", tag="sums0_3_0", align_bytes=64)
+        w2_codes = keep.tile([P, K], U32, name="w2_codes", tag="sums0_%d_0" % LAST, align_bytes=64)
         nc.vector.quantize_mx(
-            out=w2_codes[:].bitcast(FP8X4), scales=w2_plane[:], in_=w2_bf[:].rearrange("p n j -> p (n j)")
+            out=w2_codes[:].bitcast(FP8X4), scales=w2_scale[:], in_=w2_bf[:].rearrange("p n j -> p (n j)")
         )
 
-        r_last = [
-            staged_tile("r_last%d" % c, [P, width(cols)], F32, 4 * cols.start) for c, cols in enumerate(PIECES)
-        ]
+        r_last = [relay_tile("r_last%d" % c, [P, width(cols)], F32, 4 * cols.start) for c, cols in enumerate(PIECES)]
         for c, cols in enumerate(QUARTERS):
             if c < len(PIECES):
                 nc.vector.tensor_copy(r_last[c][:], stream[LAST][:].indirect(entries(list2, PIECES[c])))
             nc.scalar.copy(r_bf[:, cols, LAST], within(PIECES, r_last, cols))
             nc.vector.quantize_mx(
                 out=r_codes[:, cols].bitcast(FP8X4),
-                scales=r_plane[:, cols],
+                scales=r_scale[:, cols],
                 in_=r_bf[:, cols, :].rearrange("p s j -> p (s j)"),
             )
-            if c != 2:
-                piece = min(c, 2)
-                direct(1, piece, r_codes_at, r_plane, w2_codes, w2_plane)
-                scatter_gated(1, PIECES[piece], list2, spread2[0])
-        turned_planes(
-            1, r_codes_at, r_plane, w2_codes, w2_plane, lambda bank: bank[:].rearrange("s (t m) -> s t m", t=PACK)
-        )
+            for piece, piece_cols in enumerate(PIECES):
+                if piece_cols.stop == cols.stop:
+                    direct(1, piece, r_codes_at, r_scale, w2_codes, w2_scale)
+                    scatter_gated(1, piece_cols, list2, spread2[0])
+        turned_planes(1, r_codes_at, r_scale, w2_codes, w2_scale, "s (t m) -> s t m")
         for t in range(LAST):
-            if t == 1:
-                for cols in HALVES:
-                    nc.vector.tensor_copy(spread2[1][:].indirect(entries(list2, cols)), sums_at(1, t, cols))
-            if t > 1:
-                nc.vector.tensor_copy(spread2[t % 2][:].indirect(list2[:]), sums[1][t][0][:])
-            pieces = 4 if t == LAST - 1 else 2
-            result = staged_tile("result1", [P, T], F32) if t == 1 else stream[max(t - 1, 0)]
-            for h in range(pieces):
-                cols = slice(h * T // pieces, (h + 1) * T // pieces)
+            if t > 0:
+                for cols in cuts[1][t]:
+                    nc.vector.tensor_copy(spread2[t % 2][:].indirect(entries(list2, cols)), sums_at(1, t, cols))
+            result = relay_tile("result1", [P, T], F32) if t == 1 else stream[max(t - 1, 0)]
+            for cols in PLANE2_CUTS_LAYER2 if t == LAST - 1 else TOKEN_HALVES:
                 nc.gpsimd.tensor_tensor(result[:, cols], stream[t][:, cols], spread2[t % 2][:, cols], ADD)
                 nc.sync.dma_start(out_rows[:, t, cols], result[:, cols])
             if t == 0:
                 for c, cols in enumerate(PIECES):
                     nc.gpsimd.tensor_tensor(last_sum[:, cols], sums_at(1, LAST, cols), r_last[c][:], ADD)
         nc.vector.tensor_copy(stream[LAST][:].indirect(list2[:]), last_sum[:])
-        for h in range(4):
-            cols = slice(h * T // 4, (h + 1) * T // 4)
+        for cols in PLANE2_CUTS_LAYER2:
             nc.scalar.dma_start(out_rows[:, LAST, cols], stream[LAST][:, cols])

@@ -77,18 +77,22 @@ def tile_moe_mod_none_kernel(
         gate_rows = [sbuf("gate_rows%d" % layer, [P, P], F32) for layer in range(2)]
         gate_cols = [sbuf("gate_cols%d" % layer, [P, BLOCKS], F32) for layer in range(2)]
         ident = sbuf("ident", [P, P], F32)
-        w2_bf = sbuf("w2_bf", [P, K, PACK], BF16)
+        w2_raw = sbuf("w2_raw", [P, PACK, K], F32)
         w2_scale = sbuf("w2_scale", [P, K], U8)
-        stream = [sbuf("stream%d" % t, [P, T], F32) for t in range(PACK)]
+        w2_codes0 = sbuf("w2_codes0", [P, P], I32)
+        w2_scale0 = sbuf("w2_scale0", [P, P], U8)
+        before = [sbuf("before%d" % t, [P, T], F32) for t in range(PACK)]
+        stream = [sbuf("stream%d" % t, [P, T], F32) for t in range(2)]
+
         spread1 = [sbuf("spread1_%d" % i, [P, T], F32) for i in range(2)]
-        spread2 = [sbuf("spread2_%d" % i, [P, T], F32) for i in range(2)]
+        spread2 = [sbuf("spread2_0", [P, T], F32)]
         x_codes = [sbuf("x_codes%d" % c, [P, width(cols)], U32) for c, cols in enumerate(PIECES)]
         x_scale = sbuf("x_scale", [P, S], U8)
         r_bf = sbuf("r_bf", [P, S, PACK], BF16)
-        r_codes = sbuf("r_codes", [P, S], U32)
+        r_codes = []
         r_scale = sbuf("r_scale", [P, S], U8)
         turned = [relay_tile("turned0", [P, BLOCKS, LAST, P], F32), sbuf("turned1", [P, BLOCKS, LAST, P], F32)]
-        cuts = [[HALVES, WHOLE, WHOLE, WHOLE], [PIECES, WHOLE, WHOLE, WHOLE]]
+        cuts = [[PIECES, WHOLE, WHOLE, WHOLE], [PIECES, HALVES, WHOLE, WHOLE]]
         sums = [
             [
                 [sbuf("sums%d_%d_%d" % (layer, t, c), [P, width(cols)], F32) for c, cols in enumerate(cuts[layer][t])]
@@ -100,19 +104,18 @@ def tile_moe_mod_none_kernel(
         def sums_at(layer, t, cols):
             return within(cuts[layer][t], sums[layer][t], cols)
 
-        last_sum = sbuf("last_sum", [P, S], F32)
 
         direct_banks = [psum.tile([P, K], F32, name="direct%d" % i) for i in range(2)]
         product_banks = [psum.tile([P, K], F32, name="product%d" % i) for i in range(3)]
         turn_banks = [psum.tile([P, K], F32, name="turn%d" % i) for i in range(3)]
 
-        nc.gpsimd.memset(tok_scales[:].bitcast(I32), 0)
-        nc.gpsimd.memset(w1_scale[:].bitcast(I32), 0)
+        nc.vector.memset(tok_scales[:].bitcast(I32), 0)
+        nc.vector.memset(w1_scale[:].bitcast(I32), 0)
         make_identity(nc, ident[:])
+        nc.gpsimd.memset(w2_scale[:].bitcast(I32), 0)
         nc.gpsimd.memset(spread1[0][:], 0.0)
-        nc.vector.memset(spread1[1][:], 0.0)
-        for tile in spread2:
-            nc.scalar.copy(tile[:], spread1[1][:])
+        nc.vector.memset(spread2[0][:], 0.0)
+        nc.scalar.copy(spread1[1][:], spread2[0][:])
 
         xr_rows = xr.rearrange("(p t) n -> p t n", t=PACK)
         out_rows = out.rearrange("(p t) n -> p t n", t=PACK)
@@ -133,10 +136,13 @@ def tile_moe_mod_none_kernel(
         nc.sync.dma_start(tok_words[:], x_words[0].rearrange("p t d -> p (t d)").bitcast(I32))
         nc.sync.dma_start(w1_codes[:], w1_words[0].rearrange("p i d -> p (i d)").bitcast(I32))
         load_scales(w1_scale, w1_scales)
-        nc.sync.dma_start(gates[0][:], gate1)
+        for cols in (PIECES[0], slice(PIECES[0].stop, S)):
+            nc.sync.dma_start(gates[0][:, cols], gate1[:, cols])
         load_gate_rows(1, gate2)
-        for t in range(PACK):
-            nc.sync.dma_start(stream[t][:], xr_rows[:, t, :])
+        nc.sync.dma_start(before[0][:], xr_rows[:, 0, :])
+        nc.sync.dma_start(w2_raw[:], w2.rearrange("(p j) n -> p j n", j=PACK))
+        for t in range(1, PACK):
+            nc.sync.dma_start(before[t][:, 0:T], xr_rows[:, t, :])
         nc.sync.dma_start(gates[1][:], gate2)
 
         def turn_gate(layer):
@@ -147,7 +153,7 @@ def tile_moe_mod_none_kernel(
             return within(PIECES, x_codes, cols)
 
         def r_codes_at(cols):
-            return r_codes[:, cols]
+            return within(PIECES, r_codes, cols)
 
         def mx(bank, lhs_codes, lhs_scale, rhs_codes, rhs_scale):
             nc.tensor.matmul_mx(
@@ -160,11 +166,11 @@ def tile_moe_mod_none_kernel(
                 stop=True,
             )
 
-        def direct(layer, c, codes_at, scale, w_codes, w_scale):
+        def direct(layer, c, codes_at, scale, w_codes, w_scale, empty=nc.scalar.copy):
             cols = PIECES[c]
             bank = direct_banks[c % len(direct_banks)][:, 0 : width(cols)]
             mx(bank, w_codes[:, 0:P], w_scale[:, 0:P], codes_at(cols), scale[:, cols])
-            nc.scalar.copy(sums_at(layer, 0, cols), bank)
+            empty(sums_at(layer, 0, cols), bank)
 
         def scatter_gated(layer, cols, lst, window):
             nc.vector.tensor_tensor(
@@ -182,11 +188,17 @@ def tile_moe_mod_none_kernel(
                 scale=gate_cols[layer][:, b : b + 1],
             )
 
-        def turn_back(layer, t, half):
+        def turn_back(layer, t, half, added=None):
             bank = turn_banks[(len(HALVES) * (t - 1) + half) % len(turn_banks)]
             for j in range(BANK_BLOCKS):
                 block = turned[layer][:, BANK_BLOCKS * half + j, t - 1, :]
-                nc.tensor.transpose(bank[:, j * P : (j + 1) * P], block, ident[:])
+                if added is None:
+                    nc.tensor.transpose(bank[:, j * P : (j + 1) * P], block, ident[:])
+                else:
+                    for term, first in ((block, True), (added[:, BANK_BLOCKS * half + j, :], False)):
+                        nc.tensor.matmul(
+                            bank[:, j * P : (j + 1) * P], term, ident[:], start=first, stop=not first, is_transpose=True
+                        )
             nc.scalar.copy(sums_at(layer, t, HALVES[half]), bank[:])
 
         def turned_planes(layer, codes_at, scale, w_codes, w_scale, by_plane):
@@ -194,82 +206,111 @@ def tile_moe_mod_none_kernel(
                 for b in range(BANK_BLOCKS * half, BANK_BLOCKS * (half + 1)):
                     product(layer, b, codes_at, scale, w_codes, w_scale, by_plane)
                 turn_back(layer, 1, half)
-            for t in range(2, PACK):
-                for half in range(len(HALVES)):
-                    turn_back(layer, t, half)
 
-        def round_w2(half, stage):
-            staged = stage[:].rearrange("p (j n) -> p j n", j=PACK)
-            nc.sync.dma_start(
-                staged, w2.rearrange("(p j) n -> p j n", j=PACK)[:, :, half * K // 2 : (half + 1) * K // 2]
-            )
+        def round_w2(half):
+            cols = slice(half * K // 2, (half + 1) * K // 2)
             nc.gpsimd.tensor_scalar(
-                w2_bf[:].rearrange("p (u m) j -> p m u j", u=PACK)[:, half * P // 2 : (half + 1) * P // 2, :, :],
-                staged.rearrange("p j (m u) -> p m u j", u=PACK),
-                1.0,
-                0.0,
-                MULT,
-                ADD,
+                w2_bf[:, cols, :], w2_raw[:, :, cols].rearrange("p j n -> p n j"), 1.0, 0.0, MULT, ADD
             )
+
+        def plane0_columns(codes0, scale0, codes, scale):
+            nc.gpsimd.tensor_copy(codes0[:], codes[:, 0:K:PACK])
+            nc.gpsimd.tensor_copy(scale0[:], scale[:, 0:K:PACK])
 
         turn_gate(0)
+        nc.vector.tensor_copy(x_scale[:], tok_scales[:].indirect(list1[:]))
         for c, cols in enumerate(PIECES):
-            nc.vector.tensor_copy(x_scale[:, cols], tok_scales[:].indirect(entries(list1, cols)))
             nc.vector.tensor_copy(x_codes[c][:], tok_words[:].bitcast(U32).indirect(entries(list1, cols)))
             if c == 0:
-                nc.gpsimd.tensor_copy(w1_codes0[:], w1_codes[:, 0:K:PACK])
-                nc.gpsimd.tensor_copy(w1_scale0[:], w1_scale[:, 0:K:PACK])
+                plane0_columns(w1_codes0, w1_scale0, w1_codes, w1_scale)
         for c in range(len(PIECES)):
             direct(0, c, x_codes_at, x_scale, w1_codes0, w1_scale0)
-        for cols in HALVES:
+        for cols in PIECES:
             scatter_gated(0, cols, list1, spread1[0])
         turned_planes(0, x_codes_at, x_scale, w1_codes, w1_scale, "s (m t) -> s t m")
-        w2_stages = [gates[0], sums[0][1][0]]
+        for t in range(2, PACK):
+            for half in range(len(HALVES)):
+                turn_back(0, t, half)
         for t in range(PACK):
             if t > 0:
                 nc.vector.tensor_copy(spread1[t % 2][:].indirect(list1[:]), sums[0][t][0][:])
-            if t < LAST:
-                stream_bf = relay_tile("stream_bf%d" % t, [P, T], BF16)
-                for cols in PLANE2_CUTS_LAYER1 if t == LAST - 1 else TOKEN_HALVES:
-                    nc.gpsimd.tensor_tensor(stream[t][:, cols], stream[t][:, cols], spread1[t % 2][:, cols], ADD)
+            if t < 2:
+                stream_bf = relay_tile("stream_bf%d" % t, [P, T], BF16, t * T)
+                for cols in TOKEN_HALVES:
+                    nc.gpsimd.tensor_tensor(stream[t][:, cols], before[t][:, cols], spread1[t % 2][:, cols], ADD)
                     nc.scalar.copy(stream_bf[:, cols], stream[t][:, cols])
+            if t == 2:
+                stream_bf = sbuf("stream_bf2", [P, T], BF16)
+                nc.gpsimd.tensor_tensor(stream_bf[:], before[t][:], spread1[t % 2][:], ADD)
+            if t < LAST:
                 nc.scalar.activation(r_bf[:, :, t], stream_bf[:].indirect(list2[:]), COPY)
-            if t < len(w2_stages):
-                round_w2(t, w2_stages[t])
+            if t == 0:
+                w2_bf = keep.tile([P, K, PACK], BF16, name="w2_bf", tag="before0", align_bytes=64)
+            if t < 2:
+                round_w2(t)
             if t == 0:
                 turn_gate(1)
-        nc.vector.tensor_tensor(stream[LAST][:], stream[LAST][:], spread1[LAST % 2][:], ADD)
-        w2_codes = keep.tile([P, K], U32, name="w2_codes", tag="sums0_%d_0" % LAST, align_bytes=64)
+        last_bf = relay_tile("last_bf", [P, T], BF16)
+        nc.vector.tensor_tensor(last_bf[:], before[LAST][:], spread1[LAST % 2][:], ADD)
+        w2_codes = relay_tile("w2_codes", [P, K], I32, 2 * T)
         nc.vector.quantize_mx(
             out=w2_codes[:].bitcast(FP8X4), scales=w2_scale[:], in_=w2_bf[:].rearrange("p n j -> p (n j)")
         )
+        plane0_columns(w2_codes0, w2_scale0, w2_codes, w2_scale)
 
-        r_last = [relay_tile("r_last%d" % c, [P, width(cols)], F32, 4 * cols.start) for c, cols in enumerate(PIECES)]
-        for c, cols in enumerate(QUARTERS):
-            if c < len(PIECES):
-                nc.vector.tensor_copy(r_last[c][:], stream[LAST][:].indirect(entries(list2, PIECES[c])))
-            nc.scalar.copy(r_bf[:, cols, LAST], within(PIECES, r_last, cols))
+        for c, cols in enumerate(PIECES):
+            nc.scalar.activation(r_bf[:, cols, LAST], last_bf[:].indirect(entries(list2, cols)), COPY)
+            if c == len(PIECES) - 1:
+                r_codes.append(keep.tile([P, width(cols)], U32, name="r_codes_last", tag="sums1_0_0", align_bytes=64))
+            else:
+                r_codes.append(sbuf("r_codes%d" % c, [P, width(cols)], U32))
             nc.vector.quantize_mx(
-                out=r_codes[:, cols].bitcast(FP8X4),
+                out=r_codes[c][:].bitcast(FP8X4),
                 scales=r_scale[:, cols],
                 in_=r_bf[:, cols, :].rearrange("p s j -> p (s j)"),
             )
-            for piece, piece_cols in enumerate(PIECES):
-                if piece_cols.stop == cols.stop:
-                    direct(1, piece, r_codes_at, r_scale, w2_codes, w2_scale)
-                    scatter_gated(1, piece_cols, list2, spread2[0])
-        turned_planes(1, r_codes_at, r_scale, w2_codes, w2_scale, "s (t m) -> s t m")
-        for t in range(LAST):
+            direct(1, c, r_codes_at, r_scale, w2_codes0, w2_scale0, nc.vector.tensor_copy if c == 0 else nc.scalar.copy)
+            scatter_gated(1, cols, list2, spread2[0])
+        spread2.append(keep.tile([P, T], F32, name="spread2_1", tag="r_bf", align_bytes=64))
+        nc.gpsimd.memset(spread2[1][:], 0.0)
+        turned_planes(1, r_codes_at, r_scale, w2_codes, w2_scale, "s (m t) -> s t m")
+        for half in range(len(HALVES)):
+            turn_back(1, LAST - 1, half)
+        last_turned = sbuf("last_turned", [P, T], F32)
+        r_last = sbuf("r_last", [P, T], F32)
+        for g in range(T // K):
+            bank = product_banks[g % len(product_banks)]
+            for j in range(BANK_BLOCKS):
+                cols = slice(g * K + j * P, g * K + (j + 1) * P)
+                for term, first in ((before[LAST], True), (spread1[LAST % 2], False)):
+                    nc.tensor.matmul(
+                        bank[:, j * P : (j + 1) * P], term[:, cols], ident[:], start=first, stop=not first, is_transpose=True
+                    )
+            nc.scalar.copy(last_turned[:, g * K : (g + 1) * K], bank[:])
+        for g in range(T // K):
+            bank = turn_banks[(g + 2) % len(turn_banks)]
+            for j in range(BANK_BLOCKS):
+                cols = slice(g * K + j * P, g * K + (j + 1) * P)
+                nc.tensor.transpose(bank[:, j * P : (j + 1) * P], last_turned[:, cols], ident[:])
+            nc.scalar.copy(r_last[:, g * K : (g + 1) * K], bank[:])
+        for half in range(len(HALVES)):
+            turn_back(1, LAST, half)
+        for t in range(PACK):
             if t > 0:
                 for cols in cuts[1][t]:
                     nc.vector.tensor_copy(spread2[t % 2][:].indirect(entries(list2, cols)), sums_at(1, t, cols))
-            result = relay_tile("result1", [P, T], F32) if t == 1 else stream[max(t - 1, 0)]
-            for cols in PLANE2_CUTS_LAYER2 if t == LAST - 1 else TOKEN_HALVES:
-                nc.gpsimd.tensor_tensor(result[:, cols], stream[t][:, cols], spread2[t % 2][:, cols], ADD)
-                nc.sync.dma_start(out_rows[:, t, cols], result[:, cols])
-            if t == 0:
-                for c, cols in enumerate(PIECES):
-                    nc.gpsimd.tensor_tensor(last_sum[:, cols], sums_at(1, LAST, cols), r_last[c][:], ADD)
-        nc.vector.tensor_copy(stream[LAST][:].indirect(list2[:]), last_sum[:])
-        for cols in PLANE2_CUTS_LAYER2:
-            nc.scalar.dma_start(out_rows[:, LAST, cols], stream[LAST][:, cols])
+            if t < 2:
+                result = keep.tile([P, T], F32, name="result%d" % t, tag="before%d" % t, align_bytes=64)
+                nc.gpsimd.tensor_tensor(result[:], stream[t][:], spread2[t % 2][:], ADD)
+                nc.sync.dma_start(out_rows[:, t, :], result[:])
+                if t == 0:
+                    stream.append(keep.tile([P, T], F32, name="stream2", tag="stream0", align_bytes=64))
+                cols = TOKEN_HALVES[t]
+                nc.gpsimd.tensor_tensor(stream[2][:, cols], before[2][:, cols], spread1[0][:, cols], ADD)
+            if t == 2:
+                for cols in PLANE2_CUTS_LAYER2:
+                    nc.gpsimd.tensor_tensor(stream[t][:, cols], stream[t][:, cols], spread2[t % 2][:, cols], ADD)
+                    nc.sync.dma_start(out_rows[:, t, cols], stream[t][:, cols])
+        for cols in token_cuts(0, 640, 1280, 1792, T):
+            nc.vector.tensor_tensor(r_last[:, cols], r_last[:, cols], spread2[LAST % 2][:, cols], ADD)
+            nc.scalar.dma_start(out_rows[:, LAST, cols], r_last[:, cols])

@@ -35,6 +35,10 @@ def token_cuts(*bounds):
     return [slice(a, b) for a, b in zip(bounds, bounds[1:])]
 
 
+VECTOR_CUTS = token_cuts(0, 512, 1024, 1536)
+GPSIMD_CUT = slice(1536, T)
+W2_CUTS = token_cuts(0, 176, 352, K)
+BANK_CUTS = token_cuts(0, 512, 1024, 1536, T)
 TOKEN_HALVES = token_cuts(0, T // 2, T)
 PLANE2_CUTS_LAYER1 = token_cuts(0, 1024, 1792, T)
 PLANE2_CUTS_LAYER2 = token_cuts(0, 1024, 1536, T)
@@ -88,11 +92,12 @@ def tile_moe_mod_none_kernel(
         spread2 = [sbuf("spread2_0", [P, T], F32)]
         x_codes = [sbuf("x_codes%d" % c, [P, width(cols)], U32) for c, cols in enumerate(PIECES)]
         x_scale = sbuf("x_scale", [P, S], U8)
+        staged = sbuf("staged", [P, T], F32)
         r_bf = sbuf("r_bf", [P, S, PACK], BF16)
         r_codes = []
         r_scale = sbuf("r_scale", [P, S], U8)
         turned = [relay_tile("turned0", [P, BLOCKS, LAST, P], F32), sbuf("turned1", [P, BLOCKS, LAST, P], F32)]
-        cuts = [[PIECES, WHOLE, WHOLE, WHOLE], [PIECES, HALVES, WHOLE, WHOLE]]
+        cuts = [[PIECES, HALVES, WHOLE, WHOLE], [PIECES, HALVES, WHOLE, WHOLE]]
         sums = [
             [
                 [sbuf("sums%d_%d_%d" % (layer, t, c), [P, width(cols)], F32) for c, cols in enumerate(cuts[layer][t])]
@@ -141,7 +146,7 @@ def tile_moe_mod_none_kernel(
         load_gate_rows(1, gate2)
         nc.sync.dma_start(before[0][:], xr_rows[:, 0, :])
         nc.sync.dma_start(w2_raw[:], w2.rearrange("(p j) n -> p j n", j=PACK))
-        for t in range(1, PACK):
+        for t in (1, LAST, 2):
             nc.sync.dma_start(before[t][:, 0:T], xr_rows[:, t, :])
         nc.sync.dma_start(gates[1][:], gate2)
 
@@ -188,27 +193,35 @@ def tile_moe_mod_none_kernel(
                 scale=gate_cols[layer][:, b : b + 1],
             )
 
-        def turn_back(layer, t, half, added=None):
+        def turn_back(layer, t, half):
             bank = turn_banks[(len(HALVES) * (t - 1) + half) % len(turn_banks)]
             for j in range(BANK_BLOCKS):
                 block = turned[layer][:, BANK_BLOCKS * half + j, t - 1, :]
-                if added is None:
-                    nc.tensor.transpose(bank[:, j * P : (j + 1) * P], block, ident[:])
-                else:
-                    for term, first in ((block, True), (added[:, BANK_BLOCKS * half + j, :], False)):
-                        nc.tensor.matmul(
-                            bank[:, j * P : (j + 1) * P], term, ident[:], start=first, stop=not first, is_transpose=True
-                        )
+                nc.tensor.transpose(bank[:, j * P : (j + 1) * P], block, ident[:])
             nc.scalar.copy(sums_at(layer, t, HALVES[half]), bank[:])
 
-        def turned_planes(layer, codes_at, scale, w_codes, w_scale, by_plane):
-            for half in range(len(HALVES)):
-                for b in range(BANK_BLOCKS * half, BANK_BLOCKS * (half + 1)):
-                    product(layer, b, codes_at, scale, w_codes, w_scale, by_plane)
-                turn_back(layer, 1, half)
+        def products(layer, half, codes_at, scale, w_codes, w_scale):
+            for b in range(BANK_BLOCKS * half, BANK_BLOCKS * (half + 1)):
+                product(layer, b, codes_at, scale, w_codes, w_scale, "s (m t) -> s t m")
 
-        def round_w2(half):
-            cols = slice(half * K // 2, (half + 1) * K // 2)
+        def turn_sum(terms, cols, bank, staged):
+            for c in range(cols.start, cols.stop, P):
+                for i, term in enumerate(terms):
+                    nc.tensor.matmul(
+                        bank[:, c - cols.start : c - cols.start + P],
+                        term[:, c : c + P],
+                        ident[:],
+                        start=i == 0,
+                        stop=i == len(terms) - 1,
+                        is_transpose=True,
+                    )
+            nc.scalar.copy(staged[:, cols], bank[:, 0 : width(cols)])
+
+        def turn_again(staged, cols, bank):
+            for c in range(cols.start, cols.stop, P):
+                nc.tensor.transpose(bank[:, c - cols.start : c - cols.start + P], staged[:, c : c + P], ident[:])
+
+        def round_w2(cols):
             nc.gpsimd.tensor_scalar(
                 w2_bf[:, cols, :], w2_raw[:, :, cols].rearrange("p j n -> p n j"), 1.0, 0.0, MULT, ADD
             )
@@ -223,17 +236,21 @@ def tile_moe_mod_none_kernel(
             nc.vector.tensor_copy(x_codes[c][:], tok_words[:].bitcast(U32).indirect(entries(list1, cols)))
             if c == 0:
                 plane0_columns(w1_codes0, w1_scale0, w1_codes, w1_scale)
-        for c in range(len(PIECES)):
+        for c, cols in enumerate(PIECES):
+            if c == len(PIECES) - 1:
+                products(0, 0, x_codes_at, x_scale, w1_codes, w1_scale)
             direct(0, c, x_codes_at, x_scale, w1_codes0, w1_scale0)
-        for cols in PIECES:
             scatter_gated(0, cols, list1, spread1[0])
-        turned_planes(0, x_codes_at, x_scale, w1_codes, w1_scale, "s (m t) -> s t m")
+        turn_back(0, 1, 0)
+        products(0, 1, x_codes_at, x_scale, w1_codes, w1_scale)
+        turn_back(0, 1, 1)
         for t in range(2, PACK):
             for half in range(len(HALVES)):
                 turn_back(0, t, half)
         for t in range(PACK):
             if t > 0:
-                nc.vector.tensor_copy(spread1[t % 2][:].indirect(list1[:]), sums[0][t][0][:])
+                for cols in cuts[0][t]:
+                    nc.vector.tensor_copy(spread1[t % 2][:].indirect(entries(list1, cols)), sums_at(0, t, cols))
             if t < 2:
                 stream_bf = relay_tile("stream_bf%d" % t, [P, T], BF16, t * T)
                 for cols in TOKEN_HALVES:
@@ -246,12 +263,20 @@ def tile_moe_mod_none_kernel(
                 nc.scalar.activation(r_bf[:, :, t], stream_bf[:].indirect(list2[:]), COPY)
             if t == 0:
                 w2_bf = keep.tile([P, K, PACK], BF16, name="w2_bf", tag="before0", align_bytes=64)
-            if t < 2:
-                round_w2(t)
+            if t < LAST:
+                round_w2(W2_CUTS[t])
             if t == 0:
                 turn_gate(1)
+                for cols, bank in zip(VECTOR_CUTS, turn_banks):
+                    turn_sum([before[LAST]], cols, bank, staged)
+                for cols, bank in zip(VECTOR_CUTS, product_banks):
+                    turn_again(staged, cols, bank)
         last_bf = relay_tile("last_bf", [P, T], BF16)
-        nc.vector.tensor_tensor(last_bf[:], before[LAST][:], spread1[LAST % 2][:], ADD)
+        for cols, bank in zip(VECTOR_CUTS, product_banks):
+            nc.vector.tensor_tensor(last_bf[:, cols], bank[:, 0 : width(cols)], spread1[LAST % 2][:, cols], ADD)
+        nc.gpsimd.tensor_tensor(
+            last_bf[:, GPSIMD_CUT], before[LAST][:, GPSIMD_CUT], spread1[LAST % 2][:, GPSIMD_CUT], ADD
+        )
         w2_codes = relay_tile("w2_codes", [P, K], I32, 2 * T)
         nc.vector.quantize_mx(
             out=w2_codes[:].bitcast(FP8X4), scales=w2_scale[:], in_=w2_bf[:].rearrange("p n j -> p (n j)")
@@ -269,48 +294,55 @@ def tile_moe_mod_none_kernel(
                 scales=r_scale[:, cols],
                 in_=r_bf[:, cols, :].rearrange("p s j -> p (s j)"),
             )
+            if c == len(PIECES) - 1:
+                products(1, 0, r_codes_at, r_scale, w2_codes, w2_scale)
             direct(1, c, r_codes_at, r_scale, w2_codes0, w2_scale0, nc.vector.tensor_copy if c == 0 else nc.scalar.copy)
             scatter_gated(1, cols, list2, spread2[0])
         spread2.append(keep.tile([P, T], F32, name="spread2_1", tag="r_bf", align_bytes=64))
         nc.gpsimd.memset(spread2[1][:], 0.0)
-        turned_planes(1, r_codes_at, r_scale, w2_codes, w2_scale, "s (m t) -> s t m")
+        turn_back(1, 1, 0)
+        products(1, 1, r_codes_at, r_scale, w2_codes, w2_scale)
+        turn_back(1, 1, 1)
         for half in range(len(HALVES)):
-            turn_back(1, LAST - 1, half)
-        last_turned = sbuf("last_turned", [P, T], F32)
-        r_last = sbuf("r_last", [P, T], F32)
-        for g in range(T // K):
-            bank = product_banks[g % len(product_banks)]
-            for j in range(BANK_BLOCKS):
-                cols = slice(g * K + j * P, g * K + (j + 1) * P)
-                for term, first in ((before[LAST], True), (spread1[LAST % 2], False)):
-                    nc.tensor.matmul(
-                        bank[:, j * P : (j + 1) * P], term[:, cols], ident[:], start=first, stop=not first, is_transpose=True
-                    )
-            nc.scalar.copy(last_turned[:, g * K : (g + 1) * K], bank[:])
-        for g in range(T // K):
-            bank = turn_banks[(g + 2) % len(turn_banks)]
-            for j in range(BANK_BLOCKS):
-                cols = slice(g * K + j * P, g * K + (j + 1) * P)
-                nc.tensor.transpose(bank[:, j * P : (j + 1) * P], last_turned[:, cols], ident[:])
-            nc.scalar.copy(r_last[:, g * K : (g + 1) * K], bank[:])
+            turn_back(1, 2, half)
+        stream.append(sbuf("stream2", [P, T], F32))
+        for g, cols in enumerate(BANK_CUTS):
+            turn_sum([before[2], spread1[0]], cols, product_banks[g % 3], staged)
+        for g, cols in enumerate(BANK_CUTS):
+            turn_again(staged, cols, turn_banks[g % 3])
+            nc.scalar.copy(stream[2][:, cols], turn_banks[g % 3][:])
+        staged_last = sbuf("staged_last", [P, T], F32)
+        r_last = sbuf("r_last", [P, width(GPSIMD_CUT)], F32)
+        for g, cols in enumerate(BANK_CUTS):
+            turn_sum([before[LAST], spread1[1]], cols, direct_banks[g % 2], staged_last)
+        for cols, bank in zip(VECTOR_CUTS, product_banks):
+            turn_again(staged_last, cols, bank)
+        for cols, bank in zip(token_cuts(GPSIMD_CUT.start, T - 2 * P, T), turn_banks[1:]):
+            turn_again(staged_last, cols, bank)
+            nc.scalar.copy(
+                r_last[:, cols.start - GPSIMD_CUT.start : cols.stop - GPSIMD_CUT.start], bank[:, 0 : width(cols)]
+            )
         for half in range(len(HALVES)):
             turn_back(1, LAST, half)
         for t in range(PACK):
             if t > 0:
                 for cols in cuts[1][t]:
                     nc.vector.tensor_copy(spread2[t % 2][:].indirect(entries(list2, cols)), sums_at(1, t, cols))
-            if t < 2:
-                result = keep.tile([P, T], F32, name="result%d" % t, tag="before%d" % t, align_bytes=64)
-                nc.gpsimd.tensor_tensor(result[:], stream[t][:], spread2[t % 2][:], ADD)
-                nc.sync.dma_start(out_rows[:, t, :], result[:])
-                if t == 0:
-                    stream.append(keep.tile([P, T], F32, name="stream2", tag="stream0", align_bytes=64))
-                cols = TOKEN_HALVES[t]
-                nc.gpsimd.tensor_tensor(stream[2][:, cols], before[2][:, cols], spread1[0][:, cols], ADD)
-            if t == 2:
-                for cols in PLANE2_CUTS_LAYER2:
+            if t < LAST:
+                for cols in PLANE2_CUTS_LAYER2 if t == 2 else [slice(0, T)]:
                     nc.gpsimd.tensor_tensor(stream[t][:, cols], stream[t][:, cols], spread2[t % 2][:, cols], ADD)
                     nc.sync.dma_start(out_rows[:, t, cols], stream[t][:, cols])
-        for cols in token_cuts(0, 640, 1280, 1792, T):
-            nc.vector.tensor_tensor(r_last[:, cols], r_last[:, cols], spread2[LAST % 2][:, cols], ADD)
-            nc.scalar.dma_start(out_rows[:, LAST, cols], r_last[:, cols])
+        result = sbuf("result", [P, GPSIMD_CUT.start], F32)
+        for cols in token_cuts(0, 256, 512, 1024, GPSIMD_CUT.start):
+            g = cols.start // K
+            nc.vector.tensor_tensor(
+                result[:, cols],
+                product_banks[g][:, cols.start - g * K : cols.stop - g * K],
+                spread2[LAST % 2][:, cols],
+                ADD,
+            )
+            nc.scalar.dma_start(out_rows[:, LAST, cols], result[:, cols])
+        for cols in token_cuts(GPSIMD_CUT.start, T - 2 * P, T):
+            part = r_last[:, cols.start - GPSIMD_CUT.start : cols.stop - GPSIMD_CUT.start]
+            nc.gpsimd.tensor_tensor(part, part, spread2[LAST % 2][:, cols], ADD)
+            nc.sync.dma_start(out_rows[:, LAST, cols], part)

@@ -29,6 +29,7 @@ QUARTERS = [slice(c * S // 4, (c + 1) * S // 4) for c in range(4)]
 HALVES = [slice(0, S // 2), slice(S // 2, S)]
 WHOLE = [slice(0, S)]
 PIECES = [QUARTERS[0], QUARTERS[1], HALVES[1]]
+HEAD_REST = [slice(0, 3 * P), slice(3 * P, S)]
 
 
 def token_cuts(*bounds):
@@ -90,14 +91,14 @@ def tile_moe_mod_none_kernel(
 
         spread1 = [sbuf("spread1_%d" % i, [P, T], F32) for i in range(2)]
         spread2 = [sbuf("spread2_0", [P, T], F32)]
-        x_codes = [sbuf("x_codes%d" % c, [P, width(cols)], U32) for c, cols in enumerate(PIECES)]
+        x_codes = [sbuf("x_codes%d" % c, [P, width(cols)], U32) for c, cols in enumerate(HEAD_REST)]
         x_scale = sbuf("x_scale", [P, S], U8)
         staged = sbuf("staged", [P, T], F32)
         r_bf = sbuf("r_bf", [P, S, PACK], BF16)
         r_codes = []
         r_scale = sbuf("r_scale", [P, S], U8)
         turned = [relay_tile("turned0", [P, BLOCKS, LAST, P], F32), sbuf("turned1", [P, BLOCKS, LAST, P], F32)]
-        cuts = [[PIECES, HALVES, WHOLE, WHOLE], [PIECES, HALVES, WHOLE, WHOLE]]
+        cuts = [[HEAD_REST, HALVES, WHOLE, WHOLE], [PIECES, HALVES, WHOLE, WHOLE]]
         sums = [
             [
                 [sbuf("sums%d_%d_%d" % (layer, t, c), [P, width(cols)], F32) for c, cols in enumerate(cuts[layer][t])]
@@ -120,14 +121,13 @@ def tile_moe_mod_none_kernel(
         nc.gpsimd.memset(w2_scale[:].bitcast(I32), 0)
         nc.gpsimd.memset(spread1[0][:], 0.0)
         nc.vector.memset(spread2[0][:], 0.0)
-        nc.scalar.copy(spread1[1][:], spread2[0][:])
 
         xr_rows = xr.rearrange("(p t) n -> p t n", t=PACK)
         out_rows = out.rearrange("(p t) n -> p t n", t=PACK)
 
-        def load_scales(tile, scales):
+        def load_scales(queue, tile, scales):
             for q in range(QUADRANTS):
-                nc.sync.dma_start(
+                queue.dma_start(
                     tile[32 * q : 32 * q + 4, :].bitcast(I32), scales[0, 4 * q : 4 * q + 4, :].bitcast(I32)
                 )
 
@@ -135,18 +135,20 @@ def tile_moe_mod_none_kernel(
             nc.sync.dma_start(gate_rows[layer][:], gate.rearrange("p (b s) -> (p b) s", s=P)[0:P, :])
 
         nc.sync.dma_start(list1[:], offs)
-        nc.sync.dma_start(list2[:], offs2)
-        load_gate_rows(0, gate1)
-        load_scales(tok_scales, x_scales)
-        nc.sync.dma_start(tok_words[:], x_words[0].rearrange("p t d -> p (t d)").bitcast(I32))
         nc.sync.dma_start(w1_codes[:], w1_words[0].rearrange("p i d -> p (i d)").bitcast(I32))
-        load_scales(w1_scale, w1_scales)
-        for cols in (PIECES[0], slice(PIECES[0].stop, S)):
+        load_scales(nc.sync, tok_scales, x_scales)
+        load_gate_rows(0, gate1)
+        nc.sync.dma_start(tok_words[:], x_words[0].rearrange("p t d -> p (t d)").bitcast(I32))
+        load_scales(nc.sync, w1_scale, w1_scales)
+        nc.scalar.copy(spread1[1][:], spread2[0][:])
+        nc.sync.dma_start(list2[:], offs2)
+        for cols in HEAD_REST:
             nc.sync.dma_start(gates[0][:, cols], gate1[:, cols])
         load_gate_rows(1, gate2)
-        nc.sync.dma_start(before[0][:], xr_rows[:, 0, :])
+        for t in (0, LAST):
+            nc.sync.dma_start(before[t][:], xr_rows[:, t, :])
         nc.sync.dma_start(w2_raw[:], w2.rearrange("(p j) n -> p j n", j=PACK))
-        for t in (1, LAST, 2):
+        for t in (1, 2):
             nc.sync.dma_start(before[t][:, 0:T], xr_rows[:, t, :])
         nc.sync.dma_start(gates[1][:], gate2)
 
@@ -155,7 +157,7 @@ def tile_moe_mod_none_kernel(
             nc.scalar.activation(gate_cols[layer][:], turn_banks[-1][:, 0:BLOCKS], COPY)
 
         def x_codes_at(cols):
-            return within(PIECES, x_codes, cols)
+            return within(HEAD_REST, x_codes, cols)
 
         def r_codes_at(cols):
             return within(PIECES, r_codes, cols)
@@ -171,11 +173,12 @@ def tile_moe_mod_none_kernel(
                 stop=True,
             )
 
-        def direct(layer, c, codes_at, scale, w_codes, w_scale, empty=nc.scalar.copy):
-            cols = PIECES[c]
-            bank = direct_banks[c % len(direct_banks)][:, 0 : width(cols)]
-            mx(bank, w_codes[:, 0:P], w_scale[:, 0:P], codes_at(cols), scale[:, cols])
-            empty(sums_at(layer, 0, cols), bank)
+        def direct(layer, bank, passes, codes_at, scale, w_codes, w_scale, empty=nc.scalar.copy):
+            cols = slice(passes[0].start, passes[-1].stop)
+            for run in passes:
+                part = bank[:, run.start - cols.start : run.stop - cols.start]
+                mx(part, w_codes[:], w_scale[:], codes_at(run), scale[:, run])
+            empty(sums_at(layer, 0, cols), bank[:, 0 : width(cols)])
 
         def scatter_gated(layer, cols, lst, window):
             nc.vector.tensor_tensor(
@@ -226,27 +229,35 @@ def tile_moe_mod_none_kernel(
                 w2_bf[:, cols, :], w2_raw[:, :, cols].rearrange("p j n -> p n j"), 1.0, 0.0, MULT, ADD
             )
 
-        def plane0_columns(codes0, scale0, codes, scale):
-            nc.gpsimd.tensor_copy(codes0[:], codes[:, 0:K:PACK])
-            nc.gpsimd.tensor_copy(scale0[:], scale[:, 0:K:PACK])
+        def plane0_columns(engine, codes0, scale0, codes, scale):
+            engine.tensor_copy(codes0[:], codes[:, 0:K:PACK])
+            engine.tensor_copy(scale0[:], scale[:, 0:K:PACK])
 
         turn_gate(0)
         nc.vector.tensor_copy(x_scale[:], tok_scales[:].indirect(list1[:]))
-        for c, cols in enumerate(PIECES):
+        for c, cols in enumerate(HEAD_REST):
             nc.vector.tensor_copy(x_codes[c][:], tok_words[:].bitcast(U32).indirect(entries(list1, cols)))
             if c == 0:
-                plane0_columns(w1_codes0, w1_scale0, w1_codes, w1_scale)
-        for c, cols in enumerate(PIECES):
-            if c == len(PIECES) - 1:
-                products(0, 0, x_codes_at, x_scale, w1_codes, w1_scale)
-            direct(0, c, x_codes_at, x_scale, w1_codes0, w1_scale0)
-            scatter_gated(0, cols, list1, spread1[0])
+                plane0_columns(nc.gpsimd, w1_codes0, w1_scale0, w1_codes, w1_scale)
+        direct(0, product_banks[0], token_cuts(0, 2 * P, 3 * P), x_codes_at, x_scale, w1_codes0, w1_scale0)
+        scatter_gated(0, HEAD_REST[0], list1, spread1[0])
+        for b in range(1):
+            product(0, b, x_codes_at, x_scale, w1_codes, w1_scale, "s (m t) -> s t m")
+        for c, run in enumerate(token_cuts(3 * P, 7 * P, S)):
+            direct(0, product_banks[c + 1], [run], x_codes_at, x_scale, w1_codes0, w1_scale0)
+        scatter_gated(0, HEAD_REST[1], list1, spread1[0])
+        for b in range(1, BANK_BLOCKS):
+            product(0, b, x_codes_at, x_scale, w1_codes, w1_scale, "s (m t) -> s t m")
         turn_back(0, 1, 0)
         products(0, 1, x_codes_at, x_scale, w1_codes, w1_scale)
         turn_back(0, 1, 1)
         for t in range(2, PACK):
             for half in range(len(HALVES)):
                 turn_back(0, t, half)
+        for cols, bank in zip(VECTOR_CUTS, turn_banks):
+            turn_sum([before[LAST]], cols, bank, staged)
+        for cols, bank in zip(VECTOR_CUTS, product_banks):
+            turn_again(staged, cols, bank)
         for t in range(PACK):
             if t > 0:
                 for cols in cuts[0][t]:
@@ -267,10 +278,6 @@ def tile_moe_mod_none_kernel(
                 round_w2(W2_CUTS[t])
             if t == 0:
                 turn_gate(1)
-                for cols, bank in zip(VECTOR_CUTS, turn_banks):
-                    turn_sum([before[LAST]], cols, bank, staged)
-                for cols, bank in zip(VECTOR_CUTS, product_banks):
-                    turn_again(staged, cols, bank)
         last_bf = relay_tile("last_bf", [P, T], BF16)
         for cols, bank in zip(VECTOR_CUTS, product_banks):
             nc.vector.tensor_tensor(last_bf[:, cols], bank[:, 0 : width(cols)], spread1[LAST % 2][:, cols], ADD)
@@ -281,7 +288,7 @@ def tile_moe_mod_none_kernel(
         nc.vector.quantize_mx(
             out=w2_codes[:].bitcast(FP8X4), scales=w2_scale[:], in_=w2_bf[:].rearrange("p n j -> p (n j)")
         )
-        plane0_columns(w2_codes0, w2_scale0, w2_codes, w2_scale)
+        plane0_columns(nc.vector, w2_codes0, w2_scale0, w2_codes, w2_scale)
 
         for c, cols in enumerate(PIECES):
             nc.scalar.activation(r_bf[:, cols, LAST], last_bf[:].indirect(entries(list2, cols)), COPY)
@@ -296,7 +303,7 @@ def tile_moe_mod_none_kernel(
             )
             if c == len(PIECES) - 1:
                 products(1, 0, r_codes_at, r_scale, w2_codes, w2_scale)
-            direct(1, c, r_codes_at, r_scale, w2_codes0, w2_scale0, nc.vector.tensor_copy if c == 0 else nc.scalar.copy)
+            direct(1, direct_banks[c % 2], [cols], r_codes_at, r_scale, w2_codes0, w2_scale0, nc.vector.tensor_copy if c == 0 else nc.scalar.copy)
             scatter_gated(1, cols, list2, spread2[0])
         spread2.append(keep.tile([P, T], F32, name="spread2_1", tag="r_bf", align_bytes=64))
         nc.gpsimd.memset(spread2[1][:], 0.0)

@@ -90,7 +90,7 @@ def tile_moe_mod_none_kernel(
         stream = [sbuf("stream%d" % t, [P, T], F32) for t in range(2)]
 
         spread1 = [sbuf("spread1_%d" % i, [P, T], F32) for i in range(2)]
-        spread2 = [sbuf("spread2_0", [P, T], F32)]
+        spread2 = [sbuf("spread2_%d" % i, [P, T], F32) for i in range(2)]
         x_codes = [sbuf("x_codes%d" % c, [P, width(cols)], U32) for c, cols in enumerate(HEAD_REST)]
         x_scale = sbuf("x_scale", [P, S], U8)
         staged = sbuf("staged", [P, T], F32)
@@ -118,9 +118,9 @@ def tile_moe_mod_none_kernel(
         nc.vector.memset(tok_scales[:].bitcast(I32), 0)
         nc.vector.memset(w1_scale[:].bitcast(I32), 0)
         make_identity(nc, ident[:])
-        nc.gpsimd.memset(w2_scale[:].bitcast(I32), 0)
-        nc.gpsimd.memset(spread1[0][:], 0.0)
-        nc.vector.memset(spread2[0][:], 0.0)
+        nc.vector.memset(spread1[0][:], 0.0)
+        nc.vector.memset(w2_scale[:].bitcast(I32), 0)
+        nc.gpsimd.tensor_scalar(spread2[1][:], spread1[0][:], 1.0, 0.0, MULT, ADD)
 
         xr_rows = xr.rearrange("(p t) n -> p t n", t=PACK)
         out_rows = out.rearrange("(p t) n -> p t n", t=PACK)
@@ -140,7 +140,8 @@ def tile_moe_mod_none_kernel(
         load_gate_rows(0, gate1)
         nc.sync.dma_start(tok_words[:], x_words[0].rearrange("p t d -> p (t d)").bitcast(I32))
         load_scales(nc.sync, w1_scale, w1_scales)
-        nc.scalar.copy(spread1[1][:], spread2[0][:])
+        for tile in (spread1[1], spread2[0]):
+            nc.scalar.copy(tile[:], spread1[0][:])
         nc.sync.dma_start(list2[:], offs2)
         for cols in HEAD_REST:
             nc.sync.dma_start(gates[0][:, cols], gate1[:, cols])
@@ -305,19 +306,16 @@ def tile_moe_mod_none_kernel(
                 products(1, 0, r_codes_at, r_scale, w2_codes, w2_scale)
             direct(1, direct_banks[c % 2], [cols], r_codes_at, r_scale, w2_codes0, w2_scale0, nc.vector.tensor_copy if c == 0 else nc.scalar.copy)
             scatter_gated(1, cols, list2, spread2[0])
-        spread2.append(keep.tile([P, T], F32, name="spread2_1", tag="r_bf", align_bytes=64))
-        nc.gpsimd.memset(spread2[1][:], 0.0)
         turn_back(1, 1, 0)
         products(1, 1, r_codes_at, r_scale, w2_codes, w2_scale)
         turn_back(1, 1, 1)
-        for half in range(len(HALVES)):
-            turn_back(1, 2, half)
-        stream.append(sbuf("stream2", [P, T], F32))
-        for g, cols in enumerate(BANK_CUTS):
-            turn_sum([before[2], spread1[0]], cols, product_banks[g % 3], staged)
-        for g, cols in enumerate(BANK_CUTS):
-            turn_again(staged, cols, turn_banks[g % 3])
-            nc.scalar.copy(stream[2][:, cols], turn_banks[g % 3][:])
+        for t in range(2, PACK):
+            for half in range(len(HALVES)):
+                turn_back(1, t, half)
+        r2_end = sbuf("r2_end", [P, width(GPSIMD_CUT)], F32)
+        turn_sum([before[2], spread1[0]], GPSIMD_CUT, product_banks[0], staged)
+        turn_again(staged, GPSIMD_CUT, turn_banks[0])
+        nc.scalar.copy(r2_end[:], turn_banks[0][:])
         staged_last = sbuf("staged_last", [P, T], F32)
         r_last = sbuf("r_last", [P, width(GPSIMD_CUT)], F32)
         for g, cols in enumerate(BANK_CUTS):
@@ -329,17 +327,24 @@ def tile_moe_mod_none_kernel(
             nc.scalar.copy(
                 r_last[:, cols.start - GPSIMD_CUT.start : cols.stop - GPSIMD_CUT.start], bank[:, 0 : width(cols)]
             )
-        for half in range(len(HALVES)):
-            turn_back(1, LAST, half)
         for t in range(PACK):
             if t > 0:
                 for cols in cuts[1][t]:
                     nc.vector.tensor_copy(spread2[t % 2][:].indirect(entries(list2, cols)), sums_at(1, t, cols))
-            if t < LAST:
-                for cols in PLANE2_CUTS_LAYER2 if t == 2 else [slice(0, T)]:
-                    nc.gpsimd.tensor_tensor(stream[t][:, cols], stream[t][:, cols], spread2[t % 2][:, cols], ADD)
-                    nc.sync.dma_start(out_rows[:, t, cols], stream[t][:, cols])
-        result = sbuf("result", [P, GPSIMD_CUT.start], F32)
+            if t < 2:
+                done = keep.tile([P, T], F32, name="done%d" % t, tag="before%d" % t, align_bytes=64)
+                nc.gpsimd.tensor_tensor(done[:], stream[t][:], spread2[t % 2][:], ADD)
+                nc.sync.dma_start(out_rows[:, t, :], done[:])
+                if t == 0:
+                    r2 = keep.tile([P, GPSIMD_CUT.start], F32, name="r2", tag="stream0", align_bytes=64)
+                cols = token_cuts(0, GPSIMD_CUT.start // 2, GPSIMD_CUT.start)[t]
+                nc.gpsimd.tensor_tensor(r2[:, cols], before[2][:, cols], spread1[0][:, cols], ADD)
+            if t == 2:
+                for cols in PLANE2_CUTS_LAYER2:
+                    part = r2_end[:] if cols == GPSIMD_CUT else r2[:, cols]
+                    nc.gpsimd.tensor_tensor(part, part, spread2[t % 2][:, cols], ADD)
+                    nc.sync.dma_start(out_rows[:, t, cols], part)
+        result = keep.tile([P, GPSIMD_CUT.start], F32, name="result", tag="spread2_0", align_bytes=64)
         for cols in token_cuts(0, 256, 512, 1024, GPSIMD_CUT.start):
             g = cols.start // K
             nc.vector.tensor_tensor(
@@ -348,8 +353,8 @@ def tile_moe_mod_none_kernel(
                 spread2[LAST % 2][:, cols],
                 ADD,
             )
-            nc.scalar.dma_start(out_rows[:, LAST, cols], result[:, cols])
+            nc.sync.dma_start(out_rows[:, LAST, cols], result[:, cols])
         for cols in token_cuts(GPSIMD_CUT.start, T - 2 * P, T):
             part = r_last[:, cols.start - GPSIMD_CUT.start : cols.stop - GPSIMD_CUT.start]
             nc.gpsimd.tensor_tensor(part, part, spread2[LAST % 2][:, cols], ADD)
-            nc.sync.dma_start(out_rows[:, LAST, cols], part)
+            nc.scalar.dma_start(out_rows[:, LAST, cols], part)

@@ -319,10 +319,10 @@ def tile_moe_mod_none_kernel(
         staged_last = sbuf("staged_last", [P, T], F32)
         r_last = sbuf("r_last", [P, width(GPSIMD_CUT)], F32)
         for g, cols in enumerate(BANK_CUTS):
-            turn_sum([before[LAST], spread1[1]], cols, direct_banks[g % 2], staged_last)
+            turn_sum([before[LAST], spread1[1]], cols, turn_banks[(g + 1) % 3], staged_last)
         for cols, bank in zip(VECTOR_CUTS, product_banks):
             turn_again(staged_last, cols, bank)
-        for cols, bank in zip(token_cuts(GPSIMD_CUT.start, T - 2 * P, T), turn_banks[1:]):
+        for cols, bank in zip(token_cuts(GPSIMD_CUT.start, T - 2 * P, T), direct_banks):
             turn_again(staged_last, cols, bank)
             nc.scalar.copy(
                 r_last[:, cols.start - GPSIMD_CUT.start : cols.stop - GPSIMD_CUT.start], bank[:, 0 : width(cols)]

@@ -38,7 +38,8 @@ def token_cuts(*bounds):
 
 VECTOR_CUTS = token_cuts(0, 512, 1024, 1536)
 GPSIMD_CUT = slice(1536, T)
-W2_CUTS = token_cuts(0, 176, 352, K)
+W2_CUTS = token_cuts(0, 112, 224, 320)
+W2_SCALAR_CUT = slice(320, K)
 BANK_CUTS = token_cuts(0, 512, 1024, 1536, T)
 TOKEN_HALVES = token_cuts(0, T // 2, T)
 PLANE2_CUTS_LAYER1 = token_cuts(0, 1024, 1792, T)
@@ -279,6 +280,8 @@ def tile_moe_mod_none_kernel(
                 round_w2(W2_CUTS[t])
             if t == 0:
                 turn_gate(1)
+            if t == 1:
+                nc.scalar.copy(w2_bf[:, W2_SCALAR_CUT, :], w2_raw[:, :, W2_SCALAR_CUT].rearrange("p j n -> p n j"))
         last_bf = relay_tile("last_bf", [P, T], BF16)
         for cols, bank in zip(VECTOR_CUTS, product_banks):
             nc.vector.tensor_tensor(last_bf[:, cols], bank[:, 0 : width(cols)], spread1[LAST % 2][:, cols], ADD)

@@ -23,6 +23,7 @@ LAST = PACK - 1
 GROUP = 16
 QUADRANTS = 4
 BLOCKS = S // P
+PLANE2_BYTES = BLOCKS * LAST * P * 4
 BANK_BLOCKS = 4
 
 QUARTERS = [slice(c * S // 4, (c + 1) * S // 4) for c in range(4)]
@@ -38,8 +39,10 @@ def token_cuts(*bounds):
 
 VECTOR_CUTS = token_cuts(0, 512, 1024, 1536)
 GPSIMD_CUT = slice(1536, T)
-W2_CUTS = token_cuts(0, 112, 224, 320)
-W2_SCALAR_CUT = slice(320, K)
+MIDDLE_CUTS = token_cuts(0, 512, 1024, 1408)
+MIDDLE_REST = slice(1408, T)
+W2_CUTS = token_cuts(0, 192, 384)
+W2_SCALAR_CUT = slice(384, K)
 BANK_CUTS = token_cuts(0, 512, 1024, 1536, T)
 TOKEN_HALVES = token_cuts(0, T // 2, T)
 PLANE2_CUTS_LAYER1 = token_cuts(0, 1024, 1792, T)
@@ -87,11 +90,18 @@ def tile_moe_mod_none_kernel(
         w2_scale = sbuf("w2_scale", [P, K], U8)
         w2_codes0 = sbuf("w2_codes0", [P, P], I32)
         w2_scale0 = sbuf("w2_scale0", [P, P], U8)
-        before = [sbuf("before%d" % t, [P, T], F32) for t in range(PACK)]
+        before = [
+            relay_tile("before2", [P, T], F32, PLANE2_BYTES) if t == 2 else sbuf("before%d" % t, [P, T], F32)
+            for t in range(PACK)
+        ]
+        again2 = sbuf("again2", [P, T], F32)
         stream = [sbuf("stream%d" % t, [P, T], F32) for t in range(2)]
 
         spread1 = [sbuf("spread1_%d" % i, [P, T], F32) for i in range(2)]
-        spread2 = [sbuf("spread2_%d" % i, [P, T], F32) for i in range(2)]
+        spread2 = [
+            keep.tile([P, T], F32, name="spread2_0", tag="tok_words", align_bytes=64),
+            sbuf("spread2_1", [P, T], F32),
+        ]
         x_codes = [sbuf("x_codes%d" % c, [P, width(cols)], U32) for c, cols in enumerate(HEAD_REST)]
         x_scale = sbuf("x_scale", [P, S], U8)
         staged = sbuf("staged", [P, T], F32)
@@ -99,7 +109,7 @@ def tile_moe_mod_none_kernel(
         r_codes = []
         r_scale = sbuf("r_scale", [P, S], U8)
         turned = [relay_tile("turned0", [P, BLOCKS, LAST, P], F32), sbuf("turned1", [P, BLOCKS, LAST, P], F32)]
-        cuts = [[HEAD_REST, HALVES, WHOLE, WHOLE], [PIECES, HALVES, WHOLE, WHOLE]]
+        cuts = [[HEAD_REST, HALVES, WHOLE, WHOLE], [PIECES, WHOLE, WHOLE, WHOLE]]
         sums = [
             [
                 [sbuf("sums%d_%d_%d" % (layer, t, c), [P, width(cols)], F32) for c, cols in enumerate(cuts[layer][t])]
@@ -116,18 +126,18 @@ def tile_moe_mod_none_kernel(
         product_banks = [psum.tile([P, K], F32, name="product%d" % i) for i in range(3)]
         turn_banks = [psum.tile([P, K], F32, name="turn%d" % i) for i in range(3)]
 
-        nc.vector.memset(tok_scales[:].bitcast(I32), 0)
+        nc.gpsimd.memset(tok_scales[:].bitcast(I32), 0)
         nc.vector.memset(w1_scale[:].bitcast(I32), 0)
         make_identity(nc, ident[:])
         nc.vector.memset(spread1[0][:], 0.0)
-        nc.vector.memset(w2_scale[:].bitcast(I32), 0)
+        nc.gpsimd.memset(w2_scale[:].bitcast(I32), 0)
         nc.gpsimd.tensor_scalar(spread2[1][:], spread1[0][:], 1.0, 0.0, MULT, ADD)
 
         xr_rows = xr.rearrange("(p t) n -> p t n", t=PACK)
         out_rows = out.rearrange("(p t) n -> p t n", t=PACK)
 
-        def load_scales(queue, tile, scales):
-            for q in range(QUADRANTS):
+        def load_scales(queue, tile, scales, quadrants):
+            for q in quadrants:
                 queue.dma_start(
                     tile[32 * q : 32 * q + 4, :].bitcast(I32), scales[0, 4 * q : 4 * q + 4, :].bitcast(I32)
                 )
@@ -136,16 +146,16 @@ def tile_moe_mod_none_kernel(
             nc.sync.dma_start(gate_rows[layer][:], gate.rearrange("p (b s) -> (p b) s", s=P)[0:P, :])
 
         nc.sync.dma_start(list1[:], offs)
-        nc.sync.dma_start(w1_codes[:], w1_words[0].rearrange("p i d -> p (i d)").bitcast(I32))
-        load_scales(nc.sync, tok_scales, x_scales)
         load_gate_rows(0, gate1)
+        load_scales(nc.sync, tok_scales, x_scales, (0, 1, 2))
+        load_scales(nc.scalar, tok_scales, x_scales, (3,))
         nc.sync.dma_start(tok_words[:], x_words[0].rearrange("p t d -> p (t d)").bitcast(I32))
-        load_scales(nc.sync, w1_scale, w1_scales)
-        for tile in (spread1[1], spread2[0]):
-            nc.scalar.copy(tile[:], spread1[0][:])
-        nc.sync.dma_start(list2[:], offs2)
+        load_scales(nc.sync, w1_scale, w1_scales, range(QUADRANTS))
+        nc.sync.dma_start(w1_codes[:], w1_words[0].rearrange("p i d -> p (i d)").bitcast(I32))
+        nc.scalar.copy(spread1[1][:], spread1[0][:])
         for cols in HEAD_REST:
             nc.sync.dma_start(gates[0][:, cols], gate1[:, cols])
+        nc.sync.dma_start(list2[:], offs2)
         load_gate_rows(1, gate2)
         for t in (0, LAST):
             nc.sync.dma_start(before[t][:], xr_rows[:, t, :])
@@ -153,6 +163,7 @@ def tile_moe_mod_none_kernel(
         for t in (1, 2):
             nc.sync.dma_start(before[t][:, 0:T], xr_rows[:, t, :])
         nc.sync.dma_start(gates[1][:], gate2)
+        nc.sync.dma_start(again2[:], xr_rows[:, 2, :])
 
         def turn_gate(layer):
             nc.tensor.transpose(turn_banks[-1][:, 0:P], gate_rows[layer][:], ident[:])
@@ -240,7 +251,9 @@ def tile_moe_mod_none_kernel(
         for c, cols in enumerate(HEAD_REST):
             nc.vector.tensor_copy(x_codes[c][:], tok_words[:].bitcast(U32).indirect(entries(list1, cols)))
             if c == 0:
-                plane0_columns(nc.gpsimd, w1_codes0, w1_scale0, w1_codes, w1_scale)
+                nc.gpsimd.tensor_copy(w1_scale0[:], w1_scale[:, 0:K:PACK])
+                nc.gpsimd.tensor_copy(w1_codes0[:], w1_codes[:, 0:K:PACK])
+        nc.gpsimd.memset(spread2[0][:], 0.0)
         direct(0, product_banks[0], token_cuts(0, 2 * P, 3 * P), x_codes_at, x_scale, w1_codes0, w1_scale0)
         scatter_gated(0, HEAD_REST[0], list1, spread1[0])
         for b in range(1):
@@ -256,9 +269,9 @@ def tile_moe_mod_none_kernel(
         for t in range(2, PACK):
             for half in range(len(HALVES)):
                 turn_back(0, t, half)
-        for cols, bank in zip(VECTOR_CUTS, turn_banks):
+        for cols, bank in zip(MIDDLE_CUTS, turn_banks):
             turn_sum([before[LAST]], cols, bank, staged)
-        for cols, bank in zip(VECTOR_CUTS, product_banks):
+        for cols, bank in zip(MIDDLE_CUTS, product_banks):
             turn_again(staged, cols, bank)
         for t in range(PACK):
             if t > 0:
@@ -272,23 +285,22 @@ def tile_moe_mod_none_kernel(
             if t == 2:
                 stream_bf = sbuf("stream_bf2", [P, T], BF16)
                 nc.gpsimd.tensor_tensor(stream_bf[:], before[t][:], spread1[t % 2][:], ADD)
-            if t < LAST:
-                nc.scalar.activation(r_bf[:, :, t], stream_bf[:].indirect(list2[:]), COPY)
-            if t == 0:
-                w2_bf = keep.tile([P, K, PACK], BF16, name="w2_bf", tag="before0", align_bytes=64)
-            if t < LAST:
-                round_w2(W2_CUTS[t])
             if t == 0:
                 turn_gate(1)
             if t == 1:
+                w2_bf = keep.tile([P, K, PACK], BF16, name="w2_bf", tag="before1", align_bytes=64)
                 nc.scalar.copy(w2_bf[:, W2_SCALAR_CUT, :], w2_raw[:, :, W2_SCALAR_CUT].rearrange("p j n -> p n j"))
-        last_bf = relay_tile("last_bf", [P, T], BF16)
-        for cols, bank in zip(VECTOR_CUTS, product_banks):
+            if t < LAST:
+                nc.scalar.activation(r_bf[:, :, t], stream_bf[:].indirect(list2[:]), COPY)
+            if t in (1, 2):
+                round_w2(W2_CUTS[t - 1])
+        last_bf = relay_tile("last_bf", [P, T], BF16, PLANE2_BYTES)
+        for cols, bank in zip(MIDDLE_CUTS, product_banks):
             nc.vector.tensor_tensor(last_bf[:, cols], bank[:, 0 : width(cols)], spread1[LAST % 2][:, cols], ADD)
         nc.gpsimd.tensor_tensor(
-            last_bf[:, GPSIMD_CUT], before[LAST][:, GPSIMD_CUT], spread1[LAST % 2][:, GPSIMD_CUT], ADD
+            last_bf[:, MIDDLE_REST], before[LAST][:, MIDDLE_REST], spread1[LAST % 2][:, MIDDLE_REST], ADD
         )
-        w2_codes = relay_tile("w2_codes", [P, K], I32, 2 * T)
+        w2_codes = relay_tile("w2_codes", [P, K], I32, PLANE2_BYTES + 2 * T)
         nc.vector.quantize_mx(
             out=w2_codes[:].bitcast(FP8X4), scales=w2_scale[:], in_=w2_bf[:].rearrange("p n j -> p (n j)")
         )
@@ -316,7 +328,7 @@ def tile_moe_mod_none_kernel(
             for half in range(len(HALVES)):
                 turn_back(1, t, half)
         r2_end = sbuf("r2_end", [P, width(GPSIMD_CUT)], F32)
-        turn_sum([before[2], spread1[0]], GPSIMD_CUT, product_banks[0], staged)
+        turn_sum([again2, spread1[0]], GPSIMD_CUT, product_banks[0], staged)
         turn_again(staged, GPSIMD_CUT, turn_banks[0])
         nc.scalar.copy(r2_end[:], turn_banks[0][:])
         staged_last = sbuf("staged_last", [P, T], F32)
@@ -341,13 +353,13 @@ def tile_moe_mod_none_kernel(
                 if t == 0:
                     r2 = keep.tile([P, GPSIMD_CUT.start], F32, name="r2", tag="stream0", align_bytes=64)
                 cols = token_cuts(0, GPSIMD_CUT.start // 2, GPSIMD_CUT.start)[t]
-                nc.gpsimd.tensor_tensor(r2[:, cols], before[2][:, cols], spread1[0][:, cols], ADD)
+                nc.gpsimd.tensor_tensor(r2[:, cols], again2[:, cols], spread1[0][:, cols], ADD)
             if t == 2:
                 for cols in PLANE2_CUTS_LAYER2:
                     part = r2_end[:] if cols == GPSIMD_CUT else r2[:, cols]
                     nc.gpsimd.tensor_tensor(part, part, spread2[t % 2][:, cols], ADD)
                     nc.sync.dma_start(out_rows[:, t, cols], part)
-        result = keep.tile([P, GPSIMD_CUT.start], F32, name="result", tag="spread2_0", align_bytes=64)
+        result = keep.tile([P, GPSIMD_CUT.start], F32, name="result", tag="tok_words", align_bytes=64)
         for cols in token_cuts(0, 256, 512, 1024, GPSIMD_CUT.start):
             g = cols.start // K
             nc.vector.tensor_tensor(

@@ -24,6 +24,7 @@ GROUP = 16
 QUADRANTS = 4
 BLOCKS = S // P
 PLANE2_BYTES = BLOCKS * LAST * P * 4
+PLANE1_BYTES = PLANE2_BYTES + T * 4
 BANK_BLOCKS = 4
 
 QUARTERS = [slice(c * S // 4, (c + 1) * S // 4) for c in range(4)]
@@ -37,14 +38,15 @@ def token_cuts(*bounds):
     return [slice(a, b) for a, b in zip(bounds, bounds[1:])]
 
 
+TOKEN_HALVES = token_cuts(0, T // 2, T)
 VECTOR_CUTS = token_cuts(0, 512, 1024, 1536)
 GPSIMD_CUT = slice(1536, T)
 MIDDLE_CUTS = token_cuts(0, 512, 1024, 1408)
 MIDDLE_REST = slice(1408, T)
-W2_CUTS = token_cuts(0, 192, 384)
-W2_SCALAR_CUT = slice(384, K)
+W2_CUTS = token_cuts(0, 192, 320, K)
+W2_RUNS = token_cuts(0, 128, 192, 320, 448, K)
+ADD_CUTS = [TOKEN_HALVES, token_cuts(0, 1024, 1792, T)]
 BANK_CUTS = token_cuts(0, 512, 1024, 1536, T)
-TOKEN_HALVES = token_cuts(0, T // 2, T)
 PLANE2_CUTS_LAYER1 = token_cuts(0, 1024, 1792, T)
 PLANE2_CUTS_LAYER2 = token_cuts(0, 1024, 1536, T)
 
@@ -84,14 +86,16 @@ def tile_moe_mod_none_kernel(
         w1_scale0 = sbuf("w1_scale0", [P, P], U8)
         gates = [sbuf("gate%d" % layer, [P, S], F32) for layer in range(2)]
         gate_rows = [sbuf("gate_rows%d" % layer, [P, P], F32) for layer in range(2)]
-        gate_cols = [sbuf("gate_cols%d" % layer, [P, BLOCKS], F32) for layer in range(2)]
+        gate_cols = [sbuf("gate_cols0", [P, BLOCKS], F32), relay_tile("gate_cols1", [P, BLOCKS], F32, PLANE1_BYTES)]
         ident = sbuf("ident", [P, P], F32)
         w2_raw = sbuf("w2_raw", [P, PACK, K], F32)
         w2_scale = sbuf("w2_scale", [P, K], U8)
         w2_codes0 = sbuf("w2_codes0", [P, P], I32)
         w2_scale0 = sbuf("w2_scale0", [P, P], U8)
         before = [
-            relay_tile("before2", [P, T], F32, PLANE2_BYTES) if t == 2 else sbuf("before%d" % t, [P, T], F32)
+            relay_tile("before%d" % t, [P, T], F32, (PLANE1_BYTES, PLANE2_BYTES)[t - 1])
+            if t in (1, 2)
+            else sbuf("before%d" % t, [P, T], F32)
             for t in range(PACK)
         ]
         again2 = sbuf("again2", [P, T], F32)
@@ -106,7 +110,10 @@ def tile_moe_mod_none_kernel(
         x_scale = sbuf("x_scale", [P, S], U8)
         staged = sbuf("staged", [P, T], F32)
         r_bf = sbuf("r_bf", [P, S, PACK], BF16)
+        gate_first = sbuf("gate_first", [P, width(PIECES[0])], F32)
+        first = sbuf("first", [P, width(PIECES[0])], F32)
         r_codes = []
+        w2_bf = []
         r_scale = sbuf("r_scale", [P, S], U8)
         turned = [relay_tile("turned0", [P, BLOCKS, LAST, P], F32), sbuf("turned1", [P, BLOCKS, LAST, P], F32)]
         cuts = [[HEAD_REST, HALVES, WHOLE, WHOLE], [PIECES, WHOLE, WHOLE, WHOLE]]
@@ -162,7 +169,8 @@ def tile_moe_mod_none_kernel(
         nc.sync.dma_start(w2_raw[:], w2.rearrange("(p j) n -> p j n", j=PACK))
         for t in (1, 2):
             nc.sync.dma_start(before[t][:, 0:T], xr_rows[:, t, :])
-        nc.sync.dma_start(gates[1][:], gate2)
+        nc.sync.dma_start(gate_first[:], gate2[:, PIECES[0]])
+        nc.sync.dma_start(gates[1][:, PIECES[0].stop : S], gate2[:, PIECES[0].stop : S])
         nc.sync.dma_start(again2[:], xr_rows[:, 2, :])
 
         def turn_gate(layer):
@@ -237,9 +245,9 @@ def tile_moe_mod_none_kernel(
             for c in range(cols.start, cols.stop, P):
                 nc.tensor.transpose(bank[:, c - cols.start : c - cols.start + P], staged[:, c : c + P], ident[:])
 
-        def round_w2(cols):
+        def round_w2(tile, cols):
             nc.gpsimd.tensor_scalar(
-                w2_bf[:, cols, :], w2_raw[:, :, cols].rearrange("p j n -> p n j"), 1.0, 0.0, MULT, ADD
+                tile[:], w2_raw[:, :, cols].rearrange("p j n -> p n j"), 1.0, 0.0, MULT, ADD
             )
 
         def plane0_columns(engine, codes0, scale0, codes, scale):
@@ -279,21 +287,23 @@ def tile_moe_mod_none_kernel(
                     nc.vector.tensor_copy(spread1[t % 2][:].indirect(entries(list1, cols)), sums_at(0, t, cols))
             if t < 2:
                 stream_bf = relay_tile("stream_bf%d" % t, [P, T], BF16, t * T)
-                for cols in TOKEN_HALVES:
+                for cols in ADD_CUTS[t]:
                     nc.gpsimd.tensor_tensor(stream[t][:, cols], before[t][:, cols], spread1[t % 2][:, cols], ADD)
                     nc.scalar.copy(stream_bf[:, cols], stream[t][:, cols])
             if t == 2:
                 stream_bf = sbuf("stream_bf2", [P, T], BF16)
                 nc.gpsimd.tensor_tensor(stream_bf[:], before[t][:], spread1[t % 2][:], ADD)
-            if t == 0:
-                turn_gate(1)
             if t == 1:
-                w2_bf = keep.tile([P, K, PACK], BF16, name="w2_bf", tag="before1", align_bytes=64)
-                nc.scalar.copy(w2_bf[:, W2_SCALAR_CUT, :], w2_raw[:, :, W2_SCALAR_CUT].rearrange("p j n -> p n j"))
+                turn_gate(1)
             if t < LAST:
                 nc.scalar.activation(r_bf[:, :, t], stream_bf[:].indirect(list2[:]), COPY)
-            if t in (1, 2):
-                round_w2(W2_CUTS[t - 1])
+            if t < LAST:
+                shape = [P, width(W2_CUTS[t]), PACK]
+                if t == 0:
+                    w2_bf.append(keep.tile(shape, BF16, name="w2_bf0", tag="before0", align_bytes=64))
+                else:
+                    w2_bf.append(relay_tile("w2_bf%d" % t, shape, BF16, (PLANE1_BYTES + 64, PLANE2_BYTES + 3 * T)[t - 1]))
+                round_w2(w2_bf[t], W2_CUTS[t])
         last_bf = relay_tile("last_bf", [P, T], BF16, PLANE2_BYTES)
         for cols, bank in zip(MIDDLE_CUTS, product_banks):
             nc.vector.tensor_tensor(last_bf[:, cols], bank[:, 0 : width(cols)], spread1[LAST % 2][:, cols], ADD)
@@ -301,15 +311,18 @@ def tile_moe_mod_none_kernel(
             last_bf[:, MIDDLE_REST], before[LAST][:, MIDDLE_REST], spread1[LAST % 2][:, MIDDLE_REST], ADD
         )
         w2_codes = relay_tile("w2_codes", [P, K], I32, PLANE2_BYTES + 2 * T)
-        nc.vector.quantize_mx(
-            out=w2_codes[:].bitcast(FP8X4), scales=w2_scale[:], in_=w2_bf[:].rearrange("p n j -> p (n j)")
-        )
+        for cols in W2_RUNS:
+            nc.vector.quantize_mx(
+                out=w2_codes[:, cols].bitcast(FP8X4),
+                scales=w2_scale[:, cols],
+                in_=within(W2_CUTS, w2_bf, cols).rearrange("p n j -> p (n j)"),
+            )
         plane0_columns(nc.vector, w2_codes0, w2_scale0, w2_codes, w2_scale)
 
         for c, cols in enumerate(PIECES):
             nc.scalar.activation(r_bf[:, cols, LAST], last_bf[:].indirect(entries(list2, cols)), COPY)
             if c == len(PIECES) - 1:
-                r_codes.append(keep.tile([P, width(cols)], U32, name="r_codes_last", tag="sums1_0_0", align_bytes=64))
+                r_codes.append(keep.tile([P, width(cols)], U32, name="r_codes_last", tag="gate_first", align_bytes=64))
             else:
                 r_codes.append(sbuf("r_codes%d" % c, [P, width(cols)], U32))
             nc.vector.quantize_mx(
@@ -319,7 +332,12 @@ def tile_moe_mod_none_kernel(
             )
             if c == len(PIECES) - 1:
                 products(1, 0, r_codes_at, r_scale, w2_codes, w2_scale)
-            direct(1, direct_banks[c % 2], [cols], r_codes_at, r_scale, w2_codes0, w2_scale0, nc.vector.tensor_copy if c == 0 else nc.scalar.copy)
+            if c == 0:
+                mx(direct_banks[0][:, cols], w2_codes0[:], w2_scale0[:], r_codes_at(cols), r_scale[:, cols])
+                nc.vector.tensor_tensor(first[:], direct_banks[0][:, cols], gate_first[:], MULT)
+                nc.vector.tensor_copy(spread2[0][:].indirect(entries(list2, cols)), first[:])
+                continue
+            direct(1, direct_banks[c % 2], [cols], r_codes_at, r_scale, w2_codes0, w2_scale0)
             scatter_gated(1, cols, list2, spread2[0])
         turn_back(1, 1, 0)
         products(1, 1, r_codes_at, r_scale, w2_codes, w2_scale)
@@ -347,7 +365,7 @@ def tile_moe_mod_none_kernel(
                 for cols in cuts[1][t]:
                     nc.vector.tensor_copy(spread2[t % 2][:].indirect(entries(list2, cols)), sums_at(1, t, cols))
             if t < 2:
-                done = keep.tile([P, T], F32, name="done%d" % t, tag="before%d" % t, align_bytes=64)
+                done = keep.tile([P, T], F32, name="done0", tag="before0", align_bytes=64) if t == 0 else relay_tile("done1", [P, T], F32, PLANE1_BYTES)
                 nc.gpsimd.tensor_tensor(done[:], stream[t][:], spread2[t % 2][:], ADD)
                 nc.sync.dma_start(out_rows[:, t, :], done[:])
                 if t == 0:

@@ -153,12 +153,12 @@ def tile_moe_mod_none_kernel(
             nc.sync.dma_start(gate_rows[layer][:], gate.rearrange("p (b s) -> (p b) s", s=P)[0:P, :])
 
         nc.sync.dma_start(list1[:], offs)
-        load_gate_rows(0, gate1)
+        nc.sync.dma_start(w1_codes[:], w1_words[0].rearrange("p i d -> p (i d)").bitcast(I32))
         load_scales(nc.sync, tok_scales, x_scales, (0, 1, 2))
         load_scales(nc.scalar, tok_scales, x_scales, (3,))
         nc.sync.dma_start(tok_words[:], x_words[0].rearrange("p t d -> p (t d)").bitcast(I32))
         load_scales(nc.sync, w1_scale, w1_scales, range(QUADRANTS))
-        nc.sync.dma_start(w1_codes[:], w1_words[0].rearrange("p i d -> p (i d)").bitcast(I32))
+        load_gate_rows(0, gate1)
         nc.scalar.copy(spread1[1][:], spread1[0][:])
         for cols in HEAD_REST:
             nc.sync.dma_start(gates[0][:, cols], gate1[:, cols])
@@ -259,8 +259,7 @@ def tile_moe_mod_none_kernel(
         for c, cols in enumerate(HEAD_REST):
             nc.vector.tensor_copy(x_codes[c][:], tok_words[:].bitcast(U32).indirect(entries(list1, cols)))
             if c == 0:
-                nc.gpsimd.tensor_copy(w1_scale0[:], w1_scale[:, 0:K:PACK])
-                nc.gpsimd.tensor_copy(w1_codes0[:], w1_codes[:, 0:K:PACK])
+                plane0_columns(nc.gpsimd, w1_codes0, w1_scale0, w1_codes, w1_scale)
         nc.gpsimd.memset(spread2[0][:], 0.0)
         direct(0, product_banks[0], token_cuts(0, 2 * P, 3 * P), x_codes_at, x_scale, w1_codes0, w1_scale0)
         scatter_gated(0, HEAD_REST[0], list1, spread1[0])
@@ -339,8 +338,8 @@ def tile_moe_mod_none_kernel(
                 continue
             direct(1, direct_banks[c % 2], [cols], r_codes_at, r_scale, w2_codes0, w2_scale0)
             scatter_gated(1, cols, list2, spread2[0])
-        turn_back(1, 1, 0)
         products(1, 1, r_codes_at, r_scale, w2_codes, w2_scale)
+        turn_back(1, 1, 0)
         turn_back(1, 1, 1)
         for t in range(2, PACK):
             for half in range(len(HALVES)):

@@ -20,35 +20,34 @@ MULT = mybir.AluOpType.mult
 P = 128
 PACK = 4
 LAST = PACK - 1
+RUN = 8
 GROUP = 16
 QUADRANTS = 4
 BLOCKS = S // P
-PLANE2_BYTES = BLOCKS * LAST * P * 4
-PLANE1_BYTES = PLANE2_BYTES + T * 4
-BANK_BLOCKS = 4
-
-QUARTERS = [slice(c * S // 4, (c + 1) * S // 4) for c in range(4)]
-HALVES = [slice(0, S // 2), slice(S // 2, S)]
-WHOLE = [slice(0, S)]
-PIECES = [QUARTERS[0], QUARTERS[1], HALVES[1]]
-HEAD_REST = [slice(0, 3 * P), slice(3 * P, S)]
+BANK = 512
+PLANE_BYTES = T * 4
+PLANE2_AT = BLOCKS * LAST * P * 4
+PLANE1_AT = PLANE2_AT + PLANE_BYTES
+ZEROS_AT = PLANE1_AT + PLANE_BYTES
 
 
-def token_cuts(*bounds):
+def cuts(*bounds):
     return [slice(a, b) for a, b in zip(bounds, bounds[1:])]
 
 
-TOKEN_HALVES = token_cuts(0, T // 2, T)
-VECTOR_CUTS = token_cuts(0, 512, 1024, 1536)
-GPSIMD_CUT = slice(1536, T)
-MIDDLE_CUTS = token_cuts(0, 512, 1024, 1408)
+HALVES = cuts(0, S // 2, S)
+WHOLE = cuts(0, S)
+HEAD_REST = cuts(0, 3 * P, S)
+PIECES = cuts(0, S // 4, S // 2, S)
+FIRST_REST = cuts(0, S // 4, S)
+MIDDLE_CUTS = cuts(0, 512, 1024, 1408)
 MIDDLE_REST = slice(1408, T)
-W2_CUTS = token_cuts(0, 192, 320, K)
-W2_RUNS = token_cuts(0, 128, 192, 320, 448, K)
-ADD_CUTS = [TOKEN_HALVES, token_cuts(0, 1024, 1792, T)]
-BANK_CUTS = token_cuts(0, 512, 1024, 1536, T)
-PLANE2_CUTS_LAYER1 = token_cuts(0, 1024, 1792, T)
-PLANE2_CUTS_LAYER2 = token_cuts(0, 1024, 1536, T)
+W2_HALVES = cuts(0, K // 2, K)
+ADD_CUTS = [cuts(0, T // 2, T), cuts(0, 1024, 1792, T)]
+BANK_CUTS = cuts(0, 512, 1024, 1536, T)
+PLANE2_CUTS = cuts(0, 1024, 1536, T)
+CLOSING_VECTOR = cuts(0, 256, 512, 1024, 1536)
+CLOSING_GPSIMD = cuts(1536, 1792, T)
 
 
 def tile_moe_mod_none_kernel(
@@ -60,10 +59,10 @@ def tile_moe_mod_none_kernel(
         relay = ctx.enter_context(tc.tile_pool(name="relay", bufs=1))
         psum = ctx.enter_context(tc.psum_pool(name="psum", bufs=1))
 
-        def sbuf(name, shape, dtype):
-            return keep.tile(shape, dtype, name=name, align_bytes=64)
+        def sbuf(name, shape, dtype, tag=None):
+            return keep.tile(shape, dtype, name=name, tag=tag or name, align_bytes=64)
 
-        def relay_tile(name, shape, dtype, offset=0):
+        def relay_tile(name, shape, dtype, offset):
             return relay.tile(shape, dtype, name=name, offset=offset, align_bytes=64)
 
         def width(cols):
@@ -76,72 +75,62 @@ def tile_moe_mod_none_kernel(
         def entries(lst, cols):
             return lst[:, cols.start // GROUP : cols.stop // GROUP]
 
-        list1 = sbuf("list1", [P, S // GROUP], U16)
-        list2 = sbuf("list2", [P, S // GROUP], U16)
+        def plane(array, t):
+            return array.rearrange("(g t j) n -> t g j n", t=PACK, j=RUN)[t]
+
+        lists = [sbuf("list%d" % layer, [P, S // GROUP], U16) for layer in range(2)]
         tok_words = sbuf("tok_words", [P, T], I32)
         tok_scales = sbuf("tok_scales", [P, T], U8)
+        w1_codes_raw = sbuf("w1_codes_raw", [P, K], I32)
+        w1_scale_raw = relay_tile("w1_scale_raw", [P, K], U8, ZEROS_AT + PLANE_BYTES - K // 2)
         w1_codes = sbuf("w1_codes", [P, K], I32)
         w1_scale = sbuf("w1_scale", [P, K], U8)
-        w1_codes0 = sbuf("w1_codes0", [P, P], I32)
-        w1_scale0 = sbuf("w1_scale0", [P, P], U8)
-        gates = [sbuf("gate%d" % layer, [P, S], F32) for layer in range(2)]
+        gate1_head = sbuf("gate1_head", [P, width(HEAD_REST[0])], F32)
+        gate1_rest = sbuf("gate1_rest", [P, width(HEAD_REST[1])], F32)
+        gate_first = sbuf("gate_first", [P, width(PIECES[0])], F32)
+        gate2_all = sbuf("gate2_all", [P, S], F32)
         gate_rows = [sbuf("gate_rows%d" % layer, [P, P], F32) for layer in range(2)]
-        gate_cols = [sbuf("gate_cols0", [P, BLOCKS], F32), relay_tile("gate_cols1", [P, BLOCKS], F32, PLANE1_BYTES)]
+        gate_cols = [sbuf("gate_cols0", [P, BLOCKS], F32), relay_tile("gate_cols1", [P, BLOCKS], F32, PLANE1_AT)]
         ident = sbuf("ident", [P, P], F32)
         w2_raw = sbuf("w2_raw", [P, PACK, K], F32)
         w2_scale = sbuf("w2_scale", [P, K], U8)
-        w2_codes0 = sbuf("w2_codes0", [P, P], I32)
-        w2_scale0 = sbuf("w2_scale0", [P, P], U8)
         before = [
-            relay_tile("before%d" % t, [P, T], F32, (PLANE1_BYTES, PLANE2_BYTES)[t - 1])
-            if t in (1, 2)
-            else sbuf("before%d" % t, [P, T], F32)
-            for t in range(PACK)
+            sbuf("before0", [P, T], F32),
+            relay_tile("before1", [P, T], F32, PLANE1_AT),
+            relay_tile("before2", [P, T], F32, PLANE2_AT),
+            sbuf("before3", [P, T], F32),
         ]
         again2 = sbuf("again2", [P, T], F32)
         stream = [sbuf("stream%d" % t, [P, T], F32) for t in range(2)]
-
-        spread1 = [sbuf("spread1_%d" % i, [P, T], F32) for i in range(2)]
-        spread2 = [
-            keep.tile([P, T], F32, name="spread2_0", tag="tok_words", align_bytes=64),
-            sbuf("spread2_1", [P, T], F32),
-        ]
         x_codes = [sbuf("x_codes%d" % c, [P, width(cols)], U32) for c, cols in enumerate(HEAD_REST)]
         x_scale = sbuf("x_scale", [P, S], U8)
         staged = sbuf("staged", [P, T], F32)
         r_bf = sbuf("r_bf", [P, S, PACK], BF16)
-        gate_first = sbuf("gate_first", [P, width(PIECES[0])], F32)
-        first = sbuf("first", [P, width(PIECES[0])], F32)
-        r_codes = []
-        w2_bf = []
         r_scale = sbuf("r_scale", [P, S], U8)
-        turned = [relay_tile("turned0", [P, BLOCKS, LAST, P], F32), sbuf("turned1", [P, BLOCKS, LAST, P], F32)]
-        cuts = [[HEAD_REST, HALVES, WHOLE, WHOLE], [PIECES, WHOLE, WHOLE, WHOLE]]
+        turned = [relay_tile("turned0", [P, BLOCKS, LAST, P], F32, 0), sbuf("turned1", [P, BLOCKS, LAST, P], F32)]
+        pieces = [[HEAD_REST, HEAD_REST, WHOLE, WHOLE], [FIRST_REST, HALVES, WHOLE, WHOLE]]
         sums = [
             [
-                [sbuf("sums%d_%d_%d" % (layer, t, c), [P, width(cols)], F32) for c, cols in enumerate(cuts[layer][t])]
+                [sbuf("sums%d_%d_%d" % (layer, t, c), [P, width(cols)], F32) for c, cols in enumerate(pieces[layer][t])]
                 for t in range(PACK)
             ]
             for layer in range(2)
         ]
 
         def sums_at(layer, t, cols):
-            return within(cuts[layer][t], sums[layer][t], cols)
+            return within(pieces[layer][t], sums[layer][t], cols)
 
+        direct_banks = [psum.tile([P, BANK], F32, name="direct%d" % i) for i in range(2)]
+        product_banks = [psum.tile([P, BANK], F32, name="product%d" % i) for i in range(3)]
+        turn_banks = [psum.tile([P, BANK], F32, name="turn%d" % i) for i in range(3)]
 
-        direct_banks = [psum.tile([P, K], F32, name="direct%d" % i) for i in range(2)]
-        product_banks = [psum.tile([P, K], F32, name="product%d" % i) for i in range(3)]
-        turn_banks = [psum.tile([P, K], F32, name="turn%d" % i) for i in range(3)]
-
+        spread = [[sbuf("spread0_0", [P, T], F32), sbuf("spread0_1", [P, T], F32)], [None, sbuf("spread1_1", [P, T], F32)]]
         nc.gpsimd.memset(tok_scales[:].bitcast(I32), 0)
-        nc.vector.memset(w1_scale[:].bitcast(I32), 0)
+        nc.vector.memset(w1_scale_raw[:].bitcast(I32), 0)
         make_identity(nc, ident[:])
-        nc.vector.memset(spread1[0][:], 0.0)
+        nc.vector.memset(spread[0][0][:], 0.0)
         nc.gpsimd.memset(w2_scale[:].bitcast(I32), 0)
-        nc.gpsimd.tensor_scalar(spread2[1][:], spread1[0][:], 1.0, 0.0, MULT, ADD)
-
-        xr_rows = xr.rearrange("(p t) n -> p t n", t=PACK)
-        out_rows = out.rearrange("(p t) n -> p t n", t=PACK)
+        nc.gpsimd.tensor_scalar(spread[1][1][:], spread[0][0][:], 1.0, 0.0, MULT, ADD)
 
         def load_scales(queue, tile, scales, quadrants):
             for q in quadrants:
@@ -152,36 +141,39 @@ def tile_moe_mod_none_kernel(
         def load_gate_rows(layer, gate):
             nc.sync.dma_start(gate_rows[layer][:], gate.rearrange("p (b s) -> (p b) s", s=P)[0:P, :])
 
-        nc.sync.dma_start(list1[:], offs)
-        nc.sync.dma_start(w1_codes[:], w1_words[0].rearrange("p i d -> p (i d)").bitcast(I32))
+        nc.sync.dma_start(lists[0][:], offs)
+        nc.sync.dma_start(w1_codes_raw[:], w1_words[0].rearrange("p i d -> p (i d)").bitcast(I32))
         load_scales(nc.sync, tok_scales, x_scales, (0, 1, 2))
         load_scales(nc.scalar, tok_scales, x_scales, (3,))
         nc.sync.dma_start(tok_words[:], x_words[0].rearrange("p t d -> p (t d)").bitcast(I32))
-        load_scales(nc.sync, w1_scale, w1_scales, range(QUADRANTS))
+        load_scales(nc.sync, w1_scale_raw, w1_scales, range(QUADRANTS))
         load_gate_rows(0, gate1)
-        nc.scalar.copy(spread1[1][:], spread1[0][:])
-        for cols in HEAD_REST:
-            nc.sync.dma_start(gates[0][:, cols], gate1[:, cols])
-        nc.sync.dma_start(list2[:], offs2)
+        nc.scalar.copy(spread[0][1][:], spread[0][0][:])
+        nc.sync.dma_start(gate1_head[:], gate1[:, HEAD_REST[0]])
+        nc.sync.dma_start(gate1_rest[:], gate1[:, HEAD_REST[1]])
+        nc.sync.dma_start(lists[1][:], offs2)
         load_gate_rows(1, gate2)
         for t in (0, LAST):
-            nc.sync.dma_start(before[t][:], xr_rows[:, t, :])
-        nc.sync.dma_start(w2_raw[:], w2.rearrange("(p j) n -> p j n", j=PACK))
+            nc.sync.dma_start(before[t][:], plane(xr, t))
+        for t in range(PACK):
+            nc.sync.dma_start(w2_raw[:, t, :], plane(w2, t))
         for t in (1, 2):
-            nc.sync.dma_start(before[t][:, 0:T], xr_rows[:, t, :])
+            nc.sync.dma_start(before[t][:], plane(xr, t))
         nc.sync.dma_start(gate_first[:], gate2[:, PIECES[0]])
-        nc.sync.dma_start(gates[1][:, PIECES[0].stop : S], gate2[:, PIECES[0].stop : S])
-        nc.sync.dma_start(again2[:], xr_rows[:, 2, :])
+        nc.sync.dma_start(gate2_all[:], gate2)
+        nc.sync.dma_start(again2[:], plane(xr, 2))
 
         def turn_gate(layer):
             nc.tensor.transpose(turn_banks[-1][:, 0:P], gate_rows[layer][:], ident[:])
             nc.scalar.activation(gate_cols[layer][:], turn_banks[-1][:, 0:BLOCKS], COPY)
 
-        def x_codes_at(cols):
-            return within(HEAD_REST, x_codes, cols)
+        r_codes = []
+        w_codes = [w1_codes]
+        w_scale = [w1_scale, w2_scale]
+        slot_scale = [x_scale, r_scale]
 
-        def r_codes_at(cols):
-            return within(PIECES, r_codes, cols)
+        def slot_codes(layer, cols):
+            return within(HEAD_REST, x_codes, cols) if layer == 0 else within(PIECES, r_codes, cols)
 
         def mx(bank, lhs_codes, lhs_scale, rhs_codes, rhs_scale):
             nc.tensor.matmul_mx(
@@ -194,41 +186,59 @@ def tile_moe_mod_none_kernel(
                 stop=True,
             )
 
-        def direct(layer, bank, passes, codes_at, scale, w_codes, w_scale, empty=nc.scalar.copy):
-            cols = slice(passes[0].start, passes[-1].stop)
+        def direct(layer, t, bank, passes):
+            rows = slice(t * P, (t + 1) * P)
             for run in passes:
-                part = bank[:, run.start - cols.start : run.stop - cols.start]
-                mx(part, w_codes[:], w_scale[:], codes_at(run), scale[:, run])
-            empty(sums_at(layer, 0, cols), bank[:, 0 : width(cols)])
+                part = bank[:, run.start - passes[0].start : run.stop - passes[0].start]
+                mx(part, w_codes[layer][:, rows], w_scale[layer][:, rows], slot_codes(layer, run), slot_scale[layer][:, run])
 
-        def scatter_gated(layer, cols, lst, window):
+        def direct_sums(layer, t, bank, passes):
+            direct(layer, t, bank, passes)
+            cols = slice(passes[0].start, passes[-1].stop)
+            nc.scalar.copy(sums_at(layer, t, cols), bank[:, 0 : width(cols)])
+
+        def scatter_gated(layer, t, cols, gate):
             nc.vector.tensor_tensor(
-                window[:].indirect(entries(lst, cols)), sums_at(layer, 0, cols), gates[layer][:, cols], MULT
+                spread[layer][t % LAST][:].indirect(entries(lists[layer], cols)), sums_at(layer, t, cols), gate, MULT
             )
 
-        def product(layer, b, codes_at, scale, w_codes, w_scale, by_plane):
-            cols = slice(b * P, (b + 1) * P)
-            bank = product_banks[b % len(product_banks)]
-            mx(bank[:], codes_at(cols), scale[:, cols], w_codes[:], w_scale[:])
-            nc.scalar.activation(
-                turned[layer][:, b, :, :],
-                bank[:].rearrange(by_plane, t=PACK)[:, 1:PACK, :],
-                COPY,
-                scale=gate_cols[layer][:, b : b + 1],
-            )
+        def scatter(layer, t, cols):
+            nc.vector.tensor_copy(spread[layer][t % LAST][:].indirect(entries(lists[layer], cols)), sums_at(layer, t, cols))
 
-        def turn_back(layer, t, half):
-            bank = turn_banks[(len(HALVES) * (t - 1) + half) % len(turn_banks)]
-            for j in range(BANK_BLOCKS):
-                block = turned[layer][:, BANK_BLOCKS * half + j, t - 1, :]
-                nc.tensor.transpose(bank[:, j * P : (j + 1) * P], block, ident[:])
-            nc.scalar.copy(sums_at(layer, t, HALVES[half]), bank[:])
+        def products(layer, planes, blocks, bank):
+            n = width(planes) * P
+            rows = slice(planes.start * P, planes.stop * P)
+            for i, b in enumerate(blocks):
+                cols = slice(b * P, (b + 1) * P)
+                mx(
+                    bank[:, i * n : (i + 1) * n],
+                    slot_codes(layer, cols),
+                    slot_scale[layer][:, cols],
+                    w_codes[layer][:, rows],
+                    w_scale[layer][:, rows],
+                )
+            for i, b in enumerate(blocks):
+                nc.scalar.activation(
+                    turned[layer][:, b, planes.start - 1 : planes.stop - 1, :].rearrange("s t m -> s (t m)"),
+                    bank[:, i * n : (i + 1) * n],
+                    COPY,
+                    scale=gate_cols[layer][:, b : b + 1],
+                )
 
-        def products(layer, half, codes_at, scale, w_codes, w_scale):
-            for b in range(BANK_BLOCKS * half, BANK_BLOCKS * (half + 1)):
-                product(layer, b, codes_at, scale, w_codes, w_scale, "s (m t) -> s t m")
+        def turn_back(layer, t, cols, bank):
+            for c in range(cols.start, cols.stop, P):
+                nc.tensor.transpose(
+                    bank[:, c - cols.start : c - cols.start + P], turned[layer][:, c // P, t - 1, :], ident[:]
+                )
+            nc.scalar.copy(sums_at(layer, t, cols), bank[:, 0 : width(cols)])
 
-        def turn_sum(terms, cols, bank, staged):
+        def late_planes(layer):
+            for pair in range(BLOCKS // 2):
+                products(layer, slice(2, PACK), [2 * pair, 2 * pair + 1], product_banks[pair % 3])
+            for i, (t, cols) in enumerate([(t, cols) for t in (2, LAST) for cols in HALVES]):
+                turn_back(layer, t, cols, turn_banks[(i + 2) % 3])
+
+        def turn_sum(terms, cols, bank):
             for c in range(cols.start, cols.stop, P):
                 for i, term in enumerate(terms):
                     nc.tensor.matmul(
@@ -241,152 +251,139 @@ def tile_moe_mod_none_kernel(
                     )
             nc.scalar.copy(staged[:, cols], bank[:, 0 : width(cols)])
 
-        def turn_again(staged, cols, bank):
+        def turn_again(cols, bank):
             for c in range(cols.start, cols.stop, P):
                 nc.tensor.transpose(bank[:, c - cols.start : c - cols.start + P], staged[:, c : c + P], ident[:])
 
         def round_w2(tile, cols):
-            nc.gpsimd.tensor_scalar(
-                tile[:], w2_raw[:, :, cols].rearrange("p j n -> p n j"), 1.0, 0.0, MULT, ADD
+            by_plane = w2_raw[:].rearrange("p u (g t j) -> p t g j u", t=PACK, j=RUN)
+            for t in range(cols.start // P, cols.stop // P):
+                part = tile[:, t * P - cols.start : (t + 1) * P - cols.start, :]
+                nc.gpsimd.tensor_scalar(
+                    part.rearrange("p (g j) u -> p g j u", j=RUN), by_plane[:, t, :, :, :], 1.0, 0.0, MULT, ADD
+                )
+
+        def to_plane_order(dst, src, run):
+            nc.gpsimd.tensor_copy(
+                dst.rearrange("p (t g j) -> p t g j", t=PACK, j=run), src.rearrange("p (g t j) -> p t g j", t=PACK, j=run)
             )
 
-        def plane0_columns(engine, codes0, scale0, codes, scale):
-            engine.tensor_copy(codes0[:], codes[:, 0:K:PACK])
-            engine.tensor_copy(scale0[:], scale[:, 0:K:PACK])
-
+        head, rest = HEAD_REST
+        to_plane_order(w1_codes[:], w1_codes_raw[:], RUN)
+        to_plane_order(w1_scale[:].bitcast(I32), w1_scale_raw[:].bitcast(I32), RUN // 4)
+        spread[0].append(relay_tile("spread0_2", [P, T], F32, ZEROS_AT))
+        spread[1].append(relay_tile("spread1_2", [P, T], F32, ZEROS_AT + PLANE_BYTES))
         turn_gate(0)
-        nc.vector.tensor_copy(x_scale[:], tok_scales[:].indirect(list1[:]))
+        nc.vector.tensor_copy(x_scale[:], tok_scales[:].indirect(lists[0][:]))
         for c, cols in enumerate(HEAD_REST):
-            nc.vector.tensor_copy(x_codes[c][:], tok_words[:].bitcast(U32).indirect(entries(list1, cols)))
-            if c == 0:
-                plane0_columns(nc.gpsimd, w1_codes0, w1_scale0, w1_codes, w1_scale)
-        nc.gpsimd.memset(spread2[0][:], 0.0)
-        direct(0, product_banks[0], token_cuts(0, 2 * P, 3 * P), x_codes_at, x_scale, w1_codes0, w1_scale0)
-        scatter_gated(0, HEAD_REST[0], list1, spread1[0])
-        for b in range(1):
-            product(0, b, x_codes_at, x_scale, w1_codes, w1_scale, "s (m t) -> s t m")
-        for c, run in enumerate(token_cuts(3 * P, 7 * P, S)):
-            direct(0, product_banks[c + 1], [run], x_codes_at, x_scale, w1_codes0, w1_scale0)
-        scatter_gated(0, HEAD_REST[1], list1, spread1[0])
-        for b in range(1, BANK_BLOCKS):
-            product(0, b, x_codes_at, x_scale, w1_codes, w1_scale, "s (m t) -> s t m")
-        turn_back(0, 1, 0)
-        products(0, 1, x_codes_at, x_scale, w1_codes, w1_scale)
-        turn_back(0, 1, 1)
-        for t in range(2, PACK):
-            for half in range(len(HALVES)):
-                turn_back(0, t, half)
+            nc.vector.tensor_copy(x_codes[c][:], tok_words[:].bitcast(U32).indirect(entries(lists[0], cols)))
+        spread[1][0] = sbuf("spread1_0", [P, T], F32, tag="tok_words")
+        for tile in (spread[0][2], spread[1][2], spread[1][0]):
+            nc.gpsimd.memset(tile[:], 0.0)
+        for t, bank in ((0, product_banks[0]), (1, direct_banks[0])):
+            direct_sums(0, t, bank, cuts(0, 2 * P, 3 * P))
+            scatter_gated(0, t, head, gate1_head[:])
+        for run, bank in zip(cuts(3 * P, 7 * P, S), product_banks[1:]):
+            direct_sums(0, 0, bank, [run])
+        scatter_gated(0, 0, rest, gate1_rest[:])
+        products(0, slice(1, 2), range(3, 7), direct_banks[1])
+        products(0, slice(1, 2), range(7, BLOCKS), direct_banks[0])
+        for cols, bank in zip(cuts(3 * P, 7 * P, S), turn_banks):
+            turn_back(0, 1, cols, bank)
+        scatter(0, 1, rest)
+        late_planes(0)
         for cols, bank in zip(MIDDLE_CUTS, turn_banks):
-            turn_sum([before[LAST]], cols, bank, staged)
+            turn_sum([before[LAST]], cols, bank)
         for cols, bank in zip(MIDDLE_CUTS, product_banks):
-            turn_again(staged, cols, bank)
+            turn_again(cols, bank)
+        w2_bf = []
         for t in range(PACK):
-            if t > 0:
-                for cols in cuts[0][t]:
-                    nc.vector.tensor_copy(spread1[t % 2][:].indirect(entries(list1, cols)), sums_at(0, t, cols))
+            if t >= 2:
+                scatter(0, t, WHOLE[0])
             if t < 2:
                 stream_bf = relay_tile("stream_bf%d" % t, [P, T], BF16, t * T)
                 for cols in ADD_CUTS[t]:
-                    nc.gpsimd.tensor_tensor(stream[t][:, cols], before[t][:, cols], spread1[t % 2][:, cols], ADD)
+                    nc.gpsimd.tensor_tensor(stream[t][:, cols], before[t][:, cols], spread[0][t][:, cols], ADD)
                     nc.scalar.copy(stream_bf[:, cols], stream[t][:, cols])
             if t == 2:
                 stream_bf = sbuf("stream_bf2", [P, T], BF16)
-                nc.gpsimd.tensor_tensor(stream_bf[:], before[t][:], spread1[t % 2][:], ADD)
+                nc.gpsimd.tensor_tensor(stream_bf[:], before[t][:], spread[0][t][:], ADD)
             if t == 1:
                 turn_gate(1)
             if t < LAST:
-                nc.scalar.activation(r_bf[:, :, t], stream_bf[:].indirect(list2[:]), COPY)
-            if t < LAST:
-                shape = [P, width(W2_CUTS[t]), PACK]
-                if t == 0:
-                    w2_bf.append(keep.tile(shape, BF16, name="w2_bf0", tag="before0", align_bytes=64))
-                else:
-                    w2_bf.append(relay_tile("w2_bf%d" % t, shape, BF16, (PLANE1_BYTES + 64, PLANE2_BYTES + 3 * T)[t - 1]))
-                round_w2(w2_bf[t], W2_CUTS[t])
-        last_bf = relay_tile("last_bf", [P, T], BF16, PLANE2_BYTES)
+                nc.scalar.activation(r_bf[:, :, t], stream_bf[:].indirect(lists[1][:]), COPY)
+            if t in (1, 2):
+                at = (PLANE1_AT + 64, PLANE2_AT + 3 * T)[t - 1]
+                w2_bf.append(relay_tile("w2_bf%d" % t, [P, K // 2, PACK], BF16, at))
+                round_w2(w2_bf[t - 1], W2_HALVES[t - 1])
+        last_bf = relay_tile("last_bf", [P, T], BF16, PLANE2_AT)
         for cols, bank in zip(MIDDLE_CUTS, product_banks):
-            nc.vector.tensor_tensor(last_bf[:, cols], bank[:, 0 : width(cols)], spread1[LAST % 2][:, cols], ADD)
-        nc.gpsimd.tensor_tensor(
-            last_bf[:, MIDDLE_REST], before[LAST][:, MIDDLE_REST], spread1[LAST % 2][:, MIDDLE_REST], ADD
-        )
-        w2_codes = relay_tile("w2_codes", [P, K], I32, PLANE2_BYTES + 2 * T)
-        for cols in W2_RUNS:
+            nc.vector.tensor_tensor(last_bf[:, cols], bank[:, 0 : width(cols)], spread[0][0][:, cols], ADD)
+        nc.gpsimd.tensor_tensor(last_bf[:, MIDDLE_REST], before[LAST][:, MIDDLE_REST], spread[0][0][:, MIDDLE_REST], ADD)
+        w_codes.append(relay_tile("w2_codes", [P, K], I32, PLANE2_AT + 2 * T))
+        for tile, cols in zip(w2_bf, W2_HALVES):
             nc.vector.quantize_mx(
-                out=w2_codes[:, cols].bitcast(FP8X4),
+                out=w_codes[1][:, cols].bitcast(FP8X4),
                 scales=w2_scale[:, cols],
-                in_=within(W2_CUTS, w2_bf, cols).rearrange("p n j -> p (n j)"),
+                in_=tile[:].rearrange("p n j -> p (n j)"),
             )
-        plane0_columns(nc.vector, w2_codes0, w2_scale0, w2_codes, w2_scale)
 
+        first, rest = FIRST_REST
         for c, cols in enumerate(PIECES):
-            nc.scalar.activation(r_bf[:, cols, LAST], last_bf[:].indirect(entries(list2, cols)), COPY)
-            if c == len(PIECES) - 1:
-                r_codes.append(keep.tile([P, width(cols)], U32, name="r_codes_last", tag="gate_first", align_bytes=64))
-            else:
-                r_codes.append(sbuf("r_codes%d" % c, [P, width(cols)], U32))
+            nc.scalar.activation(r_bf[:, cols, LAST], last_bf[:].indirect(entries(lists[1], cols)), COPY)
+            r_codes.append(sbuf("r_codes%d" % c, [P, width(cols)], U32, tag="gate_first" if c == 2 else None))
             nc.vector.quantize_mx(
                 out=r_codes[c][:].bitcast(FP8X4),
                 scales=r_scale[:, cols],
                 in_=r_bf[:, cols, :].rearrange("p s j -> p (s j)"),
             )
-            if c == len(PIECES) - 1:
-                products(1, 0, r_codes_at, r_scale, w2_codes, w2_scale)
             if c == 0:
-                mx(direct_banks[0][:, cols], w2_codes0[:], w2_scale0[:], r_codes_at(cols), r_scale[:, cols])
-                nc.vector.tensor_tensor(first[:], direct_banks[0][:, cols], gate_first[:], MULT)
-                nc.vector.tensor_copy(spread2[0][:].indirect(entries(list2, cols)), first[:])
-                continue
-            direct(1, direct_banks[c % 2], [cols], r_codes_at, r_scale, w2_codes0, w2_scale0)
-            scatter_gated(1, cols, list2, spread2[0])
-        products(1, 1, r_codes_at, r_scale, w2_codes, w2_scale)
-        turn_back(1, 1, 0)
-        turn_back(1, 1, 1)
-        for t in range(2, PACK):
-            for half in range(len(HALVES)):
-                turn_back(1, t, half)
-        r2_end = sbuf("r2_end", [P, width(GPSIMD_CUT)], F32)
-        turn_sum([again2, spread1[0]], GPSIMD_CUT, product_banks[0], staged)
-        turn_again(staged, GPSIMD_CUT, turn_banks[0])
-        nc.scalar.copy(r2_end[:], turn_banks[0][:])
-        staged_last = sbuf("staged_last", [P, T], F32)
-        r_last = sbuf("r_last", [P, width(GPSIMD_CUT)], F32)
+                direct(1, 0, direct_banks[0], [cols])
+                nc.vector.tensor_tensor(sums_at(1, 0, cols), direct_banks[0][:, cols], gate_first[:], MULT)
+                scatter(1, 0, cols)
+        direct_sums(1, 1, direct_banks[1], PIECES[0:2])
+        scatter_gated(1, 1, HALVES[0], gate2_all[:, HALVES[0]])
+        for run, bank in zip(PIECES[1:], product_banks):
+            direct_sums(1, 0, bank, [run])
+        scatter_gated(1, 0, rest, gate2_all[:, rest])
+        products(1, slice(1, 2), range(BLOCKS // 2, BLOCKS), product_banks[2])
+        turn_back(1, 1, HALVES[1], turn_banks[1])
+        scatter(1, 1, HALVES[1])
+        late_planes(1)
+        r2 = sbuf("r2", [P, T], F32, tag="before0")
         for g, cols in enumerate(BANK_CUTS):
-            turn_sum([before[LAST], spread1[1]], cols, turn_banks[(g + 1) % 3], staged_last)
-        for cols, bank in zip(VECTOR_CUTS, product_banks):
-            turn_again(staged_last, cols, bank)
-        for cols, bank in zip(token_cuts(GPSIMD_CUT.start, T - 2 * P, T), direct_banks):
-            turn_again(staged_last, cols, bank)
-            nc.scalar.copy(
-                r_last[:, cols.start - GPSIMD_CUT.start : cols.stop - GPSIMD_CUT.start], bank[:, 0 : width(cols)]
-            )
+            turn_sum([again2, spread[0][2]], cols, product_banks[(g + 1) % 3])
+        for g, cols in enumerate(BANK_CUTS):
+            turn_again(cols, turn_banks[g % 3])
+            nc.scalar.copy(r2[:, cols], turn_banks[g % 3][:])
+        for g, cols in enumerate(BANK_CUTS):
+            turn_sum([before[LAST], spread[0][0]], cols, turn_banks[(g + 1) % 3])
+        for cols, bank in zip(BANK_CUTS[0:3], product_banks):
+            turn_again(cols, bank)
+        r_last = [sbuf("r_last%d" % c, [P, width(cols)], F32) for c, cols in enumerate(CLOSING_GPSIMD)]
+        for cols, bank, tile in zip(CLOSING_GPSIMD, direct_banks, r_last):
+            turn_again(cols, bank)
+            nc.scalar.copy(tile[:], bank[:, 0 : width(cols)])
         for t in range(PACK):
-            if t > 0:
-                for cols in cuts[1][t]:
-                    nc.vector.tensor_copy(spread2[t % 2][:].indirect(entries(list2, cols)), sums_at(1, t, cols))
+            if t >= 2:
+                scatter(1, t, WHOLE[0])
             if t < 2:
-                done = keep.tile([P, T], F32, name="done0", tag="before0", align_bytes=64) if t == 0 else relay_tile("done1", [P, T], F32, PLANE1_BYTES)
-                nc.gpsimd.tensor_tensor(done[:], stream[t][:], spread2[t % 2][:], ADD)
-                nc.sync.dma_start(out_rows[:, t, :], done[:])
-                if t == 0:
-                    r2 = keep.tile([P, GPSIMD_CUT.start], F32, name="r2", tag="stream0", align_bytes=64)
-                cols = token_cuts(0, GPSIMD_CUT.start // 2, GPSIMD_CUT.start)[t]
-                nc.gpsimd.tensor_tensor(r2[:, cols], again2[:, cols], spread1[0][:, cols], ADD)
+                nc.gpsimd.tensor_tensor(stream[t][:], stream[t][:], spread[1][t][:], ADD)
+                nc.sync.dma_start(plane(out, t), stream[t][:])
             if t == 2:
-                for cols in PLANE2_CUTS_LAYER2:
-                    part = r2_end[:] if cols == GPSIMD_CUT else r2[:, cols]
-                    nc.gpsimd.tensor_tensor(part, part, spread2[t % 2][:, cols], ADD)
-                    nc.sync.dma_start(out_rows[:, t, cols], part)
-        result = keep.tile([P, GPSIMD_CUT.start], F32, name="result", tag="tok_words", align_bytes=64)
-        for cols in token_cuts(0, 256, 512, 1024, GPSIMD_CUT.start):
-            g = cols.start // K
+                for cols in PLANE2_CUTS:
+                    nc.gpsimd.tensor_tensor(r2[:, cols], r2[:, cols], spread[1][t][:, cols], ADD)
+                    nc.sync.dma_start(plane(out, t)[:, :, cols], r2[:, cols])
+        result = relay_tile("result", [P, CLOSING_VECTOR[-1].stop], F32, ZEROS_AT + PLANE_BYTES)
+        for cols in CLOSING_VECTOR:
+            g = cols.start // BANK
             nc.vector.tensor_tensor(
                 result[:, cols],
-                product_banks[g][:, cols.start - g * K : cols.stop - g * K],
-                spread2[LAST % 2][:, cols],
+                product_banks[g][:, cols.start - g * BANK : cols.stop - g * BANK],
+                spread[1][0][:, cols],
                 ADD,
             )
-            nc.sync.dma_start(out_rows[:, LAST, cols], result[:, cols])
-        for cols in token_cuts(GPSIMD_CUT.start, T - 2 * P, T):
-            part = r_last[:, cols.start - GPSIMD_CUT.start : cols.stop - GPSIMD_CUT.start]
-            nc.gpsimd.tensor_tensor(part, part, spread2[LAST % 2][:, cols], ADD)
-            nc.scalar.dma_start(out_rows[:, LAST, cols], part)
+            nc.sync.dma_start(plane(out, LAST)[:, :, cols], result[:, cols])
+        for cols, tile in zip(CLOSING_GPSIMD, r_last):
+            nc.gpsimd.tensor_tensor(tile[:], tile[:], spread[1][0][:, cols], ADD)
+            nc.scalar.dma_start(plane(out, LAST)[:, :, cols], tile[:])

@@ -28,7 +28,6 @@ BANK = 512
 PLANE_BYTES = T * 4
 PLANE2_AT = BLOCKS * LAST * P * 4
 PLANE1_AT = PLANE2_AT + PLANE_BYTES
-ZEROS_AT = PLANE1_AT + PLANE_BYTES
 
 
 def cuts(*bounds):
@@ -42,7 +41,7 @@ PIECES = cuts(0, S // 4, S // 2, S)
 FIRST_REST = cuts(0, S // 4, S)
 MIDDLE_CUTS = cuts(0, 512, 1024, 1408)
 MIDDLE_REST = slice(1408, T)
-W2_HALVES = cuts(0, K // 2, K)
+W2_CUTS = cuts(0, P, 2 * P, K)
 ADD_CUTS = [cuts(0, T // 2, T), cuts(0, 1024, 1792, T)]
 BANK_CUTS = cuts(0, 512, 1024, 1536, T)
 PLANE2_CUTS = cuts(0, 1024, 1536, T)
@@ -82,7 +81,7 @@ def tile_moe_mod_none_kernel(
         tok_words = sbuf("tok_words", [P, T], I32)
         tok_scales = sbuf("tok_scales", [P, T], U8)
         w1_codes_raw = sbuf("w1_codes_raw", [P, K], I32)
-        w1_scale_raw = relay_tile("w1_scale_raw", [P, K], U8, ZEROS_AT + PLANE_BYTES - K // 2)
+        w1_scale_raw = sbuf("w1_scale_raw", [P, K], U8)
         w1_codes = sbuf("w1_codes", [P, K], I32)
         w1_scale = sbuf("w1_scale", [P, K], U8)
         gate1_head = sbuf("gate1_head", [P, width(HEAD_REST[0])], F32)
@@ -90,7 +89,7 @@ def tile_moe_mod_none_kernel(
         gate_first = sbuf("gate_first", [P, width(PIECES[0])], F32)
         gate2_all = sbuf("gate2_all", [P, S], F32)
         gate_rows = [sbuf("gate_rows%d" % layer, [P, P], F32) for layer in range(2)]
-        gate_cols = [sbuf("gate_cols0", [P, BLOCKS], F32), relay_tile("gate_cols1", [P, BLOCKS], F32, PLANE1_AT)]
+        gate_cols = [sbuf("gate_cols0", [P, BLOCKS], F32), relay_tile("gate_cols1", [P, BLOCKS], F32, T // 2)]
         ident = sbuf("ident", [P, P], F32)
         w2_raw = sbuf("w2_raw", [P, PACK, K], F32)
         w2_scale = sbuf("w2_scale", [P, K], U8)
@@ -100,7 +99,6 @@ def tile_moe_mod_none_kernel(
             relay_tile("before2", [P, T], F32, PLANE2_AT),
             sbuf("before3", [P, T], F32),
         ]
-        again2 = sbuf("again2", [P, T], F32)
         stream = [sbuf("stream%d" % t, [P, T], F32) for t in range(2)]
         x_codes = [sbuf("x_codes%d" % c, [P, width(cols)], U32) for c, cols in enumerate(HEAD_REST)]
         x_scale = sbuf("x_scale", [P, S], U8)
@@ -124,7 +122,7 @@ def tile_moe_mod_none_kernel(
         product_banks = [psum.tile([P, BANK], F32, name="product%d" % i) for i in range(3)]
         turn_banks = [psum.tile([P, BANK], F32, name="turn%d" % i) for i in range(3)]
 
-        spread = [[sbuf("spread0_0", [P, T], F32), sbuf("spread0_1", [P, T], F32)], [None, sbuf("spread1_1", [P, T], F32)]]
+        spread = [[sbuf("spread0_%d" % i, [P, T], F32) for i in range(LAST)], [None, sbuf("spread1_1", [P, T], F32)]]
         nc.gpsimd.memset(tok_scales[:].bitcast(I32), 0)
         nc.vector.memset(w1_scale_raw[:].bitcast(I32), 0)
         make_identity(nc, ident[:])
@@ -148,7 +146,8 @@ def tile_moe_mod_none_kernel(
         nc.sync.dma_start(tok_words[:], x_words[0].rearrange("p t d -> p (t d)").bitcast(I32))
         load_scales(nc.sync, w1_scale_raw, w1_scales, range(QUADRANTS))
         load_gate_rows(0, gate1)
-        nc.scalar.copy(spread[0][1][:], spread[0][0][:])
+        for tile in spread[0][1:]:
+            nc.scalar.copy(tile[:], spread[0][0][:])
         nc.sync.dma_start(gate1_head[:], gate1[:, HEAD_REST[0]])
         nc.sync.dma_start(gate1_rest[:], gate1[:, HEAD_REST[1]])
         nc.sync.dma_start(lists[1][:], offs2)
@@ -161,7 +160,6 @@ def tile_moe_mod_none_kernel(
             nc.sync.dma_start(before[t][:], plane(xr, t))
         nc.sync.dma_start(gate_first[:], gate2[:, PIECES[0]])
         nc.sync.dma_start(gate2_all[:], gate2)
-        nc.sync.dma_start(again2[:], plane(xr, 2))
 
         def turn_gate(layer):
             nc.tensor.transpose(turn_banks[-1][:, 0:P], gate_rows[layer][:], ident[:])
@@ -259,9 +257,11 @@ def tile_moe_mod_none_kernel(
             by_plane = w2_raw[:].rearrange("p u (g t j) -> p t g j u", t=PACK, j=RUN)
             for t in range(cols.start // P, cols.stop // P):
                 part = tile[:, t * P - cols.start : (t + 1) * P - cols.start, :]
-                nc.gpsimd.tensor_scalar(
-                    part.rearrange("p (g j) u -> p g j u", j=RUN), by_plane[:, t, :, :, :], 1.0, 0.0, MULT, ADD
-                )
+                part = part.rearrange("p (g j) u -> p g j u", j=RUN)
+                if t == 0:
+                    nc.scalar.copy(part, by_plane[:, t, :, :, :])
+                else:
+                    nc.gpsimd.tensor_scalar(part, by_plane[:, t, :, :, :], 1.0, 0.0, MULT, ADD)
 
         def to_plane_order(dst, src, run):
             nc.gpsimd.tensor_copy(
@@ -271,15 +271,10 @@ def tile_moe_mod_none_kernel(
         head, rest = HEAD_REST
         to_plane_order(w1_codes[:], w1_codes_raw[:], RUN)
         to_plane_order(w1_scale[:].bitcast(I32), w1_scale_raw[:].bitcast(I32), RUN // 4)
-        spread[0].append(relay_tile("spread0_2", [P, T], F32, ZEROS_AT))
-        spread[1].append(relay_tile("spread1_2", [P, T], F32, ZEROS_AT + PLANE_BYTES))
         turn_gate(0)
         nc.vector.tensor_copy(x_scale[:], tok_scales[:].indirect(lists[0][:]))
         for c, cols in enumerate(HEAD_REST):
             nc.vector.tensor_copy(x_codes[c][:], tok_words[:].bitcast(U32).indirect(entries(lists[0], cols)))
-        spread[1][0] = sbuf("spread1_0", [P, T], F32, tag="tok_words")
-        for tile in (spread[0][2], spread[1][2], spread[1][0]):
-            nc.gpsimd.memset(tile[:], 0.0)
         for t, bank in ((0, product_banks[0]), (1, direct_banks[0])):
             direct_sums(0, t, bank, cuts(0, 2 * P, 3 * P))
             scatter_gated(0, t, head, gate1_head[:])
@@ -310,18 +305,27 @@ def tile_moe_mod_none_kernel(
                 nc.gpsimd.tensor_tensor(stream_bf[:], before[t][:], spread[0][t][:], ADD)
             if t == 1:
                 turn_gate(1)
+            for c in ((), (0, 1), (2,), ())[t]:
+                shape = [P, width(W2_CUTS[c]), PACK]
+                if c == 1:
+                    w2_bf.append(sbuf("w2_bf1", shape, BF16, tag="spread0_1"))
+                else:
+                    w2_bf.append(relay_tile("w2_bf%d" % c, shape, BF16, (0, None, PLANE2_AT + 3 * T)[c]))
+                round_w2(w2_bf[c], W2_CUTS[c])
             if t < LAST:
                 nc.scalar.activation(r_bf[:, :, t], stream_bf[:].indirect(lists[1][:]), COPY)
-            if t in (1, 2):
-                at = (PLANE1_AT + 64, PLANE2_AT + 3 * T)[t - 1]
-                w2_bf.append(relay_tile("w2_bf%d" % t, [P, K // 2, PACK], BF16, at))
-                round_w2(w2_bf[t - 1], W2_HALVES[t - 1])
+        spread[1][0] = sbuf("spread1_0", [P, T], F32, tag="before0")
+        spread[1].append(relay_tile("spread1_2", [P, T], F32, PLANE1_AT))
+        for tile in (spread[1][0], spread[1][2]):
+            nc.sync.dma_start(tile[:], spread[1][1][:])
+        again2 = sbuf("again2", [P, T], F32, tag="w2_raw")
+        nc.sync.dma_start(again2[:], plane(xr, 2))
         last_bf = relay_tile("last_bf", [P, T], BF16, PLANE2_AT)
         for cols, bank in zip(MIDDLE_CUTS, product_banks):
             nc.vector.tensor_tensor(last_bf[:, cols], bank[:, 0 : width(cols)], spread[0][0][:, cols], ADD)
         nc.gpsimd.tensor_tensor(last_bf[:, MIDDLE_REST], before[LAST][:, MIDDLE_REST], spread[0][0][:, MIDDLE_REST], ADD)
         w_codes.append(relay_tile("w2_codes", [P, K], I32, PLANE2_AT + 2 * T))
-        for tile, cols in zip(w2_bf, W2_HALVES):
+        for tile, cols in zip(w2_bf, W2_CUTS):
             nc.vector.quantize_mx(
                 out=w_codes[1][:, cols].bitcast(FP8X4),
                 scales=w2_scale[:, cols],
@@ -350,7 +354,7 @@ def tile_moe_mod_none_kernel(
         turn_back(1, 1, HALVES[1], turn_banks[1])
         scatter(1, 1, HALVES[1])
         late_planes(1)
-        r2 = sbuf("r2", [P, T], F32, tag="before0")
+        r2 = sbuf("r2", [P, T], F32, tag="tok_words")
         for g, cols in enumerate(BANK_CUTS):
             turn_sum([again2, spread[0][2]], cols, product_banks[(g + 1) % 3])
         for g, cols in enumerate(BANK_CUTS):
@@ -374,7 +378,7 @@ def tile_moe_mod_none_kernel(
                 for cols in PLANE2_CUTS:
                     nc.gpsimd.tensor_tensor(r2[:, cols], r2[:, cols], spread[1][t][:, cols], ADD)
                     nc.sync.dma_start(plane(out, t)[:, :, cols], r2[:, cols])
-        result = relay_tile("result", [P, CLOSING_VECTOR[-1].stop], F32, ZEROS_AT + PLANE_BYTES)
+        result = relay_tile("result", [P, CLOSING_VECTOR[-1].stop], F32, PLANE1_AT)
         for cols in CLOSING_VECTOR:
             g = cols.start // BANK
             nc.vector.tensor_tensor(

@@ -20,7 +20,6 @@ MULT = mybir.AluOpType.mult
 P = 128
 PACK = 4
 LAST = PACK - 1
-RUN = 8
 GROUP = 16
 QUADRANTS = 4
 BLOCKS = S // P
@@ -28,6 +27,7 @@ BANK = 512
 PLANE_BYTES = T * 4
 PLANE2_AT = BLOCKS * LAST * P * 4
 PLANE1_AT = PLANE2_AT + PLANE_BYTES
+W1_AT = PLANE1_AT + PLANE_BYTES
 
 
 def cuts(*bounds):
@@ -41,7 +41,7 @@ PIECES = cuts(0, S // 4, S // 2, S)
 FIRST_REST = cuts(0, S // 4, S)
 MIDDLE_CUTS = cuts(0, 512, 1024, 1408)
 MIDDLE_REST = slice(1408, T)
-W2_CUTS = cuts(0, P, 2 * P, K)
+PAIRS = cuts(0, K // 2, K)
 ADD_CUTS = [cuts(0, T // 2, T), cuts(0, 1024, 1792, T)]
 BANK_CUTS = cuts(0, 512, 1024, 1536, T)
 PLANE2_CUTS = cuts(0, 1024, 1536, T)
@@ -75,14 +75,14 @@ def tile_moe_mod_none_kernel(
             return lst[:, cols.start // GROUP : cols.stop // GROUP]
 
         def plane(array, t):
-            return array.rearrange("(g t j) n -> t g j n", t=PACK, j=RUN)[t]
+            return array.rearrange("(p t) n -> p t n", t=PACK)[:, t, :]
 
         lists = [sbuf("list%d" % layer, [P, S // GROUP], U16) for layer in range(2)]
         tok_words = sbuf("tok_words", [P, T], I32)
         tok_scales = sbuf("tok_scales", [P, T], U8)
         w1_codes_raw = sbuf("w1_codes_raw", [P, K], I32)
-        w1_scale_raw = sbuf("w1_scale_raw", [P, K], U8)
-        w1_codes = sbuf("w1_codes", [P, K], I32)
+        w1_scale_raw = relay_tile("w1_scale_raw", [P, K], U8, W1_AT)
+        w1_codes = [sbuf("w1_codes0", [P, K // 2], I32), relay_tile("w1_codes1", [P, K // 2], I32, W1_AT)]
         w1_scale = sbuf("w1_scale", [P, K], U8)
         gate1_head = sbuf("gate1_head", [P, width(HEAD_REST[0])], F32)
         gate1_rest = sbuf("gate1_rest", [P, width(HEAD_REST[1])], F32)
@@ -154,8 +154,7 @@ def tile_moe_mod_none_kernel(
         load_gate_rows(1, gate2)
         for t in (0, LAST):
             nc.sync.dma_start(before[t][:], plane(xr, t))
-        for t in range(PACK):
-            nc.sync.dma_start(w2_raw[:, t, :], plane(w2, t))
+        nc.sync.dma_start(w2_raw[:], w2.rearrange("(p u) n -> p u n", u=PACK))
         for t in (1, 2):
             nc.sync.dma_start(before[t][:], plane(xr, t))
         nc.sync.dma_start(gate_first[:], gate2[:, PIECES[0]])
@@ -166,12 +165,15 @@ def tile_moe_mod_none_kernel(
             nc.scalar.activation(gate_cols[layer][:], turn_banks[-1][:, 0:BLOCKS], COPY)
 
         r_codes = []
-        w_codes = [w1_codes]
+        w2_codes = []
         w_scale = [w1_scale, w2_scale]
         slot_scale = [x_scale, r_scale]
 
         def slot_codes(layer, cols):
             return within(HEAD_REST, x_codes, cols) if layer == 0 else within(PIECES, r_codes, cols)
+
+        def weight_codes(layer, rows):
+            return within(PAIRS, w1_codes, rows) if layer == 0 else w2_codes[0][:, rows]
 
         def mx(bank, lhs_codes, lhs_scale, rhs_codes, rhs_scale):
             nc.tensor.matmul_mx(
@@ -188,7 +190,7 @@ def tile_moe_mod_none_kernel(
             rows = slice(t * P, (t + 1) * P)
             for run in passes:
                 part = bank[:, run.start - passes[0].start : run.stop - passes[0].start]
-                mx(part, w_codes[layer][:, rows], w_scale[layer][:, rows], slot_codes(layer, run), slot_scale[layer][:, run])
+                mx(part, weight_codes(layer, rows), w_scale[layer][:, rows], slot_codes(layer, run), slot_scale[layer][:, run])
 
         def direct_sums(layer, t, bank, passes):
             direct(layer, t, bank, passes)
@@ -212,7 +214,7 @@ def tile_moe_mod_none_kernel(
                     bank[:, i * n : (i + 1) * n],
                     slot_codes(layer, cols),
                     slot_scale[layer][:, cols],
-                    w_codes[layer][:, rows],
+                    weight_codes(layer, rows),
                     w_scale[layer][:, rows],
                 )
             for i, b in enumerate(blocks):
@@ -236,7 +238,7 @@ def tile_moe_mod_none_kernel(
             for i, (t, cols) in enumerate([(t, cols) for t in (2, LAST) for cols in HALVES]):
                 turn_back(layer, t, cols, turn_banks[(i + 2) % 3])
 
-        def turn_sum(terms, cols, bank):
+        def turn_sum(terms, cols, bank, staged):
             for c in range(cols.start, cols.stop, P):
                 for i, term in enumerate(terms):
                     nc.tensor.matmul(
@@ -249,28 +251,25 @@ def tile_moe_mod_none_kernel(
                     )
             nc.scalar.copy(staged[:, cols], bank[:, 0 : width(cols)])
 
-        def turn_again(cols, bank):
+        def turn_again(staged, cols, bank):
             for c in range(cols.start, cols.stop, P):
                 nc.tensor.transpose(bank[:, c - cols.start : c - cols.start + P], staged[:, c : c + P], ident[:])
 
-        def round_w2(tile, cols):
-            by_plane = w2_raw[:].rearrange("p u (g t j) -> p t g j u", t=PACK, j=RUN)
-            for t in range(cols.start // P, cols.stop // P):
-                part = tile[:, t * P - cols.start : (t + 1) * P - cols.start, :]
-                part = part.rearrange("p (g j) u -> p g j u", j=RUN)
-                if t == 0:
-                    nc.scalar.copy(part, by_plane[:, t, :, :, :])
-                else:
-                    nc.gpsimd.tensor_scalar(part, by_plane[:, t, :, :, :], 1.0, 0.0, MULT, ADD)
+        def pair_of(src, pair):
+            return src.rearrange("p (m t) -> p t m", t=PACK)[:, 2 * pair : 2 * pair + 2, :]
 
-        def to_plane_order(dst, src, run):
-            nc.gpsimd.tensor_copy(
-                dst.rearrange("p (t g j) -> p t g j", t=PACK, j=run), src.rearrange("p (g t j) -> p t g j", t=PACK, j=run)
-            )
+        def round_w2(pair, ms):
+            src = w2_raw[:].rearrange("p u (m t) -> p m t u", t=PACK)[:, ms, 2 * pair : 2 * pair + 2, :]
+            if pair == 0:
+                nc.scalar.copy(w2_bf[0][:].rearrange("p (t m) u -> p m t u", t=2)[:, ms, :, :], src)
+            else:
+                nc.gpsimd.tensor_scalar(w2_bf[-1][:].rearrange("p (t m) u -> p m t u", t=2), src, 1.0, 0.0, MULT, ADD)
 
         head, rest = HEAD_REST
-        to_plane_order(w1_codes[:], w1_codes_raw[:], RUN)
-        to_plane_order(w1_scale[:].bitcast(I32), w1_scale_raw[:].bitcast(I32), RUN // 4)
+        nc.gpsimd.tensor_copy(w1_codes[0][:].rearrange("p (t m) -> p t m", t=2), pair_of(w1_codes_raw[:], 0))
+        for pair, rows in enumerate(PAIRS):
+            nc.gpsimd.tensor_copy(w1_scale[:, rows].rearrange("p (t m) -> p t m", t=2), pair_of(w1_scale_raw[:], pair))
+        nc.gpsimd.tensor_copy(w1_codes[1][:].rearrange("p (t m) -> p t m", t=2), pair_of(w1_codes_raw[:], 1))
         turn_gate(0)
         nc.vector.tensor_copy(x_scale[:], tok_scales[:].indirect(lists[0][:]))
         for c, cols in enumerate(HEAD_REST):
@@ -287,17 +286,20 @@ def tile_moe_mod_none_kernel(
             turn_back(0, 1, cols, bank)
         scatter(0, 1, rest)
         late_planes(0)
+        staged_middle = relay_tile("staged_middle", [P, MIDDLE_REST.start], F32, 0)
         for cols, bank in zip(MIDDLE_CUTS, turn_banks):
-            turn_sum([before[LAST]], cols, bank)
+            turn_sum([before[LAST]], cols, bank, staged_middle)
         for cols, bank in zip(MIDDLE_CUTS, product_banks):
-            turn_again(cols, bank)
-        w2_bf = []
+            turn_again(staged_middle, cols, bank)
+        w2_bf = [relay_tile("w2_bf0", [P, K // 2, PACK], BF16, 3 * T)]
         for t in range(PACK):
             if t >= 2:
                 scatter(0, t, WHOLE[0])
             if t < 2:
                 stream_bf = relay_tile("stream_bf%d" % t, [P, T], BF16, t * T)
-                for cols in ADD_CUTS[t]:
+                for c, cols in enumerate(ADD_CUTS[t]):
+                    if t == 0:
+                        round_w2(0, cuts(0, P // 2, P)[c])
                     nc.gpsimd.tensor_tensor(stream[t][:, cols], before[t][:, cols], spread[0][t][:, cols], ADD)
                     nc.scalar.copy(stream_bf[:, cols], stream[t][:, cols])
             if t == 2:
@@ -305,13 +307,11 @@ def tile_moe_mod_none_kernel(
                 nc.gpsimd.tensor_tensor(stream_bf[:], before[t][:], spread[0][t][:], ADD)
             if t == 1:
                 turn_gate(1)
-            for c in ((), (0, 1), (2,), ())[t]:
-                shape = [P, width(W2_CUTS[c]), PACK]
-                if c == 1:
-                    w2_bf.append(sbuf("w2_bf1", shape, BF16, tag="spread0_1"))
-                else:
-                    w2_bf.append(relay_tile("w2_bf%d" % c, shape, BF16, (0, None, PLANE2_AT + 3 * T)[c]))
-                round_w2(w2_bf[c], W2_CUTS[c])
+                w2_bf.append(sbuf("w2_bf1", [P, P, PACK], BF16, tag="spread0_1"))
+                round_w2(1, slice(0, P // 2))
+            if t == 2:
+                w2_bf.append(relay_tile("w2_bf2", [P, P, PACK], BF16, PLANE2_AT + 3 * T))
+                round_w2(1, slice(P // 2, P))
             if t < LAST:
                 nc.scalar.activation(r_bf[:, :, t], stream_bf[:].indirect(lists[1][:]), COPY)
         spread[1][0] = sbuf("spread1_0", [P, T], F32, tag="before0")
@@ -324,12 +324,17 @@ def tile_moe_mod_none_kernel(
         for cols, bank in zip(MIDDLE_CUTS, product_banks):
             nc.vector.tensor_tensor(last_bf[:, cols], bank[:, 0 : width(cols)], spread[0][0][:, cols], ADD)
         nc.gpsimd.tensor_tensor(last_bf[:, MIDDLE_REST], before[LAST][:, MIDDLE_REST], spread[0][0][:, MIDDLE_REST], ADD)
-        w_codes.append(relay_tile("w2_codes", [P, K], I32, PLANE2_AT + 2 * T))
-        for tile, cols in zip(w2_bf, W2_CUTS):
+        w2_codes.append(relay_tile("w2_codes", [P, K], I32, PLANE2_AT + 2 * T))
+        runs = [(w2_bf[0][:], PAIRS[0])]
+        for half in range(2):
+            for t in range(2):
+                at = (2 + t) * P + half * P // 2
+                runs.append((w2_bf[1 + half][:, t * P // 2 : (t + 1) * P // 2, :], slice(at, at + P // 2)))
+        for part, cols in runs:
             nc.vector.quantize_mx(
-                out=w_codes[1][:, cols].bitcast(FP8X4),
+                out=w2_codes[0][:, cols].bitcast(FP8X4),
                 scales=w2_scale[:, cols],
-                in_=tile[:].rearrange("p n j -> p (n j)"),
+                in_=part.rearrange("p n j -> p (n j)"),
             )
 
         first, rest = FIRST_REST
@@ -356,17 +361,17 @@ def tile_moe_mod_none_kernel(
         late_planes(1)
         r2 = sbuf("r2", [P, T], F32, tag="tok_words")
         for g, cols in enumerate(BANK_CUTS):
-            turn_sum([again2, spread[0][2]], cols, product_banks[(g + 1) % 3])
+            turn_sum([again2, spread[0][2]], cols, product_banks[(g + 1) % 3], staged)
         for g, cols in enumerate(BANK_CUTS):
-            turn_again(cols, turn_banks[g % 3])
+            turn_again(staged, cols, turn_banks[g % 3])
             nc.scalar.copy(r2[:, cols], turn_banks[g % 3][:])
         for g, cols in enumerate(BANK_CUTS):
-            turn_sum([before[LAST], spread[0][0]], cols, turn_banks[(g + 1) % 3])
+            turn_sum([before[LAST], spread[0][0]], cols, turn_banks[(g + 1) % 3], staged)
         for cols, bank in zip(BANK_CUTS[0:3], product_banks):
-            turn_again(cols, bank)
+            turn_again(staged, cols, bank)
         r_last = [sbuf("r_last%d" % c, [P, width(cols)], F32) for c, cols in enumerate(CLOSING_GPSIMD)]
         for cols, bank, tile in zip(CLOSING_GPSIMD, direct_banks, r_last):
-            turn_again(cols, bank)
+            turn_again(staged, cols, bank)
             nc.scalar.copy(tile[:], bank[:, 0 : width(cols)])
         for t in range(PACK):
             if t >= 2:
@@ -377,7 +382,7 @@ def tile_moe_mod_none_kernel(
             if t == 2:
                 for cols in PLANE2_CUTS:
                     nc.gpsimd.tensor_tensor(r2[:, cols], r2[:, cols], spread[1][t][:, cols], ADD)
-                    nc.sync.dma_start(plane(out, t)[:, :, cols], r2[:, cols])
+                    nc.sync.dma_start(plane(out, t)[:, cols], r2[:, cols])
         result = relay_tile("result", [P, CLOSING_VECTOR[-1].stop], F32, PLANE1_AT)
         for cols in CLOSING_VECTOR:
             g = cols.start // BANK
@@ -387,7 +392,7 @@ def tile_moe_mod_none_kernel(
                 spread[1][0][:, cols],
                 ADD,
             )
-            nc.sync.dma_start(plane(out, LAST)[:, :, cols], result[:, cols])
+            nc.sync.dma_start(plane(out, LAST)[:, cols], result[:, cols])
         for cols, tile in zip(CLOSING_GPSIMD, r_last):
             nc.gpsimd.tensor_tensor(tile[:], tile[:], spread[1][0][:, cols], ADD)
-            nc.scalar.dma_start(plane(out, LAST)[:, :, cols], tile[:])
+            nc.scalar.dma_start(plane(out, LAST)[:, cols], tile[:])

@@ -1,7 +1,6 @@
 from contextlib import ExitStack
 
 import concourse.mybir as mybir
-from concourse.masks import make_identity
 
 K, T, S = 512, 2048, 1024
 FLOPS = 2 * 2 * K * K * S
@@ -19,34 +18,22 @@ MULT = mybir.AluOpType.mult
 
 P = 128
 PACK = 4
-LAST = PACK - 1
 GROUP = 16
 QUADRANTS = 4
-BLOCKS = S // P
 BANK = 512
-PLANE_BYTES = T * 4
-PLANE2_AT = BLOCKS * LAST * P * 4
-PLANE1_AT = PLANE2_AT + PLANE_BYTES
-W1_AT = PLANE1_AT + PLANE_BYTES
+BANKS = 8
 
 
 def cuts(*bounds):
     return [slice(a, b) for a, b in zip(bounds, bounds[1:])]
 
 
+PIECES = cuts(0, 256, 640, S)
 HALVES = cuts(0, S // 2, S)
-WHOLE = cuts(0, S)
-HEAD_REST = cuts(0, 3 * P, S)
-PIECES = cuts(0, S // 4, S // 2, S)
-FIRST_REST = cuts(0, S // 4, S)
-MIDDLE_CUTS = cuts(0, 512, 1024, 1408)
-MIDDLE_REST = slice(1408, T)
-PAIRS = cuts(0, K // 2, K)
-ADD_CUTS = [cuts(0, T // 2, T), cuts(0, 1024, 1792, T)]
-BANK_CUTS = cuts(0, 512, 1024, 1536, T)
-PLANE2_CUTS = cuts(0, 1024, 1536, T)
-CLOSING_VECTOR = cuts(0, 256, 512, 1024, 1536)
-CLOSING_GPSIMD = cuts(1536, 1792, T)
+WHOLE = slice(0, S)
+QUARTERS = cuts(0, 512, 1024, 1536, T)
+SHARED_ADD = 1280
+A, B, C, D = range(PACK)
 
 
 def tile_moe_mod_none_kernel(
@@ -55,21 +42,13 @@ def tile_moe_mod_none_kernel(
     nc = tc.nc
     with ExitStack() as ctx:
         keep = ctx.enter_context(tc.tile_pool(name="keep", bufs=1))
-        relay = ctx.enter_context(tc.tile_pool(name="relay", bufs=1))
-        psum = ctx.enter_context(tc.psum_pool(name="psum", bufs=1))
+        psum = ctx.enter_context(tc.psum_pool(name="psum", bufs=BANKS))
 
         def sbuf(name, shape, dtype, tag=None):
             return keep.tile(shape, dtype, name=name, tag=tag or name, align_bytes=64)
 
-        def relay_tile(name, shape, dtype, offset):
-            return relay.tile(shape, dtype, name=name, offset=offset, align_bytes=64)
-
         def width(cols):
             return cols.stop - cols.start
-
-        def within(pieces, tiles, cols):
-            c = max(i for i, piece in enumerate(pieces) if piece.start <= cols.start)
-            return tiles[c][:, cols.start - pieces[c].start : cols.stop - pieces[c].start]
 
         def entries(lst, cols):
             return lst[:, cols.start // GROUP : cols.stop // GROUP]
@@ -81,318 +60,161 @@ def tile_moe_mod_none_kernel(
         tok_words = sbuf("tok_words", [P, T], I32)
         tok_scales = sbuf("tok_scales", [P, T], U8)
         w1_codes_raw = sbuf("w1_codes_raw", [P, K], I32)
-        w1_scale_raw = relay_tile("w1_scale_raw", [P, K], U8, W1_AT)
-        w1_codes = [sbuf("w1_codes0", [P, K // 2], I32), relay_tile("w1_codes1", [P, K // 2], I32, W1_AT)]
-        w1_scale = sbuf("w1_scale", [P, K], U8)
-        gate1_head = sbuf("gate1_head", [P, width(HEAD_REST[0])], F32)
-        gate1_rest = sbuf("gate1_rest", [P, width(HEAD_REST[1])], F32)
-        gate_first = sbuf("gate_first", [P, width(PIECES[0])], F32)
-        gate2_all = sbuf("gate2_all", [P, S], F32)
-        gate_rows = [sbuf("gate_rows%d" % layer, [P, P], F32) for layer in range(2)]
-        gate_cols = [sbuf("gate_cols0", [P, BLOCKS], F32), relay_tile("gate_cols1", [P, BLOCKS], F32, T // 2)]
-        ident = sbuf("ident", [P, P], F32)
+        w1_scale_raw = sbuf("w1_scale_raw", [P, K], U8)
+        w_codes = [sbuf("w%d_codes" % layer, [P, K], I32) for layer in (1, 2)]
+        w_scale = [sbuf("w%d_scale" % layer, [P, K], U8) for layer in (1, 2)]
+        slot_codes = [sbuf("slot_codes%d" % layer, [P, S], U32) for layer in range(2)]
+        slot_scale = [sbuf("slot_scale%d" % layer, [P, S], U8) for layer in range(2)]
+        gates = [sbuf("gate%d" % layer, [P, S], F32) for layer in (1, 2)]
         w2_raw = sbuf("w2_raw", [P, PACK, K], F32)
-        w2_scale = sbuf("w2_scale", [P, K], U8)
-        before = [
-            sbuf("before0", [P, T], F32),
-            relay_tile("before1", [P, T], F32, PLANE1_AT),
-            relay_tile("before2", [P, T], F32, PLANE2_AT),
-            sbuf("before3", [P, T], F32),
-        ]
-        stream = [sbuf("stream%d" % t, [P, T], F32) for t in range(2)]
-        x_codes = [sbuf("x_codes%d" % c, [P, width(cols)], U32) for c, cols in enumerate(HEAD_REST)]
-        x_scale = sbuf("x_scale", [P, S], U8)
-        staged = sbuf("staged", [P, T], F32)
-        r_bf = sbuf("r_bf", [P, S, PACK], BF16)
-        r_scale = sbuf("r_scale", [P, S], U8)
-        turned = [relay_tile("turned0", [P, BLOCKS, LAST, P], F32, 0), sbuf("turned1", [P, BLOCKS, LAST, P], F32)]
-        pieces = [[HEAD_REST, HEAD_REST, WHOLE, WHOLE], [FIRST_REST, HALVES, WHOLE, WHOLE]]
-        sums = [
-            [
-                [sbuf("sums%d_%d_%d" % (layer, t, c), [P, width(cols)], F32) for c, cols in enumerate(pieces[layer][t])]
-                for t in range(PACK)
-            ]
-            for layer in range(2)
-        ]
+        w2_bf = sbuf("w2_bf", [P, K, PACK], BF16)
+        stream = [sbuf("stream%d" % t, [P, T], F32) for t in range(PACK)]
+        spread = {t: sbuf("spread%d" % t, [P, T], F32) for t in (A, B, C)}
+        spread[D] = spread[A]
+        sums = [[sbuf("sums%d_%d" % (layer, t), [P, S], F32) for t in range(PACK)] for layer in range(2)]
+        picked = [sbuf("picked%d" % c, [P, PACK, width(cols)], F32) for c, cols in enumerate(PIECES)]
+        picked_bf = [sbuf("picked_bf%d" % c, [P, width(cols), PACK], BF16) for c, cols in enumerate(PIECES)]
 
-        def sums_at(layer, t, cols):
-            return within(pieces[layer][t], sums[layer][t], cols)
-
-        direct_banks = [psum.tile([P, BANK], F32, name="direct%d" % i) for i in range(2)]
-        product_banks = [psum.tile([P, BANK], F32, name="product%d" % i) for i in range(3)]
-        turn_banks = [psum.tile([P, BANK], F32, name="turn%d" % i) for i in range(3)]
-
-        spread = [[sbuf("spread0_%d" % i, [P, T], F32) for i in range(LAST)], [None, sbuf("spread1_1", [P, T], F32)]]
         nc.gpsimd.memset(tok_scales[:].bitcast(I32), 0)
         nc.vector.memset(w1_scale_raw[:].bitcast(I32), 0)
-        make_identity(nc, ident[:])
-        nc.vector.memset(spread[0][0][:], 0.0)
-        nc.gpsimd.memset(w2_scale[:].bitcast(I32), 0)
-        nc.gpsimd.tensor_scalar(spread[1][1][:], spread[0][0][:], 1.0, 0.0, MULT, ADD)
+        nc.vector.memset(spread[A][:], 0.0)
+        nc.vector.memset(spread[C][:], 0.0)
+        nc.scalar.copy(spread[B][:], spread[A][:])
 
-        def load_scales(queue, tile, scales, quadrants):
-            for q in quadrants:
-                queue.dma_start(
+        def load_scales(tile, scales):
+            for q in range(QUADRANTS):
+                nc.sync.dma_start(
                     tile[32 * q : 32 * q + 4, :].bitcast(I32), scales[0, 4 * q : 4 * q + 4, :].bitcast(I32)
                 )
 
-        def load_gate_rows(layer, gate):
-            nc.sync.dma_start(gate_rows[layer][:], gate.rearrange("p (b s) -> (p b) s", s=P)[0:P, :])
-
         nc.sync.dma_start(lists[0][:], offs)
         nc.sync.dma_start(w1_codes_raw[:], w1_words[0].rearrange("p i d -> p (i d)").bitcast(I32))
-        load_scales(nc.sync, tok_scales, x_scales, (0, 1, 2))
-        load_scales(nc.scalar, tok_scales, x_scales, (3,))
+        load_scales(tok_scales, x_scales)
         nc.sync.dma_start(tok_words[:], x_words[0].rearrange("p t d -> p (t d)").bitcast(I32))
-        load_scales(nc.sync, w1_scale_raw, w1_scales, range(QUADRANTS))
-        load_gate_rows(0, gate1)
-        for tile in spread[0][1:]:
-            nc.scalar.copy(tile[:], spread[0][0][:])
-        nc.sync.dma_start(gate1_head[:], gate1[:, HEAD_REST[0]])
-        nc.sync.dma_start(gate1_rest[:], gate1[:, HEAD_REST[1]])
-        nc.sync.dma_start(lists[1][:], offs2)
-        load_gate_rows(1, gate2)
-        for t in (0, LAST):
-            nc.sync.dma_start(before[t][:], plane(xr, t))
+        load_scales(w1_scale_raw, w1_scales)
+        for cols in cuts(0, 256, S):
+            nc.sync.dma_start(gates[0][:, cols], gate1[:, cols])
         nc.sync.dma_start(w2_raw[:], w2.rearrange("(p u) n -> p u n", u=PACK))
-        for t in (1, 2):
-            nc.sync.dma_start(before[t][:], plane(xr, t))
-        nc.sync.dma_start(gate_first[:], gate2[:, PIECES[0]])
-        nc.sync.dma_start(gate2_all[:], gate2)
+        nc.sync.dma_start(lists[1][:], offs2)
+        for t in (A, C, B, D):
+            nc.sync.dma_start(stream[t][:], plane(xr, t))
+        nc.sync.dma_start(gates[1][:], gate2)
 
-        def turn_gate(layer):
-            nc.tensor.transpose(turn_banks[-1][:, 0:P], gate_rows[layer][:], ident[:])
-            nc.scalar.activation(gate_cols[layer][:], turn_banks[-1][:, 0:BLOCKS], COPY)
-
-        r_codes = []
-        w2_codes = []
-        w_scale = [w1_scale, w2_scale]
-        slot_scale = [x_scale, r_scale]
-
-        def slot_codes(layer, cols):
-            return within(HEAD_REST, x_codes, cols) if layer == 0 else within(PIECES, r_codes, cols)
-
-        def weight_codes(layer, rows):
-            return within(PAIRS, w1_codes, rows) if layer == 0 else w2_codes[0][:, rows]
-
-        def mx(bank, lhs_codes, lhs_scale, rhs_codes, rhs_scale):
-            nc.tensor.matmul_mx(
-                out=bank,
-                lhsT=lhs_codes.bitcast(FP8X4),
-                lhsT_scale=lhs_scale,
-                rhs=rhs_codes.bitcast(FP8X4),
-                rhs_scale=rhs_scale,
-                start=True,
-                stop=True,
-            )
-
-        def direct(layer, t, bank, passes):
+        def gated_sums(layer, t, cols):
+            bank = psum.tile([P, BANK], F32, name="bank")
             rows = slice(t * P, (t + 1) * P)
-            for run in passes:
-                part = bank[:, run.start - passes[0].start : run.stop - passes[0].start]
-                mx(part, weight_codes(layer, rows), w_scale[layer][:, rows], slot_codes(layer, run), slot_scale[layer][:, run])
-
-        def direct_sums(layer, t, bank, passes):
-            direct(layer, t, bank, passes)
-            cols = slice(passes[0].start, passes[-1].stop)
-            nc.scalar.copy(sums_at(layer, t, cols), bank[:, 0 : width(cols)])
-
-        def scatter_gated(layer, t, cols, gate):
-            nc.vector.tensor_tensor(
-                spread[layer][t % LAST][:].indirect(entries(lists[layer], cols)), sums_at(layer, t, cols), gate, MULT
-            )
-
-        def scatter(layer, t, cols):
-            nc.vector.tensor_copy(spread[layer][t % LAST][:].indirect(entries(lists[layer], cols)), sums_at(layer, t, cols))
-
-        def products(layer, planes, blocks, bank):
-            n = width(planes) * P
-            rows = slice(planes.start * P, planes.stop * P)
-            for i, b in enumerate(blocks):
-                cols = slice(b * P, (b + 1) * P)
-                mx(
-                    bank[:, i * n : (i + 1) * n],
-                    slot_codes(layer, cols),
-                    slot_scale[layer][:, cols],
-                    weight_codes(layer, rows),
-                    w_scale[layer][:, rows],
+            at = cols.start
+            while at < cols.stop:
+                n = max(n for n in (128, 256, 512) if at + n <= cols.stop)
+                nc.tensor.matmul_mx(
+                    out=bank[:, at - cols.start : at - cols.start + n],
+                    lhsT=w_codes[layer][:, rows].bitcast(FP8X4),
+                    lhsT_scale=w_scale[layer][:, rows],
+                    rhs=slot_codes[layer][:, at : at + n].bitcast(FP8X4),
+                    rhs_scale=slot_scale[layer][:, at : at + n],
+                    start=True,
+                    stop=True,
                 )
-            for i, b in enumerate(blocks):
-                nc.scalar.activation(
-                    turned[layer][:, b, planes.start - 1 : planes.stop - 1, :].rearrange("s t m -> s (t m)"),
-                    bank[:, i * n : (i + 1) * n],
-                    COPY,
-                    scale=gate_cols[layer][:, b : b + 1],
+                at = at + n
+            nc.vector.tensor_tensor(sums[layer][t][:, cols], bank[:, 0 : width(cols)], gates[layer][:, cols], MULT)
+
+        def scatter_scalar(layer, window, t, cols):
+            nc.scalar.activation(window[:].indirect(entries(lists[layer], cols)), sums[layer][t][:, cols], COPY)
+
+        def scatter_vector(layer, window, t, cols):
+            nc.vector.tensor_copy(window[:].indirect(entries(lists[layer], cols)), sums[layer][t][:, cols])
+
+        def gather_scalar(t, c):
+            nc.scalar.activation(picked[c][:, t, :], stream[t][:].indirect(entries(lists[1], PIECES[c])), COPY)
+
+        def gather_vector(t, c):
+            nc.vector.tensor_copy(picked[c][:, t, :], stream[t][:].indirect(entries(lists[1], PIECES[c])))
+
+        for planes in cuts(0, 1, PACK):
+            for tile, raw in ((w_codes[0], w1_codes_raw), (w_scale[0], w1_scale_raw)):
+                nc.gpsimd.tensor_copy(
+                    tile[:].rearrange("p (t m) -> p t m", t=PACK)[:, planes, :],
+                    raw[:].rearrange("p (m t) -> p t m", t=PACK)[:, planes, :],
                 )
-
-        def turn_back(layer, t, cols, bank):
-            for c in range(cols.start, cols.stop, P):
-                nc.tensor.transpose(
-                    bank[:, c - cols.start : c - cols.start + P], turned[layer][:, c // P, t - 1, :], ident[:]
-                )
-            nc.scalar.copy(sums_at(layer, t, cols), bank[:, 0 : width(cols)])
-
-        def late_planes(layer):
-            for pair in range(BLOCKS // 2):
-                products(layer, slice(2, PACK), [2 * pair, 2 * pair + 1], product_banks[pair % 3])
-            for i, (t, cols) in enumerate([(t, cols) for t in (2, LAST) for cols in HALVES]):
-                turn_back(layer, t, cols, turn_banks[(i + 2) % 3])
-
-        def turn_sum(terms, cols, bank, staged):
-            for c in range(cols.start, cols.stop, P):
-                for i, term in enumerate(terms):
-                    nc.tensor.matmul(
-                        bank[:, c - cols.start : c - cols.start + P],
-                        term[:, c : c + P],
-                        ident[:],
-                        start=i == 0,
-                        stop=i == len(terms) - 1,
-                        is_transpose=True,
-                    )
-            nc.scalar.copy(staged[:, cols], bank[:, 0 : width(cols)])
-
-        def turn_again(staged, cols, bank):
-            for c in range(cols.start, cols.stop, P):
-                nc.tensor.transpose(bank[:, c - cols.start : c - cols.start + P], staged[:, c : c + P], ident[:])
-
-        def pair_of(src, pair):
-            return src.rearrange("p (m t) -> p t m", t=PACK)[:, 2 * pair : 2 * pair + 2, :]
-
-        def round_w2(pair, ms):
-            src = w2_raw[:].rearrange("p u (m t) -> p m t u", t=PACK)[:, ms, 2 * pair : 2 * pair + 2, :]
-            if pair == 0:
-                nc.scalar.copy(w2_bf[0][:].rearrange("p (t m) u -> p m t u", t=2)[:, ms, :, :], src)
-            else:
-                nc.gpsimd.tensor_scalar(w2_bf[-1][:].rearrange("p (t m) u -> p m t u", t=2), src, 1.0, 0.0, MULT, ADD)
-
-        head, rest = HEAD_REST
-        nc.gpsimd.tensor_copy(w1_codes[0][:].rearrange("p (t m) -> p t m", t=2), pair_of(w1_codes_raw[:], 0))
-        for pair, rows in enumerate(PAIRS):
-            nc.gpsimd.tensor_copy(w1_scale[:, rows].rearrange("p (t m) -> p t m", t=2), pair_of(w1_scale_raw[:], pair))
-        nc.gpsimd.tensor_copy(w1_codes[1][:].rearrange("p (t m) -> p t m", t=2), pair_of(w1_codes_raw[:], 1))
-        turn_gate(0)
-        nc.vector.tensor_copy(x_scale[:], tok_scales[:].indirect(lists[0][:]))
-        for c, cols in enumerate(HEAD_REST):
-            nc.vector.tensor_copy(x_codes[c][:], tok_words[:].bitcast(U32).indirect(entries(lists[0], cols)))
-        for t, bank in ((0, product_banks[0]), (1, direct_banks[0])):
-            direct_sums(0, t, bank, cuts(0, 2 * P, 3 * P))
-            scatter_gated(0, t, head, gate1_head[:])
-        for run, bank in zip(cuts(3 * P, 7 * P, S), product_banks[1:]):
-            direct_sums(0, 0, bank, [run])
-        scatter_gated(0, 0, rest, gate1_rest[:])
-        products(0, slice(1, 2), range(3, 7), direct_banks[1])
-        products(0, slice(1, 2), range(7, BLOCKS), direct_banks[0])
-        for cols, bank in zip(cuts(3 * P, 7 * P, S), turn_banks):
-            turn_back(0, 1, cols, bank)
-        scatter(0, 1, rest)
-        late_planes(0)
-        staged_middle = relay_tile("staged_middle", [P, MIDDLE_REST.start], F32, 0)
-        for cols, bank in zip(MIDDLE_CUTS, turn_banks):
-            turn_sum([before[LAST]], cols, bank, staged_middle)
-        for cols, bank in zip(MIDDLE_CUTS, product_banks):
-            turn_again(staged_middle, cols, bank)
-        w2_bf = [relay_tile("w2_bf0", [P, K // 2, PACK], BF16, 3 * T)]
-        for t in range(PACK):
-            if t >= 2:
-                scatter(0, t, WHOLE[0])
-            if t < 2:
-                stream_bf = relay_tile("stream_bf%d" % t, [P, T], BF16, t * T)
-                for c, cols in enumerate(ADD_CUTS[t]):
-                    if t == 0:
-                        round_w2(0, cuts(0, P // 2, P)[c])
-                    nc.gpsimd.tensor_tensor(stream[t][:, cols], before[t][:, cols], spread[0][t][:, cols], ADD)
-                    nc.scalar.copy(stream_bf[:, cols], stream[t][:, cols])
-            if t == 2:
-                stream_bf = sbuf("stream_bf2", [P, T], BF16)
-                nc.gpsimd.tensor_tensor(stream_bf[:], before[t][:], spread[0][t][:], ADD)
-            if t == 1:
-                turn_gate(1)
-                w2_bf.append(sbuf("w2_bf1", [P, P, PACK], BF16, tag="spread0_1"))
-                round_w2(1, slice(0, P // 2))
-            if t == 2:
-                w2_bf.append(relay_tile("w2_bf2", [P, P, PACK], BF16, PLANE2_AT + 3 * T))
-                round_w2(1, slice(P // 2, P))
-            if t < LAST:
-                nc.scalar.activation(r_bf[:, :, t], stream_bf[:].indirect(lists[1][:]), COPY)
-        spread[1][0] = sbuf("spread1_0", [P, T], F32, tag="before0")
-        spread[1].append(relay_tile("spread1_2", [P, T], F32, PLANE1_AT))
-        for tile in (spread[1][0], spread[1][2]):
-            nc.sync.dma_start(tile[:], spread[1][1][:])
-        again2 = sbuf("again2", [P, T], F32, tag="w2_raw")
-        nc.sync.dma_start(again2[:], plane(xr, 2))
-        last_bf = relay_tile("last_bf", [P, T], BF16, PLANE2_AT)
-        for cols, bank in zip(MIDDLE_CUTS, product_banks):
-            nc.vector.tensor_tensor(last_bf[:, cols], bank[:, 0 : width(cols)], spread[0][0][:, cols], ADD)
-        nc.gpsimd.tensor_tensor(last_bf[:, MIDDLE_REST], before[LAST][:, MIDDLE_REST], spread[0][0][:, MIDDLE_REST], ADD)
-        w2_codes.append(relay_tile("w2_codes", [P, K], I32, PLANE2_AT + 2 * T))
-        runs = [(w2_bf[0][:], PAIRS[0])]
-        for half in range(2):
-            for t in range(2):
-                at = (2 + t) * P + half * P // 2
-                runs.append((w2_bf[1 + half][:, t * P // 2 : (t + 1) * P // 2, :], slice(at, at + P // 2)))
-        for part, cols in runs:
-            nc.vector.quantize_mx(
-                out=w2_codes[0][:, cols].bitcast(FP8X4),
-                scales=w2_scale[:, cols],
-                in_=part.rearrange("p n j -> p (n j)"),
-            )
-
-        first, rest = FIRST_REST
-        for c, cols in enumerate(PIECES):
-            nc.scalar.activation(r_bf[:, cols, LAST], last_bf[:].indirect(entries(lists[1], cols)), COPY)
-            r_codes.append(sbuf("r_codes%d" % c, [P, width(cols)], U32, tag="gate_first" if c == 2 else None))
-            nc.vector.quantize_mx(
-                out=r_codes[c][:].bitcast(FP8X4),
-                scales=r_scale[:, cols],
-                in_=r_bf[:, cols, :].rearrange("p s j -> p (s j)"),
-            )
-            if c == 0:
-                direct(1, 0, direct_banks[0], [cols])
-                nc.vector.tensor_tensor(sums_at(1, 0, cols), direct_banks[0][:, cols], gate_first[:], MULT)
-                scatter(1, 0, cols)
-        direct_sums(1, 1, direct_banks[1], PIECES[0:2])
-        scatter_gated(1, 1, HALVES[0], gate2_all[:, HALVES[0]])
-        for run, bank in zip(PIECES[1:], product_banks):
-            direct_sums(1, 0, bank, [run])
-        scatter_gated(1, 0, rest, gate2_all[:, rest])
-        products(1, slice(1, 2), range(BLOCKS // 2, BLOCKS), product_banks[2])
-        turn_back(1, 1, HALVES[1], turn_banks[1])
-        scatter(1, 1, HALVES[1])
-        late_planes(1)
-        r2 = sbuf("r2", [P, T], F32, tag="tok_words")
-        for g, cols in enumerate(BANK_CUTS):
-            turn_sum([again2, spread[0][2]], cols, product_banks[(g + 1) % 3], staged)
-        for g, cols in enumerate(BANK_CUTS):
-            turn_again(staged, cols, turn_banks[g % 3])
-            nc.scalar.copy(r2[:, cols], turn_banks[g % 3][:])
-        for g, cols in enumerate(BANK_CUTS):
-            turn_sum([before[LAST], spread[0][0]], cols, turn_banks[(g + 1) % 3], staged)
-        for cols, bank in zip(BANK_CUTS[0:3], product_banks):
-            turn_again(staged, cols, bank)
-        r_last = [sbuf("r_last%d" % c, [P, width(cols)], F32) for c, cols in enumerate(CLOSING_GPSIMD)]
-        for cols, bank, tile in zip(CLOSING_GPSIMD, direct_banks, r_last):
-            turn_again(staged, cols, bank)
-            nc.scalar.copy(tile[:], bank[:, 0 : width(cols)])
-        for t in range(PACK):
-            if t >= 2:
-                scatter(1, t, WHOLE[0])
-            if t < 2:
-                nc.gpsimd.tensor_tensor(stream[t][:], stream[t][:], spread[1][t][:], ADD)
-                nc.sync.dma_start(plane(out, t), stream[t][:])
-            if t == 2:
-                for cols in PLANE2_CUTS:
-                    nc.gpsimd.tensor_tensor(r2[:, cols], r2[:, cols], spread[1][t][:, cols], ADD)
-                    nc.sync.dma_start(plane(out, t)[:, cols], r2[:, cols])
-        result = relay_tile("result", [P, CLOSING_VECTOR[-1].stop], F32, PLANE1_AT)
-        for cols in CLOSING_VECTOR:
-            g = cols.start // BANK
-            nc.vector.tensor_tensor(
-                result[:, cols],
-                product_banks[g][:, cols.start - g * BANK : cols.stop - g * BANK],
-                spread[1][0][:, cols],
+        nc.vector.tensor_copy(slot_scale[0][:], tok_scales[:].indirect(lists[0][:]))
+        for cols in PIECES:
+            nc.vector.tensor_copy(slot_codes[0][:, cols], tok_words[:].bitcast(U32).indirect(entries(lists[0], cols)))
+            gated_sums(0, A, cols)
+            scatter_scalar(0, spread[A], A, cols)
+        for ms in cuts(0, P // 2, P):
+            nc.gpsimd.tensor_scalar(
+                w2_bf[:].rearrange("p (t m) u -> p m t u", t=PACK)[:, ms, :, :],
+                w2_raw[:].rearrange("p u (m t) -> p m t u", t=PACK)[:, ms, :, :],
+                1.0,
+                0.0,
+                MULT,
                 ADD,
             )
-            nc.sync.dma_start(plane(out, LAST)[:, cols], result[:, cols])
-        for cols, tile in zip(CLOSING_GPSIMD, r_last):
-            nc.gpsimd.tensor_tensor(tile[:], tile[:], spread[1][0][:, cols], ADD)
-            nc.scalar.dma_start(plane(out, LAST)[:, cols], tile[:])
+        for t in (C, B):
+            for cols in HALVES:
+                gated_sums(0, t, cols)
+        scatter_vector(0, spread[C], C, WHOLE)
+        for cols in PIECES:
+            scatter_scalar(0, spread[B], B, cols)
+        for t in (A, C):
+            for cols in QUARTERS:
+                nc.gpsimd.tensor_tensor(stream[t][:, cols], stream[t][:, cols], spread[t][:, cols], ADD)
+        nc.vector.quantize_mx(
+            out=w_codes[1][:].bitcast(FP8X4), scales=w_scale[1][:], in_=w2_bf[:].rearrange("p n u -> p (n u)")
+        )
+        for cols in HALVES:
+            gated_sums(0, D, cols)
+        for cols in PIECES:
+            scatter_scalar(0, spread[D], D, cols)
+        for c in range(len(PIECES)):
+            gather_vector(A, c)
+        cols = slice(0, SHARED_ADD)
+        nc.vector.tensor_tensor(stream[B][:, cols], stream[B][:, cols], spread[B][:, cols], ADD)
+        cols = slice(SHARED_ADD, T)
+        nc.gpsimd.tensor_tensor(stream[B][:, cols], stream[B][:, cols], spread[B][:, cols], ADD)
+        for c in range(len(PIECES)):
+            gather_vector(C, c)
+        before = stream[D]
+        stream[D] = sbuf("stream_last", [P, T], F32, tag="spread%d" % C)
+        nc.vector.tensor_tensor(stream[D][:], before[:], spread[D][:], ADD)
+        for c in range(len(PIECES)):
+            gather_scalar(B, c)
+
+        def with_residual(t, c):
+            cols = PIECES[c]
+            nc.gpsimd.tensor_tensor(sums[1][t][:, cols], sums[1][t][:, cols], picked[c][:, t, :], ADD)
+
+        for c in range(len(PIECES)):
+            gather_scalar(D, c)
+        for c, cols in enumerate(PIECES):
+            nc.vector.tensor_copy(picked_bf[c][:], picked[c][:].rearrange("p t s -> p s t"))
+            nc.vector.quantize_mx(
+                out=slot_codes[1][:, cols].bitcast(FP8X4),
+                scales=slot_scale[1][:, cols],
+                in_=picked_bf[c][:].rearrange("p s t -> p (s t)"),
+            )
+            if c < 2:
+                for t in (A, D):
+                    gated_sums(1, t, cols)
+                    with_residual(t, c)
+                    scatter_scalar(1, stream[t], t, cols)
+        for cols in HALVES:
+            gated_sums(1, C, cols)
+        for c in range(len(PIECES)):
+            with_residual(C, c)
+        gated_sums(1, A, PIECES[2])
+        with_residual(A, 2)
+        scatter_scalar(1, stream[A], A, PIECES[2])
+        nc.sync.dma_start(plane(out, A), stream[A][:])
+        for cols in HALVES:
+            gated_sums(1, B, cols)
+        gated_sums(1, D, PIECES[2])
+        scatter_vector(1, stream[C], C, WHOLE)
+        nc.sync.dma_start(plane(out, C), stream[C][:])
+        with_residual(D, 2)
+        scatter_vector(1, stream[D], D, PIECES[2])
+        nc.sync.dma_start(plane(out, D), stream[D][:])
+        for c, cols in enumerate(PIECES):
+            with_residual(B, c)
+            scatter_scalar(1, stream[B], B, cols)
+        nc.sync.dma_start(plane(out, B), stream[B][:])

@@ -32,7 +32,6 @@ PIECES = cuts(0, 256, 640, S)
 HALVES = cuts(0, S // 2, S)
 WHOLE = slice(0, S)
 QUARTERS = cuts(0, 512, 1024, 1536, T)
-SHARED_ADD = 1280
 A, B, C, D = range(PACK)
 
 
@@ -42,6 +41,7 @@ def tile_moe_mod_none_kernel(
     nc = tc.nc
     with ExitStack() as ctx:
         keep = ctx.enter_context(tc.tile_pool(name="keep", bufs=1))
+        relay = ctx.enter_context(tc.tile_pool(name="relay", bufs=1))
         psum = ctx.enter_context(tc.psum_pool(name="psum", bufs=BANKS))
 
         def sbuf(name, shape, dtype, tag=None):
@@ -60,26 +60,38 @@ def tile_moe_mod_none_kernel(
         tok_words = sbuf("tok_words", [P, T], I32)
         tok_scales = sbuf("tok_scales", [P, T], U8)
         w1_codes_raw = sbuf("w1_codes_raw", [P, K], I32)
-        w1_scale_raw = sbuf("w1_scale_raw", [P, K], U8)
+        w1_scale_raw = relay.tile([P, K], U8, name="w1_scale_raw", offset=0, align_bytes=64)
         w_codes = [sbuf("w%d_codes" % layer, [P, K], I32) for layer in (1, 2)]
         w_scale = [sbuf("w%d_scale" % layer, [P, K], U8) for layer in (1, 2)]
-        slot_codes = [sbuf("slot_codes%d" % layer, [P, S], U32) for layer in range(2)]
+        code_runs = [cuts(0, PIECES[2].start, S), [WHOLE]]
+        slot_codes = [
+            [
+                sbuf("x_codes0", [P, width(code_runs[0][0])], U32),
+                relay.tile([P, width(code_runs[0][1])], U32, name="x_codes1", offset=0, align_bytes=64),
+            ],
+            [sbuf("r_codes", [P, S], U32)],
+        ]
+
+        def codes_at(layer, cols):
+            c = max(i for i, run in enumerate(code_runs[layer]) if run.start <= cols.start)
+            first = code_runs[layer][c].start
+            return slot_codes[layer][c][:, cols.start - first : cols.stop - first]
+
         slot_scale = [sbuf("slot_scale%d" % layer, [P, S], U8) for layer in range(2)]
         gates = [sbuf("gate%d" % layer, [P, S], F32) for layer in (1, 2)]
         w2_raw = sbuf("w2_raw", [P, PACK, K], F32)
         w2_bf = sbuf("w2_bf", [P, K, PACK], BF16)
         stream = [sbuf("stream%d" % t, [P, T], F32) for t in range(PACK)]
-        spread = {t: sbuf("spread%d" % t, [P, T], F32) for t in (A, B, C)}
-        spread[D] = spread[A]
+        spread = [sbuf("spread%d" % t, [P, T], F32) for t in range(PACK)]
         sums = [[sbuf("sums%d_%d" % (layer, t), [P, S], F32) for t in range(PACK)] for layer in range(2)]
-        picked = [sbuf("picked%d" % c, [P, PACK, width(cols)], F32) for c, cols in enumerate(PIECES)]
-        picked_bf = [sbuf("picked_bf%d" % c, [P, width(cols), PACK], BF16) for c, cols in enumerate(PIECES)]
+        picked = [sbuf("picked%d" % c, [P, PACK, width(cols)], F32) for c, cols in enumerate(PIECES[0:2])]
 
         nc.gpsimd.memset(tok_scales[:].bitcast(I32), 0)
         nc.vector.memset(w1_scale_raw[:].bitcast(I32), 0)
-        nc.vector.memset(spread[A][:], 0.0)
-        nc.vector.memset(spread[C][:], 0.0)
-        nc.scalar.copy(spread[B][:], spread[A][:])
+        nc.vector.memset(spread[A][:].bitcast(I32), 0)
+        nc.gpsimd.memset(spread[C][:].bitcast(I32), 0)
+        for t in (B, D):
+            nc.scalar.copy(spread[t][:], spread[A][:])
 
         def load_scales(tile, scales):
             for q in range(QUADRANTS):
@@ -92,10 +104,10 @@ def tile_moe_mod_none_kernel(
         load_scales(tok_scales, x_scales)
         nc.sync.dma_start(tok_words[:], x_words[0].rearrange("p t d -> p (t d)").bitcast(I32))
         load_scales(w1_scale_raw, w1_scales)
-        for cols in cuts(0, 256, S):
+        for cols in cuts(0, PIECES[0].stop, S):
             nc.sync.dma_start(gates[0][:, cols], gate1[:, cols])
-        nc.sync.dma_start(w2_raw[:], w2.rearrange("(p u) n -> p u n", u=PACK))
         nc.sync.dma_start(lists[1][:], offs2)
+        nc.sync.dma_start(w2_raw[:], w2.rearrange("(p u) n -> p u n", u=PACK))
         for t in (A, C, B, D):
             nc.sync.dma_start(stream[t][:], plane(xr, t))
         nc.sync.dma_start(gates[1][:], gate2)
@@ -105,12 +117,13 @@ def tile_moe_mod_none_kernel(
             rows = slice(t * P, (t + 1) * P)
             at = cols.start
             while at < cols.stop:
-                n = max(n for n in (128, 256, 512) if at + n <= cols.stop)
+                stop = min(run.stop for run in code_runs[layer] + [cols] if run.stop > at)
+                n = max(n for n in (128, 256, 512) if at + n <= stop)
                 nc.tensor.matmul_mx(
                     out=bank[:, at - cols.start : at - cols.start + n],
                     lhsT=w_codes[layer][:, rows].bitcast(FP8X4),
                     lhsT_scale=w_scale[layer][:, rows],
-                    rhs=slot_codes[layer][:, at : at + n].bitcast(FP8X4),
+                    rhs=codes_at(layer, slice(at, at + n)).bitcast(FP8X4),
                     rhs_scale=slot_scale[layer][:, at : at + n],
                     start=True,
                     stop=True,
@@ -137,8 +150,9 @@ def tile_moe_mod_none_kernel(
                     raw[:].rearrange("p (m t) -> p t m", t=PACK)[:, planes, :],
                 )
         nc.vector.tensor_copy(slot_scale[0][:], tok_scales[:].indirect(lists[0][:]))
-        for cols in PIECES:
-            nc.vector.tensor_copy(slot_codes[0][:, cols], tok_words[:].bitcast(U32).indirect(entries(lists[0], cols)))
+        for runs, cols in zip([PIECES[0:2], [], PIECES[2:]], PIECES):
+            for run in runs:
+                nc.vector.tensor_copy(codes_at(0, run), tok_words[:].bitcast(U32).indirect(entries(lists[0], run)))
             gated_sums(0, A, cols)
             scatter_scalar(0, spread[A], A, cols)
         for ms in cuts(0, P // 2, P):
@@ -150,71 +164,76 @@ def tile_moe_mod_none_kernel(
                 MULT,
                 ADD,
             )
-        for t in (C, B):
-            for cols in HALVES:
-                gated_sums(0, t, cols)
+        for t, cols in ((B, HALVES[1]), (D, HALVES[1]), (B, HALVES[0]), (C, HALVES[0]), (C, HALVES[1])):
+            gated_sums(0, t, cols)
         scatter_vector(0, spread[C], C, WHOLE)
-        for cols in PIECES:
-            scatter_scalar(0, spread[B], B, cols)
+        gated_sums(0, D, HALVES[0])
+        first, middle, fourth = cuts(0, 256, 768, S)
+        thirds = cuts(0, 384, 768, S)
+        for t, cols in ((B, fourth), (D, fourth), (B, thirds[0]), (B, thirds[1])):
+            scatter_scalar(0, spread[t], t, cols)
         for t in (A, C):
             for cols in QUARTERS:
                 nc.gpsimd.tensor_tensor(stream[t][:, cols], stream[t][:, cols], spread[t][:, cols], ADD)
         nc.vector.quantize_mx(
             out=w_codes[1][:].bitcast(FP8X4), scales=w_scale[1][:], in_=w2_bf[:].rearrange("p n u -> p (n u)")
         )
-        for cols in HALVES:
-            gated_sums(0, D, cols)
-        for cols in PIECES:
-            scatter_scalar(0, spread[D], D, cols)
+        scatter_vector(0, spread[D], D, middle)
+        scatter_scalar(0, spread[D], D, first)
+        gather_vector(A, 0)
+        for t, freed in ((B, C), (D, B)):
+            before = stream[t]
+            stream[t] = sbuf("summed%d" % t, [P, T], F32, tag="spread%d" % freed)
+            nc.vector.tensor_tensor(stream[t][:], before[:], spread[t][:], ADD)
+        picked.append(sbuf("picked2", [P, PACK, width(PIECES[2])], F32, tag="stream%d" % D))
+        gather_vector(D, 0)
         for c in range(len(PIECES)):
-            gather_vector(A, c)
-        cols = slice(0, SHARED_ADD)
-        nc.vector.tensor_tensor(stream[B][:, cols], stream[B][:, cols], spread[B][:, cols], ADD)
-        cols = slice(SHARED_ADD, T)
-        nc.gpsimd.tensor_tensor(stream[B][:, cols], stream[B][:, cols], spread[B][:, cols], ADD)
-        for c in range(len(PIECES)):
-            gather_vector(C, c)
-        before = stream[D]
-        stream[D] = sbuf("stream_last", [P, T], F32, tag="spread%d" % C)
-        nc.vector.tensor_tensor(stream[D][:], before[:], spread[D][:], ADD)
-        for c in range(len(PIECES)):
-            gather_scalar(B, c)
+            for t in (A, C, B, D):
+                if (t, c) not in ((A, 0), (D, 0)):
+                    gather_scalar(t, c)
 
-        def with_residual(t, c):
-            cols = PIECES[c]
-            nc.gpsimd.tensor_tensor(sums[1][t][:, cols], sums[1][t][:, cols], picked[c][:, t, :], ADD)
+        def with_residual(t, cols):
+            for c, piece in enumerate(PIECES):
+                lo, hi = max(cols.start, piece.start), min(cols.stop, piece.stop)
+                if lo < hi:
+                    part = sums[1][t][:, lo:hi]
+                    nc.gpsimd.tensor_tensor(part, part, picked[c][:, t, lo - piece.start : hi - piece.start], ADD)
 
-        for c in range(len(PIECES)):
-            gather_scalar(D, c)
-        for c, cols in enumerate(PIECES):
-            nc.vector.tensor_copy(picked_bf[c][:], picked[c][:].rearrange("p t s -> p s t"))
+        def results(t, cols):
+            gated_sums(1, t, cols)
+            with_residual(t, cols)
+
+        def quantise(c):
+            rounded = sbuf("rounded%d" % c, [P, width(PIECES[c]), PACK], BF16, tag="rounded")
+            nc.vector.tensor_copy(rounded[:], picked[c][:].rearrange("p t s -> p s t"))
             nc.vector.quantize_mx(
-                out=slot_codes[1][:, cols].bitcast(FP8X4),
-                scales=slot_scale[1][:, cols],
-                in_=picked_bf[c][:].rearrange("p s t -> p (s t)"),
+                out=codes_at(1, PIECES[c]).bitcast(FP8X4),
+                scales=slot_scale[1][:, PIECES[c]],
+                in_=rounded[:].rearrange("p s t -> p (s t)"),
             )
-            if c < 2:
-                for t in (A, D):
-                    gated_sums(1, t, cols)
-                    with_residual(t, c)
-                    scatter_scalar(1, stream[t], t, cols)
-        for cols in HALVES:
-            gated_sums(1, C, cols)
-        for c in range(len(PIECES)):
-            with_residual(C, c)
-        gated_sums(1, A, PIECES[2])
-        with_residual(A, 2)
+
+        shares = cuts(0, 256, 608, S)
+        for c in range(2):
+            quantise(c)
+            for t, cols in ((A, PIECES[c]), (D, shares[c])):
+                results(t, PIECES[c])
+                scatter_scalar(1, stream[t], t, cols)
+        results(C, HALVES[0])
+        quantise(2)
+        body, last = cuts(S // 2, S - P, S)
+        results(C, body)
+        results(A, PIECES[2])
         scatter_scalar(1, stream[A], A, PIECES[2])
         nc.sync.dma_start(plane(out, A), stream[A][:])
         for cols in HALVES:
-            gated_sums(1, B, cols)
-        gated_sums(1, D, PIECES[2])
-        scatter_vector(1, stream[C], C, WHOLE)
-        nc.sync.dma_start(plane(out, C), stream[C][:])
-        with_residual(D, 2)
-        scatter_vector(1, stream[D], D, PIECES[2])
-        nc.sync.dma_start(plane(out, D), stream[D][:])
-        for c, cols in enumerate(PIECES):
-            with_residual(B, c)
+            results(B, cols)
+        gated_sums(1, C, last)
+        results(D, PIECES[2])
+        part = sums[1][C][:, last]
+        nc.vector.tensor_tensor(part, part, picked[2][:, C, width(PIECES[2]) - P :], ADD)
+        for t, cols in ((C, WHOLE), (D, shares[2])):
+            scatter_vector(1, stream[t], t, cols)
+            nc.sync.dma_start(plane(out, t), stream[t][:])
+        for cols in thirds:
             scatter_scalar(1, stream[B], B, cols)
         nc.sync.dma_start(plane(out, B), stream[B][:])

@@ -21,7 +21,6 @@ PACK = 4
 GROUP = 16
 QUADRANTS = 4
 BANK = 512
-BANKS = 8
 
 
 def cuts(*bounds):
@@ -31,7 +30,6 @@ def cuts(*bounds):
 PIECES = cuts(0, 256, 640, S)
 HALVES = cuts(0, S // 2, S)
 WHOLE = slice(0, S)
-QUARTERS = cuts(0, 512, 1024, 1536, T)
 A, B, C, D = range(PACK)
 
 
@@ -41,8 +39,7 @@ def tile_moe_mod_none_kernel(
     nc = tc.nc
     with ExitStack() as ctx:
         keep = ctx.enter_context(tc.tile_pool(name="keep", bufs=1))
-        relay = ctx.enter_context(tc.tile_pool(name="relay", bufs=1))
-        psum = ctx.enter_context(tc.psum_pool(name="psum", bufs=BANKS))
+        psum = ctx.enter_context(tc.psum_pool(name="psum", bufs=1))
 
         def sbuf(name, shape, dtype, tag=None):
             return keep.tile(shape, dtype, name=name, tag=tag or name, align_bytes=64)
@@ -60,38 +57,27 @@ def tile_moe_mod_none_kernel(
         tok_words = sbuf("tok_words", [P, T], I32)
         tok_scales = sbuf("tok_scales", [P, T], U8)
         w1_codes_raw = sbuf("w1_codes_raw", [P, K], I32)
-        w1_scale_raw = relay.tile([P, K], U8, name="w1_scale_raw", offset=0, align_bytes=64)
+        w1_scale_raw = sbuf("w1_scale_raw", [P, K], U8)
         w_codes = [sbuf("w%d_codes" % layer, [P, K], I32) for layer in (1, 2)]
         w_scale = [sbuf("w%d_scale" % layer, [P, K], U8) for layer in (1, 2)]
-        code_runs = [cuts(0, PIECES[2].start, S), [WHOLE]]
-        slot_codes = [
-            [
-                sbuf("x_codes0", [P, width(code_runs[0][0])], U32),
-                relay.tile([P, width(code_runs[0][1])], U32, name="x_codes1", offset=0, align_bytes=64),
-            ],
-            [sbuf("r_codes", [P, S], U32)],
-        ]
-
-        def codes_at(layer, cols):
-            c = max(i for i, run in enumerate(code_runs[layer]) if run.start <= cols.start)
-            first = code_runs[layer][c].start
-            return slot_codes[layer][c][:, cols.start - first : cols.stop - first]
-
+        slot_codes = [sbuf("slot_codes%d" % layer, [P, S], U32) for layer in range(2)]
         slot_scale = [sbuf("slot_scale%d" % layer, [P, S], U8) for layer in range(2)]
         gates = [sbuf("gate%d" % layer, [P, S], F32) for layer in (1, 2)]
         w2_raw = sbuf("w2_raw", [P, PACK, K], F32)
         w2_bf = sbuf("w2_bf", [P, K, PACK], BF16)
         stream = [sbuf("stream%d" % t, [P, T], F32) for t in range(PACK)]
         spread = [sbuf("spread%d" % t, [P, T], F32) for t in range(PACK)]
-        sums = [[sbuf("sums%d_%d" % (layer, t), [P, S], F32) for t in range(PACK)] for layer in range(2)]
+        sums = [
+            [sbuf("sums%d_%d" % (layer, t), [P, S], F32, tag="w2_bf" if (layer, t) == (0, C) else None) for t in range(PACK)]
+            for layer in range(2)
+        ]
         picked = [sbuf("picked%d" % c, [P, PACK, width(cols)], F32) for c, cols in enumerate(PIECES[0:2])]
 
         nc.gpsimd.memset(tok_scales[:].bitcast(I32), 0)
         nc.vector.memset(w1_scale_raw[:].bitcast(I32), 0)
         nc.vector.memset(spread[A][:].bitcast(I32), 0)
-        nc.gpsimd.memset(spread[C][:].bitcast(I32), 0)
-        for t in (B, D):
-            nc.scalar.copy(spread[t][:], spread[A][:])
+        nc.vector.tensor_copy(spread[C][:], spread[A][:])
+        nc.scalar.copy(spread[B][:], spread[A][:])
 
         def load_scales(tile, scales):
             for q in range(QUADRANTS):
@@ -104,26 +90,26 @@ def tile_moe_mod_none_kernel(
         load_scales(tok_scales, x_scales)
         nc.sync.dma_start(tok_words[:], x_words[0].rearrange("p t d -> p (t d)").bitcast(I32))
         load_scales(w1_scale_raw, w1_scales)
-        for cols in cuts(0, PIECES[0].stop, S):
-            nc.sync.dma_start(gates[0][:, cols], gate1[:, cols])
-        nc.sync.dma_start(lists[1][:], offs2)
+        nc.sync.dma_start(gates[0][:], gate1)
         nc.sync.dma_start(w2_raw[:], w2.rearrange("(p u) n -> p u n", u=PACK))
+        nc.sync.dma_start(lists[1][:], offs2)
         for t in (A, C, B, D):
             nc.sync.dma_start(stream[t][:], plane(xr, t))
         nc.sync.dma_start(gates[1][:], gate2)
 
-        def gated_sums(layer, t, cols):
-            bank = psum.tile([P, BANK], F32, name="bank")
+        def one_bank(i):
+            return psum.tile([P, BANK], F32, name="one%d" % i)[:]
+
+        def gated_sums(layer, t, cols, bank):
             rows = slice(t * P, (t + 1) * P)
             at = cols.start
             while at < cols.stop:
-                stop = min(run.stop for run in code_runs[layer] + [cols] if run.stop > at)
-                n = max(n for n in (128, 256, 512) if at + n <= stop)
+                n = max(n for n in (128, 256, 512) if at + n <= cols.stop)
                 nc.tensor.matmul_mx(
                     out=bank[:, at - cols.start : at - cols.start + n],
                     lhsT=w_codes[layer][:, rows].bitcast(FP8X4),
                     lhsT_scale=w_scale[layer][:, rows],
-                    rhs=codes_at(layer, slice(at, at + n)).bitcast(FP8X4),
+                    rhs=slot_codes[layer][:, at : at + n].bitcast(FP8X4),
                     rhs_scale=slot_scale[layer][:, at : at + n],
                     start=True,
                     stop=True,
@@ -143,17 +129,20 @@ def tile_moe_mod_none_kernel(
         def gather_vector(t, c):
             nc.vector.tensor_copy(picked[c][:, t, :], stream[t][:].indirect(entries(lists[1], PIECES[c])))
 
+        def in_plane_order(tile, raw, planes):
+            return (
+                tile.rearrange("p (t m) -> p t m", t=PACK)[:, planes, :],
+                raw.rearrange("p (m t) -> p t m", t=PACK)[:, planes, :],
+            )
+
+        nc.scalar.copy(*in_plane_order(w_codes[0][:].bitcast(U32), w1_codes_raw[:].bitcast(U32), slice(0, PACK)))
+        nc.scalar.copy(spread[D][:], spread[A][:])
         for planes in cuts(0, 1, PACK):
-            for tile, raw in ((w_codes[0], w1_codes_raw), (w_scale[0], w1_scale_raw)):
-                nc.gpsimd.tensor_copy(
-                    tile[:].rearrange("p (t m) -> p t m", t=PACK)[:, planes, :],
-                    raw[:].rearrange("p (m t) -> p t m", t=PACK)[:, planes, :],
-                )
+            nc.gpsimd.tensor_copy(*in_plane_order(w_scale[0][:], w1_scale_raw[:], planes))
         nc.vector.tensor_copy(slot_scale[0][:], tok_scales[:].indirect(lists[0][:]))
-        for runs, cols in zip([PIECES[0:2], [], PIECES[2:]], PIECES):
-            for run in runs:
-                nc.vector.tensor_copy(codes_at(0, run), tok_words[:].bitcast(U32).indirect(entries(lists[0], run)))
-            gated_sums(0, A, cols)
+        for c, cols in enumerate(PIECES):
+            nc.vector.tensor_copy(slot_codes[0][:, cols], tok_words[:].bitcast(U32).indirect(entries(lists[0], cols)))
+            gated_sums(0, A, cols, one_bank(c))
             scatter_scalar(0, spread[A], A, cols)
         for ms in cuts(0, P // 2, P):
             nc.gpsimd.tensor_scalar(
@@ -164,76 +153,85 @@ def tile_moe_mod_none_kernel(
                 MULT,
                 ADD,
             )
-        for t, cols in ((B, HALVES[1]), (D, HALVES[1]), (B, HALVES[0]), (C, HALVES[0]), (C, HALVES[1])):
-            gated_sums(0, t, cols)
-        scatter_vector(0, spread[C], C, WHOLE)
-        gated_sums(0, D, HALVES[0])
-        first, middle, fourth = cuts(0, 256, 768, S)
+        first, second, third = PIECES
+        head = slice(0, third.start)
         thirds = cuts(0, 384, 768, S)
-        for t, cols in ((B, fourth), (D, fourth), (B, thirds[0]), (B, thirds[1])):
-            scatter_scalar(0, spread[t], t, cols)
-        for t in (A, C):
-            for cols in QUARTERS:
-                nc.gpsimd.tensor_tensor(stream[t][:, cols], stream[t][:, cols], spread[t][:, cols], ADD)
+        gated_sums(0, B, HALVES[0], one_bank(3))
+        gated_sums(0, D, third, one_bank(4))
+        gated_sums(0, B, HALVES[1], one_bank(5))
         nc.vector.quantize_mx(
             out=w_codes[1][:].bitcast(FP8X4), scales=w_scale[1][:], in_=w2_bf[:].rearrange("p n u -> p (n u)")
         )
-        scatter_vector(0, spread[D], D, middle)
-        scatter_scalar(0, spread[D], D, first)
-        gather_vector(A, 0)
+        for cols, bank in zip(HALVES, (6, 7)):
+            gated_sums(0, C, cols, one_bank(bank))
+        scatter_vector(0, spread[C], C, WHOLE)
+        for cols, bank in zip((first, second), (6, 7)):
+            gated_sums(0, D, cols, one_bank(bank))
+        for t, cols in ((B, thirds[0]), (D, third), (B, thirds[1]), (B, thirds[2])):
+            scatter_scalar(0, spread[t], t, cols)
+        for t in (A, C):
+            nc.gpsimd.tensor_tensor(stream[t][:], stream[t][:], spread[t][:], ADD)
+        scatter_vector(0, spread[D], D, head)
         for t, freed in ((B, C), (D, B)):
             before = stream[t]
             stream[t] = sbuf("summed%d" % t, [P, T], F32, tag="spread%d" % freed)
             nc.vector.tensor_tensor(stream[t][:], before[:], spread[t][:], ADD)
-        picked.append(sbuf("picked2", [P, PACK, width(PIECES[2])], F32, tag="stream%d" % D))
+        picked.append(sbuf("picked2", [P, PACK, width(third)], F32, tag="stream%d" % D))
         gather_vector(D, 0)
         for c in range(len(PIECES)):
             for t in (A, C, B, D):
-                if (t, c) not in ((A, 0), (D, 0)):
+                if (t, c) != (D, 0):
                     gather_scalar(t, c)
 
-        def with_residual(t, cols):
+        def with_residual(engine, t, cols):
             for c, piece in enumerate(PIECES):
                 lo, hi = max(cols.start, piece.start), min(cols.stop, piece.stop)
                 if lo < hi:
                     part = sums[1][t][:, lo:hi]
-                    nc.gpsimd.tensor_tensor(part, part, picked[c][:, t, lo - piece.start : hi - piece.start], ADD)
-
-        def results(t, cols):
-            gated_sums(1, t, cols)
-            with_residual(t, cols)
+                    engine.tensor_tensor(part, part, picked[c][:, t, lo - piece.start : hi - piece.start], ADD)
 
         def quantise(c):
             rounded = sbuf("rounded%d" % c, [P, width(PIECES[c]), PACK], BF16, tag="rounded")
             nc.vector.tensor_copy(rounded[:], picked[c][:].rearrange("p t s -> p s t"))
             nc.vector.quantize_mx(
-                out=codes_at(1, PIECES[c]).bitcast(FP8X4),
+                out=slot_codes[1][:, PIECES[c]].bitcast(FP8X4),
                 scales=slot_scale[1][:, PIECES[c]],
                 in_=rounded[:].rearrange("p s t -> p (s t)"),
             )
 
-        shares = cuts(0, 256, 608, S)
-        for c in range(2):
-            quantise(c)
-            for t, cols in ((A, PIECES[c]), (D, shares[c])):
-                results(t, PIECES[c])
-                scatter_scalar(1, stream[t], t, cols)
-        results(C, HALVES[0])
+        quantise(0)
+        for i, t in enumerate((A, D)):
+            gated_sums(1, t, first, one_bank(i))
+        for t in (A, D):
+            with_residual(nc.vector, t, first)
+            scatter_scalar(1, stream[t], t, first)
+        quantise(1)
+        for i, t in enumerate((A, D)):
+            gated_sums(1, t, second, one_bank(2 + i))
+        with_residual(nc.vector, A, second)
+        scatter_scalar(1, stream[A], A, second)
         quantise(2)
-        body, last = cuts(S // 2, S - P, S)
-        results(C, body)
-        results(A, PIECES[2])
-        scatter_scalar(1, stream[A], A, PIECES[2])
+        held = sbuf("held", [P, width(second)], F32, tag="rounded")
+        nc.gpsimd.tensor_tensor(held[:], sums[1][D][:, second], picked[1][:, D, :], ADD)
+        nc.scalar.activation(stream[D][:].indirect(entries(lists[1], second)), held[:], COPY)
+        for i, t in enumerate((C, A, D)):
+            gated_sums(1, t, third, one_bank(4 + i))
+            with_residual(nc.gpsimd, t, third)
+        scatter_scalar(1, stream[A], A, third)
         nc.sync.dma_start(plane(out, A), stream[A][:])
-        for cols in HALVES:
-            results(B, cols)
-        gated_sums(1, C, last)
-        results(D, PIECES[2])
-        part = sums[1][C][:, last]
-        nc.vector.tensor_tensor(part, part, picked[2][:, C, width(PIECES[2]) - P :], ADD)
-        for t, cols in ((C, WHOLE), (D, shares[2])):
-            scatter_vector(1, stream[t], t, cols)
-            nc.sync.dma_start(plane(out, t), stream[t][:])
+        gated_sums(1, B, thirds[0], one_bank(4))
+        with_residual(nc.gpsimd, B, thirds[0])
+        for cols, bank in ((first, 5), (second, 6)):
+            gated_sums(1, C, cols, one_bank(bank))
+            with_residual(nc.gpsimd, C, cols)
+        for cols, bank in ((thirds[1], 4), (thirds[2], 5)):
+            gated_sums(1, B, cols, one_bank(bank))
+            with_residual(nc.gpsimd, B, cols)
+        scatter_vector(1, stream[C], C, third)
+        scatter_vector(1, stream[D], D, third)
+        nc.sync.dma_start(plane(out, D), stream[D][:])
+        scatter_vector(1, stream[C], C, head)
+        nc.sync.dma_start(plane(out, C), stream[C][:])
         for cols in thirds:
             scatter_scalar(1, stream[B], B, cols)
         nc.sync.dma_start(plane(out, B), stream[B][:])

@@ -30,7 +30,7 @@ def cuts(*bounds):
 PIECES = cuts(0, 256, 640, S)
 HALVES = cuts(0, S // 2, S)
 WHOLE = slice(0, S)
-A, B, C, D = range(PACK)
+A, D, B, C = range(PACK)
 
 
 def tile_moe_mod_none_kernel(
@@ -39,6 +39,7 @@ def tile_moe_mod_none_kernel(
     nc = tc.nc
     with ExitStack() as ctx:
         keep = ctx.enter_context(tc.tile_pool(name="keep", bufs=1))
+        relay = ctx.enter_context(tc.tile_pool(name="relay", bufs=1))
         psum = ctx.enter_context(tc.psum_pool(name="psum", bufs=1))
 
         def sbuf(name, shape, dtype, tag=None):
@@ -58,19 +59,30 @@ def tile_moe_mod_none_kernel(
         tok_scales = sbuf("tok_scales", [P, T], U8)
         w1_codes_raw = sbuf("w1_codes_raw", [P, K], I32)
         w1_scale_raw = sbuf("w1_scale_raw", [P, K], U8)
-        w_codes = [sbuf("w%d_codes" % layer, [P, K], I32) for layer in (1, 2)]
+        w_codes = [sbuf("w1_codes", [P, K], I32)]
         w_scale = [sbuf("w%d_scale" % layer, [P, K], U8) for layer in (1, 2)]
-        slot_codes = [sbuf("slot_codes%d" % layer, [P, S], U32) for layer in range(2)]
+        w1_scale_first = relay.tile([P, P], U8, name="w1_scale_first", offset=0, align_bytes=64)
+        code_runs = [cuts(0, PIECES[2].start, S), [WHOLE]]
+        slot_codes = [
+            [
+                sbuf("x_codes0", [P, width(code_runs[0][0])], U32),
+                relay.tile([P, width(code_runs[0][1])], U32, name="x_codes1", offset=0, align_bytes=64),
+            ],
+            [sbuf("r_codes", [P, S], U32)],
+        ]
+
+        def codes_at(layer, cols):
+            c = max(i for i, run in enumerate(code_runs[layer]) if run.start <= cols.start)
+            start = code_runs[layer][c].start
+            return slot_codes[layer][c][:, cols.start - start : cols.stop - start]
+
         slot_scale = [sbuf("slot_scale%d" % layer, [P, S], U8) for layer in range(2)]
         gates = [sbuf("gate%d" % layer, [P, S], F32) for layer in (1, 2)]
         w2_raw = sbuf("w2_raw", [P, PACK, K], F32)
         w2_bf = sbuf("w2_bf", [P, K, PACK], BF16)
         stream = [sbuf("stream%d" % t, [P, T], F32) for t in range(PACK)]
         spread = [sbuf("spread%d" % t, [P, T], F32) for t in range(PACK)]
-        sums = [
-            [sbuf("sums%d_%d" % (layer, t), [P, S], F32, tag="w2_bf" if (layer, t) == (0, C) else None) for t in range(PACK)]
-            for layer in range(2)
-        ]
+        sums = [[sbuf("sums%d_%d" % (layer, t), [P, S], F32) for t in range(PACK)] for layer in range(2)]
         picked = [sbuf("picked%d" % c, [P, PACK, width(cols)], F32) for c, cols in enumerate(PIECES[0:2])]
 
         nc.gpsimd.memset(tok_scales[:].bitcast(I32), 0)
@@ -86,36 +98,42 @@ def tile_moe_mod_none_kernel(
                 )
 
         nc.sync.dma_start(lists[0][:], offs)
-        nc.sync.dma_start(w1_codes_raw[:], w1_words[0].rearrange("p i d -> p (i d)").bitcast(I32))
+        nc.sync.dma_start(lists[1][:], offs2)
         load_scales(tok_scales, x_scales)
+        nc.sync.dma_start(w1_codes_raw[:], w1_words[0].rearrange("p i d -> p (i d)").bitcast(I32))
         nc.sync.dma_start(tok_words[:], x_words[0].rearrange("p t d -> p (t d)").bitcast(I32))
         load_scales(w1_scale_raw, w1_scales)
-        nc.sync.dma_start(gates[0][:], gate1)
+        for cols in cuts(0, PIECES[0].stop, S):
+            nc.sync.dma_start(gates[0][:, cols], gate1[:, cols])
         nc.sync.dma_start(w2_raw[:], w2.rearrange("(p u) n -> p u n", u=PACK))
-        nc.sync.dma_start(lists[1][:], offs2)
-        for t in (A, C, B, D):
+        nc.sync.dma_start(stream[A][:], plane(xr, A))
+        nc.sync.dma_start(spread[D][:], spread[B][:])
+        for t in (C, B, D):
             nc.sync.dma_start(stream[t][:], plane(xr, t))
         nc.sync.dma_start(gates[1][:], gate2)
 
         def one_bank(i):
             return psum.tile([P, BANK], F32, name="one%d" % i)[:]
 
-        def gated_sums(layer, t, cols, bank):
+        def gated_sums(layer, t, cols, bank, weight_scale=None, into=None):
             rows = slice(t * P, (t + 1) * P)
+            weight_scale = w_scale[layer][:, rows] if weight_scale is None else weight_scale
             at = cols.start
             while at < cols.stop:
-                n = max(n for n in (128, 256, 512) if at + n <= cols.stop)
+                stop = min(run.stop for run in code_runs[layer] + [cols] if run.stop > at)
+                n = max(n for n in (128, 256, 512) if at + n <= stop)
                 nc.tensor.matmul_mx(
                     out=bank[:, at - cols.start : at - cols.start + n],
                     lhsT=w_codes[layer][:, rows].bitcast(FP8X4),
-                    lhsT_scale=w_scale[layer][:, rows],
-                    rhs=slot_codes[layer][:, at : at + n].bitcast(FP8X4),
+                    lhsT_scale=weight_scale,
+                    rhs=codes_at(layer, slice(at, at + n)).bitcast(FP8X4),
                     rhs_scale=slot_scale[layer][:, at : at + n],
                     start=True,
                     stop=True,
                 )
                 at = at + n
-            nc.vector.tensor_tensor(sums[layer][t][:, cols], bank[:, 0 : width(cols)], gates[layer][:, cols], MULT)
+            into = sums[layer][t][:, cols] if into is None else into
+            nc.vector.tensor_tensor(into, bank[:, 0 : width(cols)], gates[layer][:, cols], MULT)
 
         def scatter_scalar(layer, window, t, cols):
             nc.scalar.activation(window[:].indirect(entries(lists[layer], cols)), sums[layer][t][:, cols], COPY)
@@ -136,13 +154,12 @@ def tile_moe_mod_none_kernel(
             )
 
         nc.scalar.copy(*in_plane_order(w_codes[0][:].bitcast(U32), w1_codes_raw[:].bitcast(U32), slice(0, PACK)))
-        nc.scalar.copy(spread[D][:], spread[A][:])
-        for planes in cuts(0, 1, PACK):
-            nc.gpsimd.tensor_copy(*in_plane_order(w_scale[0][:], w1_scale_raw[:], planes))
+        nc.gpsimd.tensor_copy(w1_scale_first[:], w1_scale_raw[:].rearrange("p (m t) -> p t m", t=PACK)[:, A, :])
+        nc.gpsimd.tensor_copy(*in_plane_order(w_scale[0][:], w1_scale_raw[:], slice(0, PACK)))
         nc.vector.tensor_copy(slot_scale[0][:], tok_scales[:].indirect(lists[0][:]))
         for c, cols in enumerate(PIECES):
-            nc.vector.tensor_copy(slot_codes[0][:, cols], tok_words[:].bitcast(U32).indirect(entries(lists[0], cols)))
-            gated_sums(0, A, cols, one_bank(c))
+            nc.vector.tensor_copy(codes_at(0, cols), tok_words[:].bitcast(U32).indirect(entries(lists[0], cols)))
+            gated_sums(0, A, cols, one_bank(c), w1_scale_first[:] if c < 2 else None)
             scatter_scalar(0, spread[A], A, cols)
         for ms in cuts(0, P // 2, P):
             nc.gpsimd.tensor_scalar(
@@ -156,28 +173,37 @@ def tile_moe_mod_none_kernel(
         first, second, third = PIECES
         head = slice(0, third.start)
         thirds = cuts(0, 384, 768, S)
-        gated_sums(0, B, HALVES[0], one_bank(3))
+        turns = cuts(0, 256, 768, S)
+        gated_sums(0, B, thirds[0], one_bank(3))
         gated_sums(0, D, third, one_bank(4))
-        gated_sums(0, B, HALVES[1], one_bank(5))
-        nc.vector.quantize_mx(
-            out=w_codes[1][:].bitcast(FP8X4), scales=w_scale[1][:], in_=w2_bf[:].rearrange("p n u -> p (n u)")
-        )
         for cols, bank in zip(HALVES, (6, 7)):
             gated_sums(0, C, cols, one_bank(bank))
         scatter_vector(0, spread[C], C, WHOLE)
-        for cols, bank in zip((first, second), (6, 7)):
-            gated_sums(0, D, cols, one_bank(bank))
-        for t, cols in ((B, thirds[0]), (D, third), (B, thirds[1]), (B, thirds[2])):
+        for t, cols, bank in ((B, thirds[1], 7), (D, second, 6), (B, thirds[2], 6), (D, first, 7)):
+            gated_sums(0, t, cols, one_bank(bank))
+        for t, cols in ((B, thirds[0]), (D, turns[2]), (B, thirds[1]), (B, thirds[2])):
             scatter_scalar(0, spread[t], t, cols)
         for t in (A, C):
             nc.gpsimd.tensor_tensor(stream[t][:], stream[t][:], spread[t][:], ADD)
-        scatter_vector(0, spread[D], D, head)
+        scatter_vector(0, spread[D], D, turns[1])
+        scatter_scalar(0, spread[D], D, turns[0])
         for t, freed in ((B, C), (D, B)):
             before = stream[t]
             stream[t] = sbuf("summed%d" % t, [P, T], F32, tag="spread%d" % freed)
             nc.vector.tensor_tensor(stream[t][:], before[:], spread[t][:], ADD)
         picked.append(sbuf("picked2", [P, PACK, width(third)], F32, tag="stream%d" % D))
         gather_vector(D, 0)
+        w_codes.append(sbuf("w2_codes", [P, K], I32, tag="spread%d" % D))
+
+        def quantise_w2(cols):
+            nc.vector.quantize_mx(
+                out=w_codes[1][:, cols].bitcast(FP8X4),
+                scales=w_scale[1][:, cols],
+                in_=w2_bf[:, cols, :].rearrange("p n u -> p (n u)"),
+            )
+
+        early, late = cuts(0, K // 2, K)
+        quantise_w2(early)
         for c in range(len(PIECES)):
             for t in (A, C, B, D):
                 if (t, c) != (D, 0):
@@ -194,44 +220,51 @@ def tile_moe_mod_none_kernel(
             rounded = sbuf("rounded%d" % c, [P, width(PIECES[c]), PACK], BF16, tag="rounded")
             nc.vector.tensor_copy(rounded[:], picked[c][:].rearrange("p t s -> p s t"))
             nc.vector.quantize_mx(
-                out=slot_codes[1][:, PIECES[c]].bitcast(FP8X4),
+                out=codes_at(1, PIECES[c]).bitcast(FP8X4),
                 scales=slot_scale[1][:, PIECES[c]],
                 in_=rounded[:].rearrange("p s t -> p (s t)"),
             )
 
         quantise(0)
-        for i, t in enumerate((A, D)):
+        quantise_w2(late)
+        for i, t in enumerate((D, A)):
             gated_sums(1, t, first, one_bank(i))
-        for t in (A, D):
+        for t in (D, A):
             with_residual(nc.vector, t, first)
             scatter_scalar(1, stream[t], t, first)
         quantise(1)
-        for i, t in enumerate((A, D)):
+        for i, t in enumerate((D, A)):
             gated_sums(1, t, second, one_bank(2 + i))
-        with_residual(nc.vector, A, second)
-        scatter_scalar(1, stream[A], A, second)
+        with_residual(nc.vector, D, second)
+        scatter_scalar(1, stream[D], D, second)
         quantise(2)
-        held = sbuf("held", [P, width(second)], F32, tag="rounded")
-        nc.gpsimd.tensor_tensor(held[:], sums[1][D][:, second], picked[1][:, D, :], ADD)
-        nc.scalar.activation(stream[D][:].indirect(entries(lists[1], second)), held[:], COPY)
-        for i, t in enumerate((C, A, D)):
-            gated_sums(1, t, third, one_bank(4 + i))
-            with_residual(nc.gpsimd, t, third)
-        scatter_scalar(1, stream[A], A, third)
-        nc.sync.dma_start(plane(out, A), stream[A][:])
-        gated_sums(1, B, thirds[0], one_bank(4))
-        with_residual(nc.gpsimd, B, thirds[0])
-        for cols, bank in ((first, 5), (second, 6)):
+        for cols, bank in ((first, 2), (second, 3)):
             gated_sums(1, C, cols, one_bank(bank))
-            with_residual(nc.gpsimd, C, cols)
-        for cols, bank in ((thirds[1], 4), (thirds[2], 5)):
+        held_a = sbuf("held_a", [P, width(second)], F32, tag="rounded")
+        nc.gpsimd.tensor_tensor(held_a[:], sums[1][A][:, second], picked[1][:, A, :], ADD)
+        nc.scalar.activation(stream[A][:].indirect(entries(lists[1], second)), held_a[:], COPY)
+        last_d = sbuf("last_d", [P, width(third)], F32, tag="turns")
+        gated_sums(1, D, third, one_bank(4), into=last_d[:])
+        nc.gpsimd.tensor_tensor(sums[1][D][:, third], last_d[:], picked[2][:, D, :], ADD)
+        gated_sums(1, B, third, one_bank(5))
+        with_residual(nc.gpsimd, B, third)
+        held_c = sbuf("held_c", [P, width(head)], F32, tag="turns")
+        for c, cols in enumerate((first, second)):
+            nc.gpsimd.tensor_tensor(held_c[:, cols], sums[1][C][:, cols], picked[c][:, C, :], ADD)
+        for i, t in enumerate((A, C)):
+            gated_sums(1, t, third, one_bank(6 + i))
+            with_residual(nc.gpsimd, t, third)
+        for cols, bank in ((first, 4), (second, 5)):
             gated_sums(1, B, cols, one_bank(bank))
             with_residual(nc.gpsimd, B, cols)
-        scatter_vector(1, stream[C], C, third)
         scatter_vector(1, stream[D], D, third)
         nc.sync.dma_start(plane(out, D), stream[D][:])
-        scatter_vector(1, stream[C], C, head)
+        for t in (B, A):
+            scatter_scalar(1, stream[t], t, third)
+        nc.sync.dma_start(plane(out, A), stream[A][:])
+        nc.vector.tensor_copy(stream[C][:].indirect(entries(lists[1], head)), held_c[:])
+        scatter_vector(1, stream[C], C, third)
         nc.sync.dma_start(plane(out, C), stream[C][:])
-        for cols in thirds:
+        for cols in (first, second):
             scatter_scalar(1, stream[B], B, cols)
-        nc.sync.dma_start(plane(out, B), stream[B][:])
+        nc.scalar.dma_start(plane(out, B), stream[B][:])

@@ -218,7 +218,10 @@ def tile_moe_mod_none_kernel(
 
         def quantise(c):
             rounded = sbuf("rounded%d" % c, [P, width(PIECES[c]), PACK], BF16, tag="rounded")
-            nc.vector.tensor_copy(rounded[:], picked[c][:].rearrange("p t s -> p s t"))
+            nc.vector.tensor_copy(
+                rounded[:].rearrange("p (c i) t -> p c t i", i=PACK),
+                picked[c][:].rearrange("p t (c i) -> p c t i", i=PACK),
+            )
             nc.vector.quantize_mx(
                 out=codes_at(1, PIECES[c]).bitcast(FP8X4),
                 scales=slot_scale[1][:, PIECES[c]],

@@ -173,23 +173,27 @@ def tile_moe_mod_none_kernel(
         first, second, third = PIECES
         head = slice(0, third.start)
         thirds = cuts(0, 384, 768, S)
-        turns = cuts(0, 256, 768, S)
+        closing, between = cuts(0, 384, third.start)
         gated_sums(0, B, thirds[0], one_bank(3))
         gated_sums(0, D, third, one_bank(4))
         for cols, bank in zip(HALVES, (6, 7)):
             gated_sums(0, C, cols, one_bank(bank))
         scatter_vector(0, spread[C], C, WHOLE)
-        for t, cols, bank in ((B, thirds[1], 7), (D, second, 6), (B, thirds[2], 6), (D, first, 7)):
+        for t, cols, bank in ((B, thirds[1], 7), (D, between, 6), (B, thirds[2], 6), (D, closing, 7)):
             gated_sums(0, t, cols, one_bank(bank))
-        for t, cols in ((B, thirds[0]), (D, turns[2]), (B, thirds[1]), (B, thirds[2])):
+        for t, cols in ((B, thirds[0]), (D, third), (B, thirds[1])):
             scatter_scalar(0, spread[t], t, cols)
-        for t in (A, C):
-            nc.gpsimd.tensor_tensor(stream[t][:], stream[t][:], spread[t][:], ADD)
-        scatter_vector(0, spread[D], D, turns[1])
-        scatter_scalar(0, spread[D], D, turns[0])
-        for t, freed in ((B, C), (D, B)):
+        nc.gpsimd.tensor_tensor(stream[A][:], stream[A][:], spread[A][:], ADD)
+        before = stream[C]
+        stream[C] = sbuf("summed%d" % C, [P, T], F32)
+        nc.gpsimd.tensor_tensor(stream[C][:], before[:], spread[C][:], ADD)
+        scatter_vector(0, spread[D], D, between)
+        scatter_vector(0, spread[B], B, thirds[2])
+        scatter_scalar(0, spread[D], D, closing)
+        gather_vector(A, 0)
+        for t, freed in ((B, "spread%d" % C), (D, "stream%d" % C)):
             before = stream[t]
-            stream[t] = sbuf("summed%d" % t, [P, T], F32, tag="spread%d" % freed)
+            stream[t] = sbuf("summed%d" % t, [P, T], F32, tag=freed)
             nc.vector.tensor_tensor(stream[t][:], before[:], spread[t][:], ADD)
         picked.append(sbuf("picked2", [P, PACK, width(third)], F32, tag="stream%d" % D))
         gather_vector(D, 0)
@@ -206,7 +210,7 @@ def tile_moe_mod_none_kernel(
         quantise_w2(early)
         for c in range(len(PIECES)):
             for t in (A, C, B, D):
-                if (t, c) != (D, 0):
+                if (t, c) not in ((A, 0), (D, 0)):
                     gather_scalar(t, c)
 
         def with_residual(engine, t, cols):
@@ -216,8 +220,8 @@ def tile_moe_mod_none_kernel(
                     part = sums[1][t][:, lo:hi]
                     engine.tensor_tensor(part, part, picked[c][:, t, lo - piece.start : hi - piece.start], ADD)
 
-        def quantise(c):
-            rounded = sbuf("rounded%d" % c, [P, width(PIECES[c]), PACK], BF16, tag="rounded")
+        def quantise(c, tag=None):
+            rounded = sbuf("rounded%d" % c, [P, width(PIECES[c]), PACK], BF16, tag=tag)
             nc.vector.tensor_copy(
                 rounded[:].rearrange("p (c i) t -> p c t i", i=PACK),
                 picked[c][:].rearrange("p t (c i) -> p c t i", i=PACK),
@@ -230,17 +234,19 @@ def tile_moe_mod_none_kernel(
 
         quantise(0)
         quantise_w2(late)
-        for i, t in enumerate((D, A)):
-            gated_sums(1, t, first, one_bank(i))
+        first_d = sbuf("first_d", [P, width(first)], F32, tag="rounded")
+        gated_sums(1, D, first, one_bank(0), into=first_d[:])
+        gated_sums(1, A, first, one_bank(1))
+        nc.vector.tensor_tensor(sums[1][D][:, first], first_d[:], picked[0][:, D, :], ADD)
+        with_residual(nc.vector, A, first)
         for t in (D, A):
-            with_residual(nc.vector, t, first)
             scatter_scalar(1, stream[t], t, first)
         quantise(1)
         for i, t in enumerate((D, A)):
             gated_sums(1, t, second, one_bank(2 + i))
         with_residual(nc.vector, D, second)
         scatter_scalar(1, stream[D], D, second)
-        quantise(2)
+        quantise(2, "rounded")
         for cols, bank in ((first, 2), (second, 3)):
             gated_sums(1, C, cols, one_bank(bank))
         held_a = sbuf("held_a", [P, width(second)], F32, tag="rounded")

@@ -83,7 +83,7 @@ def tile_moe_mod_none_kernel(
         stream = [sbuf("stream%d" % t, [P, T], F32) for t in range(PACK)]
         spread = [sbuf("spread%d" % t, [P, T], F32) for t in range(PACK)]
         sums = [[sbuf("sums%d_%d" % (layer, t), [P, S], F32) for t in range(PACK)] for layer in range(2)]
-        picked = [sbuf("picked%d" % c, [P, PACK, width(cols)], F32) for c, cols in enumerate(PIECES[0:2])]
+        picked = {1: sbuf("picked1", [P, PACK, width(PIECES[1])], F32)}
 
         nc.gpsimd.memset(tok_scales[:].bitcast(I32), 0)
         nc.vector.memset(w1_scale_raw[:].bitcast(I32), 0)
@@ -190,13 +190,14 @@ def tile_moe_mod_none_kernel(
         scatter_vector(0, spread[D], D, between)
         scatter_vector(0, spread[B], B, thirds[2])
         scatter_scalar(0, spread[D], D, closing)
-        gather_vector(A, 0)
         for t, freed in ((B, "spread%d" % C), (D, "stream%d" % C)):
             before = stream[t]
             stream[t] = sbuf("summed%d" % t, [P, T], F32, tag=freed)
             nc.vector.tensor_tensor(stream[t][:], before[:], spread[t][:], ADD)
-        picked.append(sbuf("picked2", [P, PACK, width(third)], F32, tag="stream%d" % D))
-        gather_vector(D, 0)
+        picked[0] = sbuf("picked0", [P, PACK, width(first)], F32, tag="spread%d" % B)
+        picked[2] = sbuf("picked2", [P, PACK, width(third)], F32, tag="stream%d" % D)
+        for t in (A, D):
+            gather_vector(t, 0)
         w_codes.append(sbuf("w2_codes", [P, K], I32, tag="spread%d" % D))
 
         def quantise_w2(cols):
@@ -247,33 +248,43 @@ def tile_moe_mod_none_kernel(
         with_residual(nc.vector, D, second)
         scatter_scalar(1, stream[D], D, second)
         quantise(2, "rounded")
-        for cols, bank in ((first, 2), (second, 3)):
-            gated_sums(1, C, cols, one_bank(bank))
-        held_a = sbuf("held_a", [P, width(second)], F32, tag="rounded")
-        nc.gpsimd.tensor_tensor(held_a[:], sums[1][A][:, second], picked[1][:, A, :], ADD)
-        nc.scalar.activation(stream[A][:].indirect(entries(lists[1], second)), held_a[:], COPY)
+        for t, cols, bank in ((B, first, 0), (C, first, 2), (C, second, 3)):
+            gated_sums(1, t, cols, one_bank(bank))
+        early_results = sbuf("early_results", [P, third.start], F32, tag="rounded")
         last_d = sbuf("last_d", [P, width(third)], F32, tag="turns")
+        late_results = sbuf("late_results", [P, 3, S], F32, tag="turns")
+        late_row = {A: 0, B: 1, C: 2}
+
+        def late_result(t, cols):
+            return late_results[:, late_row[t], cols]
+
+        def add_late(t, cols):
+            for c, piece in enumerate(PIECES):
+                lo, hi = max(cols.start, piece.start), min(cols.stop, piece.stop)
+                if lo < hi:
+                    part = picked[c][:, t, lo - piece.start : hi - piece.start]
+                    nc.gpsimd.tensor_tensor(late_result(t, slice(lo, hi)), sums[1][t][:, lo:hi], part, ADD)
+
+        nc.gpsimd.tensor_tensor(early_results[:, second], sums[1][A][:, second], picked[1][:, A, :], ADD)
+        nc.scalar.activation(stream[A][:].indirect(entries(lists[1], second)), early_results[:, second], COPY)
         gated_sums(1, D, third, one_bank(4), into=last_d[:])
         nc.gpsimd.tensor_tensor(sums[1][D][:, third], last_d[:], picked[2][:, D, :], ADD)
-        gated_sums(1, B, third, one_bank(5))
-        with_residual(nc.gpsimd, B, third)
-        held_c = sbuf("held_c", [P, width(head)], F32, tag="turns")
-        for c, cols in enumerate((first, second)):
-            nc.gpsimd.tensor_tensor(held_c[:, cols], sums[1][C][:, cols], picked[c][:, C, :], ADD)
-        for i, t in enumerate((A, C)):
-            gated_sums(1, t, third, one_bank(6 + i))
-            with_residual(nc.gpsimd, t, third)
-        for cols, bank in ((first, 4), (second, 5)):
-            gated_sums(1, B, cols, one_bank(bank))
-            with_residual(nc.gpsimd, B, cols)
+        nc.gpsimd.tensor_tensor(early_results[:, first], sums[1][B][:, first], picked[0][:, B, :], ADD)
+        add_late(C, head)
+        later = cuts(first.stop, 768, S)
+        for t, cols, bank in ((A, third, 5), (B, later[0], 1), (B, later[1], 6), (C, third, 7)):
+            gated_sums(1, t, cols, one_bank(bank))
+            add_late(t, cols)
+        opening, middle = cuts(0, 352, third.start)
+        rest_b = slice(first.stop, S)
         scatter_vector(1, stream[D], D, third)
         nc.sync.dma_start(plane(out, D), stream[D][:])
-        for t in (B, A):
-            scatter_scalar(1, stream[t], t, third)
+        nc.vector.tensor_copy(stream[B][:].indirect(entries(lists[1], first)), early_results[:, first])
+        for t, cols in ((C, opening), (A, third)):
+            nc.scalar.activation(stream[t][:].indirect(entries(lists[1], cols)), late_result(t, cols), COPY)
         nc.sync.dma_start(plane(out, A), stream[A][:])
-        nc.vector.tensor_copy(stream[C][:].indirect(entries(lists[1], head)), held_c[:])
-        scatter_vector(1, stream[C], C, third)
+        nc.vector.tensor_copy(stream[C][:].indirect(entries(lists[1], middle)), late_result(C, middle))
+        nc.scalar.activation(stream[C][:].indirect(entries(lists[1], third)), late_result(C, third), COPY)
         nc.sync.dma_start(plane(out, C), stream[C][:])
-        for cols in (first, second):
-            scatter_scalar(1, stream[B], B, cols)
+        nc.vector.tensor_copy(stream[B][:].indirect(entries(lists[1], rest_b)), late_result(B, rest_b))
         nc.scalar.dma_start(plane(out, B), stream[B][:])

@@ -28,7 +28,7 @@ def cuts(*bounds):
 
 
 PIECES = cuts(0, 256, 640, S)
-HALVES = cuts(0, S // 2, S)
+WORD_RUNS = cuts(0, 384, 640, S)
 WHOLE = slice(0, S)
 A, D, B, C = range(PACK)
 
@@ -62,11 +62,12 @@ def tile_moe_mod_none_kernel(
         w_codes = [sbuf("w1_codes", [P, K], I32)]
         w_scale = [sbuf("w%d_scale" % layer, [P, K], U8) for layer in (1, 2)]
         w1_scale_first = relay.tile([P, P], U8, name="w1_scale_first", offset=0, align_bytes=64)
-        code_runs = [cuts(0, PIECES[2].start, S), [WHOLE]]
+        code_runs = [WORD_RUNS, [WHOLE]]
         slot_codes = [
             [
                 sbuf("x_codes0", [P, width(code_runs[0][0])], U32),
-                relay.tile([P, width(code_runs[0][1])], U32, name="x_codes1", offset=0, align_bytes=64),
+                sbuf("x_codes1", [P, width(code_runs[0][1])], U32),
+                relay.tile([P, width(code_runs[0][2])], U32, name="x_codes2", offset=0, align_bytes=64),
             ],
             [sbuf("r_codes", [P, S], U32)],
         ]
@@ -89,7 +90,6 @@ def tile_moe_mod_none_kernel(
         nc.vector.memset(w1_scale_raw[:].bitcast(I32), 0)
         nc.vector.memset(spread[A][:].bitcast(I32), 0)
         nc.vector.tensor_copy(spread[C][:], spread[A][:])
-        nc.scalar.copy(spread[B][:], spread[A][:])
 
         def load_scales(tile, scales):
             for q in range(QUADRANTS):
@@ -98,16 +98,15 @@ def tile_moe_mod_none_kernel(
                 )
 
         nc.sync.dma_start(lists[0][:], offs)
-        nc.sync.dma_start(lists[1][:], offs2)
-        load_scales(tok_scales, x_scales)
         nc.sync.dma_start(w1_codes_raw[:], w1_words[0].rearrange("p i d -> p (i d)").bitcast(I32))
+        load_scales(tok_scales, x_scales)
         nc.sync.dma_start(tok_words[:], x_words[0].rearrange("p t d -> p (t d)").bitcast(I32))
         load_scales(w1_scale_raw, w1_scales)
-        for cols in cuts(0, PIECES[0].stop, S):
+        for cols in cuts(0, WORD_RUNS[0].stop, S):
             nc.sync.dma_start(gates[0][:, cols], gate1[:, cols])
+        nc.sync.dma_start(lists[1][:], offs2)
         nc.sync.dma_start(w2_raw[:], w2.rearrange("(p u) n -> p u n", u=PACK))
         nc.sync.dma_start(stream[A][:], plane(xr, A))
-        nc.sync.dma_start(spread[D][:], spread[B][:])
         for t in (C, B, D):
             nc.sync.dma_start(stream[t][:], plane(xr, t))
         nc.sync.dma_start(gates[1][:], gate2)
@@ -154,13 +153,22 @@ def tile_moe_mod_none_kernel(
             )
 
         nc.scalar.copy(*in_plane_order(w_codes[0][:].bitcast(U32), w1_codes_raw[:].bitcast(U32), slice(0, PACK)))
+        for t in (B, D):
+            nc.scalar.copy(spread[t][:], spread[A][:])
         nc.gpsimd.tensor_copy(w1_scale_first[:], w1_scale_raw[:].rearrange("p (m t) -> p t m", t=PACK)[:, A, :])
         nc.gpsimd.tensor_copy(*in_plane_order(w_scale[0][:], w1_scale_raw[:], slice(0, PACK)))
         nc.vector.tensor_copy(slot_scale[0][:], tok_scales[:].indirect(lists[0][:]))
-        for c, cols in enumerate(PIECES):
+        low, mid, high = WORD_RUNS
+
+        def gather_words(cols):
             nc.vector.tensor_copy(codes_at(0, cols), tok_words[:].bitcast(U32).indirect(entries(lists[0], cols)))
-            gated_sums(0, A, cols, one_bank(c), w1_scale_first[:] if c < 2 else None)
-            scatter_scalar(0, spread[A], A, cols)
+
+        for c, cols in enumerate((low, mid)):
+            gather_words(cols)
+        for c, cols in enumerate((low, mid)):
+            gated_sums(0, A, cols, one_bank(c), w1_scale_first[:])
+        scatter_scalar(0, spread[A], A, low)
+        gather_words(high)
         for ms in cuts(0, P // 2, P):
             nc.gpsimd.tensor_scalar(
                 w2_bf[:].rearrange("p (t m) u -> p m t u", t=PACK)[:, ms, :, :],
@@ -173,29 +181,29 @@ def tile_moe_mod_none_kernel(
         first, second, third = PIECES
         head = slice(0, third.start)
         thirds = cuts(0, 384, 768, S)
-        closing, between = cuts(0, 384, third.start)
-        gated_sums(0, B, thirds[0], one_bank(3))
-        gated_sums(0, D, third, one_bank(4))
-        for cols, bank in zip(HALVES, (6, 7)):
-            gated_sums(0, C, cols, one_bank(bank))
-        scatter_vector(0, spread[C], C, WHOLE)
-        for t, cols, bank in ((B, thirds[1], 7), (D, between, 6), (B, thirds[2], 6), (D, closing, 7)):
+        for t, cols, bank in ((C, low, 2), (A, high, 3), (B, thirds[0], 4)):
             gated_sums(0, t, cols, one_bank(bank))
-        for t, cols in ((B, thirds[0]), (D, third), (B, thirds[1])):
+        scatter_vector(0, spread[A], A, slice(low.stop, S))
+        later_sums = ((C, mid), (C, high), (D, low), (B, thirds[1]), (D, mid), (B, thirds[2]), (D, high))
+        for i, (t, cols) in enumerate(later_sums):
+            gated_sums(0, t, cols, one_bank((5 + i) % 8))
+        for t, cols in ((C, low), (B, thirds[0]), (C, mid), (D, low), (B, thirds[1])):
             scatter_scalar(0, spread[t], t, cols)
         nc.gpsimd.tensor_tensor(stream[A][:], stream[A][:], spread[A][:], ADD)
+        scatter_vector(0, spread[C], C, high)
         before = stream[C]
         stream[C] = sbuf("summed%d" % C, [P, T], F32)
         nc.gpsimd.tensor_tensor(stream[C][:], before[:], spread[C][:], ADD)
-        scatter_vector(0, spread[D], D, between)
+        scatter_vector(0, spread[D], D, mid)
         scatter_vector(0, spread[B], B, thirds[2])
-        scatter_scalar(0, spread[D], D, closing)
+        scatter_scalar(0, spread[D], D, high)
+        gather_vector(A, 1)
         for t, freed in ((B, "spread%d" % C), (D, "stream%d" % C)):
             before = stream[t]
             stream[t] = sbuf("summed%d" % t, [P, T], F32, tag=freed)
             nc.vector.tensor_tensor(stream[t][:], before[:], spread[t][:], ADD)
         picked[0] = sbuf("picked0", [P, PACK, width(first)], F32, tag="spread%d" % B)
-        picked[2] = sbuf("picked2", [P, PACK, width(third)], F32, tag="stream%d" % D)
+        picked[2] = sbuf("picked2", [P, PACK, width(third)], F32)
         for t in (A, D):
             gather_vector(t, 0)
         w_codes.append(sbuf("w2_codes", [P, K], I32, tag="spread%d" % D))
@@ -211,7 +219,7 @@ def tile_moe_mod_none_kernel(
         quantise_w2(early)
         for c in range(len(PIECES)):
             for t in (A, C, B, D):
-                if (t, c) not in ((A, 0), (D, 0)):
+                if (t, c) not in ((A, 0), (D, 0), (A, 1)):
                     gather_scalar(t, c)
 
         def with_residual(engine, t, cols):

@@ -58,7 +58,7 @@ def tile_moe_mod_none_kernel(
         tok_words = sbuf("tok_words", [P, T], I32)
         tok_scales = sbuf("tok_scales", [P, T], U8)
         w1_codes_raw = sbuf("w1_codes_raw", [P, K], I32)
-        w1_scale_raw = sbuf("w1_scale_raw", [P, K], U8)
+        w1_scale_raw = sbuf("w1_scale_raw", [P, K], U8, tag="spread%d" % D)
         w_codes = [sbuf("w1_codes", [P, K], I32)]
         w_scale = [sbuf("w%d_scale" % layer, [P, K], U8) for layer in (1, 2)]
         w1_scale_first = relay.tile([P, P], U8, name="w1_scale_first", offset=0, align_bytes=64)
@@ -82,14 +82,13 @@ def tile_moe_mod_none_kernel(
         w2_raw = sbuf("w2_raw", [P, PACK, K], F32)
         w2_bf = sbuf("w2_bf", [P, K, PACK], BF16)
         stream = [sbuf("stream%d" % t, [P, T], F32) for t in range(PACK)]
-        spread = [sbuf("spread%d" % t, [P, T], F32) for t in range(PACK)]
+        spread = {t: sbuf("spread%d" % t, [P, T], F32) for t in (A, B, C)}
         sums = [[sbuf("sums%d_%d" % (layer, t), [P, S], F32) for t in range(PACK)] for layer in range(2)]
         picked = {1: sbuf("picked1", [P, PACK, width(PIECES[1])], F32)}
 
         nc.gpsimd.memset(tok_scales[:].bitcast(I32), 0)
         nc.vector.memset(w1_scale_raw[:].bitcast(I32), 0)
         nc.vector.memset(spread[A][:].bitcast(I32), 0)
-        nc.vector.tensor_copy(spread[C][:], spread[A][:])
 
         def load_scales(tile, scales):
             for q in range(QUADRANTS):
@@ -153,10 +152,12 @@ def tile_moe_mod_none_kernel(
             )
 
         nc.scalar.copy(*in_plane_order(w_codes[0][:].bitcast(U32), w1_codes_raw[:].bitcast(U32), slice(0, PACK)))
-        for t in (B, D):
+        for t in (C, B):
             nc.scalar.copy(spread[t][:], spread[A][:])
         nc.gpsimd.tensor_copy(w1_scale_first[:], w1_scale_raw[:].rearrange("p (m t) -> p t m", t=PACK)[:, A, :])
         nc.gpsimd.tensor_copy(*in_plane_order(w_scale[0][:], w1_scale_raw[:], slice(0, PACK)))
+        spread[D] = sbuf("spread%d" % D, [P, T], F32)
+        nc.gpsimd.memset(spread[D][:].bitcast(I32), 0)
         nc.vector.tensor_copy(slot_scale[0][:], tok_scales[:].indirect(lists[0][:]))
         low, mid, high = WORD_RUNS
 

@@ -89,6 +89,7 @@ def tile_moe_mod_none_kernel(
         nc.gpsimd.memset(tok_scales[:].bitcast(I32), 0)
         nc.vector.memset(w1_scale_raw[:].bitcast(I32), 0)
         nc.vector.memset(spread[A][:].bitcast(I32), 0)
+        nc.vector.tensor_copy(spread[C][:], spread[A][:])
 
         def load_scales(tile, scales):
             for q in range(QUADRANTS):
@@ -97,10 +98,13 @@ def tile_moe_mod_none_kernel(
                 )
 
         nc.sync.dma_start(lists[0][:], offs)
-        nc.sync.dma_start(w1_codes_raw[:], w1_words[0].rearrange("p i d -> p (i d)").bitcast(I32))
+        words = x_words[0].rearrange("p t d -> p (t d)").bitcast(I32)
+        ahead, behind = cuts(0, T // 4, T)
+        nc.sync.dma_start(tok_words[:, ahead], words[:, ahead])
         load_scales(tok_scales, x_scales)
-        nc.sync.dma_start(tok_words[:], x_words[0].rearrange("p t d -> p (t d)").bitcast(I32))
+        nc.sync.dma_start(tok_words[:, behind], words[:, behind])
         load_scales(w1_scale_raw, w1_scales)
+        nc.sync.dma_start(w1_codes_raw[:], w1_words[0].rearrange("p i d -> p (i d)").bitcast(I32))
         for cols in cuts(0, WORD_RUNS[0].stop, S):
             nc.sync.dma_start(gates[0][:, cols], gate1[:, cols])
         nc.sync.dma_start(lists[1][:], offs2)
@@ -151,9 +155,9 @@ def tile_moe_mod_none_kernel(
                 raw.rearrange("p (m t) -> p t m", t=PACK)[:, planes, :],
             )
 
-        nc.scalar.copy(*in_plane_order(w_codes[0][:].bitcast(U32), w1_codes_raw[:].bitcast(U32), slice(0, PACK)))
-        for t in (C, B):
-            nc.scalar.copy(spread[t][:], spread[A][:])
+        nc.scalar.copy(spread[B][:], spread[A][:])
+        for planes in cuts(0, 1, PACK):
+            nc.scalar.copy(*in_plane_order(w_codes[0][:].bitcast(U32), w1_codes_raw[:].bitcast(U32), planes))
         nc.gpsimd.tensor_copy(w1_scale_first[:], w1_scale_raw[:].rearrange("p (m t) -> p t m", t=PACK)[:, A, :])
         nc.gpsimd.tensor_copy(*in_plane_order(w_scale[0][:], w1_scale_raw[:], slice(0, PACK)))
         spread[D] = sbuf("spread%d" % D, [P, T], F32)

@@ -189,7 +189,7 @@ def tile_moe_mod_none_kernel(
         for t, cols, bank in ((C, low, 2), (A, high, 3), (B, thirds[0], 4)):
             gated_sums(0, t, cols, one_bank(bank))
         scatter_vector(0, spread[A], A, slice(low.stop, S))
-        later_sums = ((C, mid), (C, high), (D, low), (B, thirds[1]), (D, mid), (B, thirds[2]), (D, high))
+        later_sums = ((C, mid), (C, high), (D, low), (B, thirds[1]), (D, mid), (D, high), (B, thirds[2]))
         for i, (t, cols) in enumerate(later_sums):
             gated_sums(0, t, cols, one_bank((5 + i) % 8))
         for t, cols in ((C, low), (B, thirds[0]), (C, mid), (D, low), (B, thirds[1])):
@@ -199,19 +199,16 @@ def tile_moe_mod_none_kernel(
         before = stream[C]
         stream[C] = sbuf("summed%d" % C, [P, T], F32)
         nc.gpsimd.tensor_tensor(stream[C][:], before[:], spread[C][:], ADD)
-        scatter_vector(0, spread[D], D, mid)
-        scatter_vector(0, spread[B], B, thirds[2])
-        scatter_scalar(0, spread[D], D, high)
-        gather_vector(A, 1)
+        scatter_vector(0, spread[D], D, slice(low.stop, S))
+        scatter_scalar(0, spread[B], B, thirds[2])
+        picked[0] = sbuf("picked0", [P, PACK, width(first)], F32)
+        gather_vector(A, 0)
         for t, freed in ((B, "spread%d" % C), (D, "stream%d" % C)):
             before = stream[t]
             stream[t] = sbuf("summed%d" % t, [P, T], F32, tag=freed)
             nc.vector.tensor_tensor(stream[t][:], before[:], spread[t][:], ADD)
-        picked[0] = sbuf("picked0", [P, PACK, width(first)], F32, tag="spread%d" % B)
         picked[2] = sbuf("picked2", [P, PACK, width(third)], F32)
-        for t in (A, D):
-            gather_vector(t, 0)
-        w_codes.append(sbuf("w2_codes", [P, K], I32, tag="spread%d" % D))
+        w_codes.append(sbuf("w2_codes", [P, K], I32, tag="stream%d" % B))
 
         def quantise_w2(cols):
             nc.vector.quantize_mx(
@@ -222,9 +219,10 @@ def tile_moe_mod_none_kernel(
 
         early, late = cuts(0, K // 2, K)
         quantise_w2(early)
+        gather_vector(D, 0)
         for c in range(len(PIECES)):
             for t in (A, C, B, D):
-                if (t, c) not in ((A, 0), (D, 0), (A, 1)):
+                if (t, c) not in ((D, 0), (A, 0)):
                     gather_scalar(t, c)
 
         def with_residual(engine, t, cols):
@@ -255,11 +253,12 @@ def tile_moe_mod_none_kernel(
         with_residual(nc.vector, A, first)
         for t in (D, A):
             scatter_scalar(1, stream[t], t, first)
-        quantise(1)
+        quantise(1, "rounded0")
         for i, t in enumerate((D, A)):
             gated_sums(1, t, second, one_bank(2 + i))
         with_residual(nc.vector, D, second)
-        scatter_scalar(1, stream[D], D, second)
+        shared_d, rest_d = cuts(first.stop, 608, S)
+        scatter_scalar(1, stream[D], D, shared_d)
         quantise(2, "rounded")
         for t, cols, bank in ((B, first, 0), (C, first, 2), (C, second, 3)):
             gated_sums(1, t, cols, one_bank(bank))
@@ -290,7 +289,7 @@ def tile_moe_mod_none_kernel(
             add_late(t, cols)
         opening, middle = cuts(0, 352, third.start)
         rest_b = slice(first.stop, S)
-        scatter_vector(1, stream[D], D, third)
+        scatter_vector(1, stream[D], D, rest_d)
         nc.sync.dma_start(plane(out, D), stream[D][:])
         nc.vector.tensor_copy(stream[B][:].indirect(entries(lists[1], first)), early_results[:, first])
         for t, cols in ((C, opening), (A, third)):

from contextlib import ExitStack

import concourse.mybir as mybir

K, T, S = 512, 2048, 1024
FLOPS = 2 * 2 * K * K * S

F32 = mybir.dt.float32
BF16 = mybir.dt.bfloat16
I32 = mybir.dt.int32
U32 = mybir.dt.uint32
U16 = mybir.dt.uint16
U8 = mybir.dt.uint8
FP8X4 = mybir.dt.float8_e4m3fn_x4
COPY = mybir.ActivationFunctionType.Copy
ADD = mybir.AluOpType.add
MULT = mybir.AluOpType.mult

P = 128
PACK = 4
GROUP = 16
QUADRANTS = 4
BANK = 512


def cuts(*bounds):
    return [slice(a, b) for a, b in zip(bounds, bounds[1:])]


PIECES = cuts(0, 256, 640, S)
WORD_RUNS = cuts(0, 384, 640, S)
WHOLE = slice(0, S)
A, D, B, C = range(PACK)


def tile_moe_mod_none_kernel(
    tc, x_words, x_scales, xr, w1_words, w1_scales, w2, gate1, gate2, offs, offs2, out
):
    nc = tc.nc
    with ExitStack() as ctx:
        keep = ctx.enter_context(tc.tile_pool(name="keep", bufs=1))
        relay = ctx.enter_context(tc.tile_pool(name="relay", bufs=1))
        psum = ctx.enter_context(tc.psum_pool(name="psum", bufs=1))

        def sbuf(name, shape, dtype, tag=None):
            return keep.tile(shape, dtype, name=name, tag=tag or name, align_bytes=64)

        def width(cols):
            return cols.stop - cols.start

        def entries(lst, cols):
            return lst[:, cols.start // GROUP : cols.stop // GROUP]

        def plane(array, t):
            return array.rearrange("(p t) n -> p t n", t=PACK)[:, t, :]

        lists = [sbuf("list%d" % layer, [P, S // GROUP], U16) for layer in range(2)]
        tok_words = sbuf("tok_words", [P, T], I32)
        tok_scales = sbuf("tok_scales", [P, T], U8)
        w1_codes_raw = sbuf("w1_codes_raw", [P, K], I32)
        w1_scale_raw = sbuf("w1_scale_raw", [P, K], U8, tag="spread%d" % D)
        w_codes = [sbuf("w1_codes", [P, K], I32)]
        w_scale = [sbuf("w%d_scale" % layer, [P, K], U8) for layer in (1, 2)]
        w1_scale_first = relay.tile([P, P], U8, name="w1_scale_first", offset=0, align_bytes=64)
        code_runs = [WORD_RUNS, [WHOLE]]
        slot_codes = [
            [
                sbuf("x_codes0", [P, width(code_runs[0][0])], U32),
                sbuf("x_codes1", [P, width(code_runs[0][1])], U32),
                relay.tile([P, width(code_runs[0][2])], U32, name="x_codes2", offset=0, align_bytes=64),
            ],
            [sbuf("r_codes", [P, S], U32)],
        ]

        def codes_at(layer, cols):
            c = max(i for i, run in enumerate(code_runs[layer]) if run.start <= cols.start)
            start = code_runs[layer][c].start
            return slot_codes[layer][c][:, cols.start - start : cols.stop - start]

        slot_scale = [sbuf("slot_scale%d" % layer, [P, S], U8) for layer in range(2)]
        gates = [sbuf("gate%d" % layer, [P, S], F32) for layer in (1, 2)]
        w2_raw = sbuf("w2_raw", [P, PACK, K], F32)
        w2_bf = sbuf("w2_bf", [P, K, PACK], BF16)
        stream = [sbuf("stream%d" % t, [P, T], F32) for t in range(PACK)]
        spread = {t: sbuf("spread%d" % t, [P, T], F32) for t in (A, B, C)}
        sums = [[sbuf("sums%d_%d" % (layer, t), [P, S], F32) for t in range(PACK)] for layer in range(2)]
        picked = {1: sbuf("picked1", [P, PACK, width(PIECES[1])], F32)}

        nc.gpsimd.memset(tok_scales[:].bitcast(I32), 0)
        nc.vector.memset(w1_scale_raw[:].bitcast(I32), 0)
        nc.vector.memset(spread[A][:].bitcast(I32), 0)
        nc.vector.tensor_copy(spread[C][:], spread[A][:])

        def load_scales(tile, scales):
            for q in range(QUADRANTS):
                nc.sync.dma_start(
                    tile[32 * q : 32 * q + 4, :].bitcast(I32), scales[0, 4 * q : 4 * q + 4, :].bitcast(I32)
                )

        nc.sync.dma_start(lists[0][:], offs)
        words = x_words[0].rearrange("p t d -> p (t d)").bitcast(I32)
        ahead, behind = cuts(0, T // 4, T)
        nc.sync.dma_start(tok_words[:, ahead], words[:, ahead])
        load_scales(tok_scales, x_scales)
        nc.sync.dma_start(tok_words[:, behind], words[:, behind])
        load_scales(w1_scale_raw, w1_scales)
        nc.sync.dma_start(w1_codes_raw[:], w1_words[0].rearrange("p i d -> p (i d)").bitcast(I32))
        for cols in cuts(0, WORD_RUNS[0].stop, S):
            nc.sync.dma_start(gates[0][:, cols], gate1[:, cols])
        nc.sync.dma_start(lists[1][:], offs2)
        nc.sync.dma_start(w2_raw[:], w2.rearrange("(p u) n -> p u n", u=PACK))
        nc.sync.dma_start(stream[A][:], plane(xr, A))
        for t in (C, B, D):
            nc.sync.dma_start(stream[t][:], plane(xr, t))
        nc.sync.dma_start(gates[1][:], gate2)

        def one_bank(i):
            return psum.tile([P, BANK], F32, name="one%d" % i)[:]

        def gated_sums(layer, t, cols, bank, weight_scale=None, into=None):
            rows = slice(t * P, (t + 1) * P)
            weight_scale = w_scale[layer][:, rows] if weight_scale is None else weight_scale
            at = cols.start
            while at < cols.stop:
                stop = min(run.stop for run in code_runs[layer] + [cols] if run.stop > at)
                n = max(n for n in (128, 256, 512) if at + n <= stop)
                nc.tensor.matmul_mx(
                    out=bank[:, at - cols.start : at - cols.start + n],
                    lhsT=w_codes[layer][:, rows].bitcast(FP8X4),
                    lhsT_scale=weight_scale,
                    rhs=codes_at(layer, slice(at, at + n)).bitcast(FP8X4),
                    rhs_scale=slot_scale[layer][:, at : at + n],
                    start=True,
                    stop=True,
                )
                at = at + n
            into = sums[layer][t][:, cols] if into is None else into
            nc.vector.tensor_tensor(into, bank[:, 0 : width(cols)], gates[layer][:, cols], MULT)

        def scatter_scalar(layer, window, t, cols):
            nc.scalar.activation(window[:].indirect(entries(lists[layer], cols)), sums[layer][t][:, cols], COPY)

        def scatter_vector(layer, window, t, cols):
            nc.vector.tensor_copy(window[:].indirect(entries(lists[layer], cols)), sums[layer][t][:, cols])

        def gather_scalar(t, c):
            nc.scalar.activation(picked[c][:, t, :], stream[t][:].indirect(entries(lists[1], PIECES[c])), COPY)

        def gather_vector(t, c):
            nc.vector.tensor_copy(picked[c][:, t, :], stream[t][:].indirect(entries(lists[1], PIECES[c])))

        def in_plane_order(tile, raw, planes):
            return (
                tile.rearrange("p (t m) -> p t m", t=PACK)[:, planes, :],
                raw.rearrange("p (m t) -> p t m", t=PACK)[:, planes, :],
            )

        nc.scalar.copy(spread[B][:], spread[A][:])
        for planes in cuts(0, 1, PACK):
            nc.scalar.copy(*in_plane_order(w_codes[0][:].bitcast(U32), w1_codes_raw[:].bitcast(U32), planes))
        nc.gpsimd.tensor_copy(w1_scale_first[:], w1_scale_raw[:].rearrange("p (m t) -> p t m", t=PACK)[:, A, :])
        nc.gpsimd.tensor_copy(*in_plane_order(w_scale[0][:], w1_scale_raw[:], slice(0, PACK)))
        spread[D] = sbuf("spread%d" % D, [P, T], F32)
        nc.gpsimd.memset(spread[D][:].bitcast(I32), 0)
        nc.vector.tensor_copy(slot_scale[0][:], tok_scales[:].indirect(lists[0][:]))
        low, mid, high = WORD_RUNS

        def gather_words(cols):
            nc.vector.tensor_copy(codes_at(0, cols), tok_words[:].bitcast(U32).indirect(entries(lists[0], cols)))

        for c, cols in enumerate((low, mid)):
            gather_words(cols)
        for c, cols in enumerate((low, mid)):
            gated_sums(0, A, cols, one_bank(c), w1_scale_first[:])
        scatter_scalar(0, spread[A], A, low)
        gather_words(high)
        for ms in cuts(0, P // 2, P):
            nc.gpsimd.tensor_scalar(
                w2_bf[:].rearrange("p (t m) u -> p m t u", t=PACK)[:, ms, :, :],
                w2_raw[:].rearrange("p u (m t) -> p m t u", t=PACK)[:, ms, :, :],
                1.0,
                0.0,
                MULT,
                ADD,
            )
        first, second, third = PIECES
        head = slice(0, third.start)
        thirds = cuts(0, 384, 768, S)
        for t, cols, bank in ((C, low, 2), (A, high, 3), (B, thirds[0], 4)):
            gated_sums(0, t, cols, one_bank(bank))
        scatter_vector(0, spread[A], A, slice(low.stop, S))
        later_sums = ((C, mid), (C, high), (D, low), (B, thirds[1]), (D, mid), (D, high), (B, thirds[2]))
        for i, (t, cols) in enumerate(later_sums):
            gated_sums(0, t, cols, one_bank((5 + i) % 8))
        for t, cols in ((C, low), (B, thirds[0]), (C, mid), (D, low), (B, thirds[1])):
            scatter_scalar(0, spread[t], t, cols)
        nc.gpsimd.tensor_tensor(stream[A][:], stream[A][:], spread[A][:], ADD)
        scatter_vector(0, spread[C], C, high)
        before = stream[C]
        stream[C] = sbuf("summed%d" % C, [P, T], F32)
        nc.gpsimd.tensor_tensor(stream[C][:], before[:], spread[C][:], ADD)
        scatter_vector(0, spread[D], D, slice(low.stop, S))
        scatter_scalar(0, spread[B], B, thirds[2])
        picked[0] = sbuf("picked0", [P, PACK, width(first)], F32)
        gather_vector(A, 0)
        for t, freed in ((B, "spread%d" % C), (D, "stream%d" % C)):
            before = stream[t]
            stream[t] = sbuf("summed%d" % t, [P, T], F32, tag=freed)
            nc.vector.tensor_tensor(stream[t][:], before[:], spread[t][:], ADD)
        picked[2] = sbuf("picked2", [P, PACK, width(third)], F32)
        w_codes.append(sbuf("w2_codes", [P, K], I32, tag="stream%d" % B))

        def quantise_w2(cols):
            nc.vector.quantize_mx(
                out=w_codes[1][:, cols].bitcast(FP8X4),
                scales=w_scale[1][:, cols],
                in_=w2_bf[:, cols, :].rearrange("p n u -> p (n u)"),
            )

        early, late = cuts(0, K // 2, K)
        quantise_w2(early)
        gather_vector(D, 0)
        for c in range(len(PIECES)):
            for t in (A, C, B, D):
                if (t, c) not in ((D, 0), (A, 0)):
                    gather_scalar(t, c)

        def with_residual(engine, t, cols):
            for c, piece in enumerate(PIECES):
                lo, hi = max(cols.start, piece.start), min(cols.stop, piece.stop)
                if lo < hi:
                    part = sums[1][t][:, lo:hi]
                    engine.tensor_tensor(part, part, picked[c][:, t, lo - piece.start : hi - piece.start], ADD)

        def quantise(c, tag=None):
            rounded = sbuf("rounded%d" % c, [P, width(PIECES[c]), PACK], BF16, tag=tag)
            nc.vector.tensor_copy(
                rounded[:].rearrange("p (c i) t -> p c t i", i=PACK),
                picked[c][:].rearrange("p t (c i) -> p c t i", i=PACK),
            )
            nc.vector.quantize_mx(
                out=codes_at(1, PIECES[c]).bitcast(FP8X4),
                scales=slot_scale[1][:, PIECES[c]],
                in_=rounded[:].rearrange("p s t -> p (s t)"),
            )

        quantise(0)
        quantise_w2(late)
        first_d = sbuf("first_d", [P, width(first)], F32, tag="rounded")
        gated_sums(1, D, first, one_bank(0), into=first_d[:])
        gated_sums(1, A, first, one_bank(1))
        nc.vector.tensor_tensor(sums[1][D][:, first], first_d[:], picked[0][:, D, :], ADD)
        with_residual(nc.vector, A, first)
        for t in (D, A):
            scatter_scalar(1, stream[t], t, first)
        quantise(1, "rounded0")
        for i, t in enumerate((D, A)):
            gated_sums(1, t, second, one_bank(2 + i))
        with_residual(nc.vector, D, second)
        shared_d, rest_d = cuts(first.stop, 608, S)
        scatter_scalar(1, stream[D], D, shared_d)
        quantise(2, "rounded")
        for t, cols, bank in ((B, first, 0), (C, first, 2), (C, second, 3)):
            gated_sums(1, t, cols, one_bank(bank))
        early_results = sbuf("early_results", [P, third.start], F32, tag="rounded")
        last_d = sbuf("last_d", [P, width(third)], F32, tag="turns")
        late_results = sbuf("late_results", [P, 3, S], F32, tag="turns")
        late_row = {A: 0, B: 1, C: 2}

        def late_result(t, cols):
            return late_results[:, late_row[t], cols]

        def add_late(t, cols):
            for c, piece in enumerate(PIECES):
                lo, hi = max(cols.start, piece.start), min(cols.stop, piece.stop)
                if lo < hi:
                    part = picked[c][:, t, lo - piece.start : hi - piece.start]
                    nc.gpsimd.tensor_tensor(late_result(t, slice(lo, hi)), sums[1][t][:, lo:hi], part, ADD)

        nc.gpsimd.tensor_tensor(early_results[:, second], sums[1][A][:, second], picked[1][:, A, :], ADD)
        nc.scalar.activation(stream[A][:].indirect(entries(lists[1], second)), early_results[:, second], COPY)
        gated_sums(1, D, third, one_bank(4), into=last_d[:])
        nc.gpsimd.tensor_tensor(sums[1][D][:, third], last_d[:], picked[2][:, D, :], ADD)
        nc.gpsimd.tensor_tensor(early_results[:, first], sums[1][B][:, first], picked[0][:, B, :], ADD)
        add_late(C, head)
        later = cuts(first.stop, 768, S)
        for t, cols, bank in ((A, third, 5), (B, later[0], 1), (B, later[1], 6), (C, third, 7)):
            gated_sums(1, t, cols, one_bank(bank))
            add_late(t, cols)
        opening, middle = cuts(0, 352, third.start)
        rest_b = slice(first.stop, S)
        scatter_vector(1, stream[D], D, rest_d)
        nc.sync.dma_start(plane(out, D), stream[D][:])
        nc.vector.tensor_copy(stream[B][:].indirect(entries(lists[1], first)), early_results[:, first])
        for t, cols in ((C, opening), (A, third)):
            nc.scalar.activation(stream[t][:].indirect(entries(lists[1], cols)), late_result(t, cols), COPY)
        nc.sync.dma_start(plane(out, A), stream[A][:])
        nc.vector.tensor_copy(stream[C][:].indirect(entries(lists[1], middle)), late_result(C, middle))
        nc.scalar.activation(stream[C][:].indirect(entries(lists[1], third)), late_result(C, third), COPY)
        nc.sync.dma_start(plane(out, C), stream[C][:])
        nc.vector.tensor_copy(stream[B][:].indirect(entries(lists[1], rest_b)), late_result(B, rest_b))
        nc.scalar.dma_start(plane(out, B), stream[B][:])
